import numpy as np
import ml_dtypes


def mxq(x, axis, fmt="e4m3"):
    dtype, down = {"e4m3": (ml_dtypes.float8_e4m3fn, 7), "e5m2": (ml_dtypes.float8_e5m2, 14)}[fmt]
    v = np.moveaxis(np.asarray(x, np.float32).astype(ml_dtypes.bfloat16).astype(np.float64), axis, -1)
    blocks = v.reshape(v.shape[:-1] + (-1, 32))
    amax = np.abs(blocks).max(-1, keepdims=True)
    byte = np.maximum(np.where(amax > 0, np.frexp(amax)[1] - 1 + 127, 0) - down, 1)
    scale = np.exp2(byte - 127.0)
    codes = (blocks / scale).astype(np.float32).astype(dtype).astype(np.float64)
    return np.moveaxis((codes * scale).reshape(v.shape), -1, axis)


WIDE = False


def mx_kscale(k):
    if not WIDE:
        return np.ones(k)
    levels = np.array([18, -18])
    if k % 512:
        return np.exp2(np.random.permutation(np.resize(levels, k // 32))).repeat(32)
    a = np.empty((k // 512, 16))
    for p in range(k // 512):
        a[p, :8] = np.random.permutation(np.resize(levels, 8))
        for g in range(8):
            far = levels[np.abs(levels - a[p, g]) >= 10]
            a[p, g + 8] = far[np.random.randint(len(far))]
    return np.exp2(a.ravel()).repeat(32)


def f64(x):
    return np.asarray(x).astype(np.float64)


def striped(idx):
    return np.tile(np.asarray(idx).reshape(-1, 16).T, (8, 1)).astype(np.uint16)


def unstriped(offs):
    return offs[:16].T.reshape(-1).astype(np.int64)


B, N, T, D, DV = 1, 1024, 2048, 512, 512


def setup_inputs():
    n = np.random.standard_normal
    idx = np.random.permutation(T)[:B * N]
    v = mx_kscale(DV)[:, None]
    coarse = lambda x: x.astype(np.float32).astype(ml_dtypes.bfloat16).astype(np.float64)
    r = np.random.randint(8, 33, T) / 16.0
    return {
        "dyT": (coarse(n((DV, T))) * v).astype(np.float32),
        "hT": coarse(n((DV, T))).astype(np.float32),
        "ts": np.tile(r, (128, 1)).astype(np.float32),
        "wm": (n((B, DV, D)) / np.sqrt(DV) / v).astype(np.float32),
        "offs": striped(idx),
    }


def reference(dyT, hT, ts, wm, offs):
    idx = unstriped(offs)
    pick = lambda x: x[:, idx].reshape(x.shape[0], B, N).transpose(1, 0, 2)
    h = pick(f64(hT))
    dz = pick(f64(ts))[:, :1, :] * pick(f64(dyT)) * 2.0 * np.maximum(h, 0.0)
    dx = mxq(f64(wm), 1, "e4m3").transpose(0, 2, 1) @ mxq(dz, 1, "e5m2")
    gx = np.zeros((D, T))
    gx[:, idx] = dx.transpose(1, 0, 2).reshape(D, B * N)
    return gx

@@ -1,0 +1,181 @@
+from contextlib import ExitStack
+
+import concourse.mybir as mybir
+
+N, T, D, DV = 1024, 2048, 512, 512
+FLOPS = 2 * N * D * DV
+
+F32 = mybir.dt.float32
+BF16 = mybir.dt.bfloat16
+U32 = mybir.dt.uint32
+U16 = mybir.dt.uint16
+U8 = mybir.dt.uint8
+E4M3X4 = mybir.dt.float8_e4m3fn_x4
+E5M2X4 = mybir.dt.float8_e5m2_x4
+ACT = mybir.ActivationFunctionType
+MULT = mybir.AluOpType.mult
+
+P = 128
+PACK = 4
+HALF = 512
+QUARTER = 256
+LIST_ROWS = 16
+D_BLOCKS = D // P
+WINDOWS = 3
+
+
+def tile_attend_gex_x_kernel(tc, dyT, hT, ts, wm, offs, out):
+    nc = tc.nc
+    with ExitStack() as ctx:
+        keep = ctx.enter_context(tc.tile_pool(name="keep", bufs=1))
+        psum = ctx.enter_context(tc.psum_pool(name="psum", bufs=1))
+
+        offsets = keep.tile([P, N // LIST_ROWS], U16, name="offsets")
+        ts_all = keep.tile([P, T], F32, name="ts_all")
+        h_all = [keep.tile([P, T], F32, name="h_all%d" % t) for t in range(PACK)]
+        dy_all = [keep.tile([P, T], F32, name="dy_all%d" % t) for t in range(PACK)]
+        wm_raw = [keep.tile([P, PACK, P], F32, name="wm_raw%d" % b) for b in range(D_BLOCKS)]
+        windows = [keep.tile([P, T], F32, name="window%d" % w) for w in range(WINDOWS)]
+
+        ts_picked = keep.tile([P, N], F32, name="ts_picked")
+        ts_size = keep.tile([P, N], F32, name="ts_size")
+        ts_sign = keep.tile([P, N], F32, name="ts_sign")
+        h_scaled = [keep.tile([P, N], F32, name="h_scaled%d" % t) for t in range(PACK)]
+        slope = [keep.tile([P, N], F32, name="slope%d" % t) for t in range(PACK)]
+        dz32 = keep.tile([P, PACK, N], F32, name="dz32")
+        dz16 = keep.tile([P, N, PACK], BF16, name="dz16", align_bytes=64)
+        dz_codes = keep.tile([P, N], U32, name="dz_codes", align_bytes=64)
+        dz_scales = keep.tile([P, N], U8, name="dz_scales", align_bytes=64)
+        wm16 = keep.tile([P, D, PACK], BF16, name="wm16", align_bytes=64)
+        wm_codes = keep.tile([P, D], U32, name="wm_codes", align_bytes=64)
+        wm_scales = keep.tile([P, D], U8, name="wm_scales", align_bytes=64)
+        dx = [keep.tile([P, N], F32, name="dx%d" % b) for b in range(D_BLOCKS)]
+
+        h_rows = hT.rearrange("(p t) c -> p t c", t=PACK)
+        dy_rows = dyT.rearrange("(p t) c -> p t c", t=PACK)
+        wm_rows = wm.rearrange("b (p t) d -> p (b t) d", t=PACK)
+
+        def listed(slots):
+            return offsets[:, slots.start // LIST_ROWS : slots.stop // LIST_ROWS]
+
+        def load_wm(b):
+            nc.sync.dma_start(wm_raw[b][:], wm_rows[:, :, b * P : (b + 1) * P])
+
+        nc.sync.dma_start(offsets[:], offs)
+        nc.sync.dma_start(ts_all[:], ts)
+        nc.sync.dma_start(h_all[0][:], h_rows[:, 0, :])
+        for t in range(1, PACK):
+            nc.sync.dma_start(h_all[t][:], h_rows[:, t, :])
+            nc.sync.dma_start(dy_all[t - 1][:], dy_rows[:, t - 1, :])
+        load_wm(0)
+        nc.sync.dma_start(dy_all[PACK - 1][:], dy_rows[:, PACK - 1, :])
+        for b in range(1, D_BLOCKS):
+            load_wm(b)
+
+        for window in windows:
+            nc.vector.memset(window[:], 0.0)
+
+        halves = [slice(0, HALF), slice(HALF, N)]
+        whole = slice(0, N)
+
+        def gather_h(t, slots):
+            nc.vector.tensor_tensor(h_scaled[t][:, slots], h_all[t][:].indirect(listed(slots)), ts_size[:, slots], MULT)
+            nc.scalar.activation(slope[t][:, slots], h_scaled[t][:, slots], ACT.Relu)
+
+        def gather_dy(t, slots):
+            nc.vector.tensor_tensor(dz32[:, t, slots], dy_all[t][:].indirect(listed(slots)), slope[t][:, slots], MULT)
+
+        def interleaved(dst, src):
+            return dst.rearrange("p (c i) t -> p c t i", i=4), src.rearrange("p t (c i) -> p c t i", i=4)
+
+        def round_dz_scalar(slots):
+            dst, src = interleaved(dz16[:, slots, :], dz32[:, :, slots])
+            nc.scalar.activation(dst, src, ACT.Copy)
+
+        def round_dz_vector(slots):
+            dst, src = interleaved(dz16[:, slots, :], dz32[:, :, slots])
+            nc.vector.tensor_copy(dst, src)
+
+        def quantize_dz(slots):
+            nc.vector.quantize_mx(
+                out=dz_codes[:, slots].bitcast(E5M2X4),
+                scales=dz_scales[:, slots],
+                in_=dz16[:, slots, :].rearrange("p c t -> p (c t)"),
+            )
+
+        def round_wm(b):
+            dst, src = interleaved(wm16[:, b * P : (b + 1) * P, :], wm_raw[b][:])
+            nc.scalar.activation(dst, src, ACT.Copy)
+
+        def quantize_wm(first, last):
+            cols = slice(first * P, last * P)
+            nc.vector.quantize_mx(
+                out=wm_codes[:, cols].bitcast(E4M3X4),
+                scales=wm_scales[:, cols],
+                in_=wm16[:, cols, :].rearrange("p c t -> p (c t)"),
+            )
+
+        def multiply(b, h):
+            cols = slice(b * P, (b + 1) * P)
+            acc = psum.tile([P, HALF], F32, name="acc%d_%d" % (b, h))
+            nc.tensor.matmul_mx(
+                out=acc[:],
+                lhsT=wm_codes[:, cols].bitcast(E4M3X4),
+                lhsT_scale=wm_scales[:, cols],
+                rhs=dz_codes[:, halves[h]].bitcast(E5M2X4),
+                rhs_scale=dz_scales[:, halves[h]],
+                start=True,
+                stop=True,
+            )
+            nc.scalar.activation(dx[b][:, halves[h]], acc[:], ACT.Copy)
+
+        def scatter(b, h):
+            slots = halves[h]
+            nc.vector.tensor_tensor(windows[b % WINDOWS][:].indirect(listed(slots)), dx[b][:, slots], ts_sign[:, slots], MULT)
+
+        def store(b):
+            nc.sync.dma_start(out[b * P : (b + 1) * P, :], windows[b % WINDOWS][:])
+
+        for slots in halves:
+            nc.vector.tensor_copy(ts_picked[:, slots], ts_all[:].indirect(listed(slots)))
+            nc.scalar.activation(ts_size[:, slots], ts_picked[:, slots], ACT.Abs, scale=2.0)
+        for slots in halves:
+            gather_h(0, slots)
+        nc.scalar.activation(ts_sign[:], ts_picked[:], ACT.Sign)
+        for t in range(1, PACK):
+            gather_h(t, whole)
+            gather_dy(t - 1, whole)
+
+        round_wm(0)
+        first, second = slice(0, QUARTER), slice(QUARTER, HALF)
+        gather_dy(PACK - 1, first)
+        round_dz_scalar(first)
+        gather_dy(PACK - 1, second)
+        quantize_wm(0, 1)
+        round_dz_vector(second)
+        round_wm(1)
+        quantize_dz(halves[0])
+        multiply(0, 0)
+        gather_dy(PACK - 1, halves[1])
+        quantize_wm(1, 2)
+        multiply(1, 0)
+        round_dz_scalar(halves[1])
+        scatter(0, 0)
+        quantize_dz(halves[1])
+        multiply(0, 1)
+        multiply(1, 1)
+        round_wm(2)
+        round_wm(3)
+        scatter(1, 0)
+        quantize_wm(2, 4)
+        for b in (2, 3):
+            for h in (0, 1):
+                multiply(b, h)
+        scatter(0, 1)
+        store(0)
+        scatter(1, 1)
+        store(1)
+        for b in (2, 3):
+            for h in (0, 1):
+                scatter(b, h)
+            store(b)

@@ -34,7 +34,7 @@ def tile_attend_gex_x_kernel(tc, dyT, hT, ts, wm, offs, out):
         ts_all = keep.tile([P, T], F32, name="ts_all")
         h_all = [keep.tile([P, T], F32, name="h_all%d" % t) for t in range(PACK)]
         dy_all = [keep.tile([P, T], F32, name="dy_all%d" % t) for t in range(PACK)]
-        wm_raw = [keep.tile([P, PACK, P], F32, name="wm_raw%d" % b) for b in range(D_BLOCKS)]
+        wm_raw = keep.tile([P, PACK, D], F32, name="wm_raw")
         windows = [keep.tile([P, T], F32, name="window%d" % w) for w in range(WINDOWS)]
 
         ts_picked = keep.tile([P, N], F32, name="ts_picked")
@@ -42,7 +42,7 @@ def tile_attend_gex_x_kernel(tc, dyT, hT, ts, wm, offs, out):
         ts_sign = keep.tile([P, N], F32, name="ts_sign")
         h_scaled = [keep.tile([P, N], F32, name="h_scaled%d" % t) for t in range(PACK)]
         slope = [keep.tile([P, N], F32, name="slope%d" % t) for t in range(PACK)]
-        dz32 = keep.tile([P, PACK, N], F32, name="dz32")
+        dz32 = keep.tile([P, 2 * PACK - 1, HALF], F32, name="dz32")
         dz16 = keep.tile([P, N, PACK], BF16, name="dz16", align_bytes=64)
         dz_codes = keep.tile([P, N], U32, name="dz_codes", align_bytes=64)
         dz_scales = keep.tile([P, N], U8, name="dz_scales", align_bytes=64)
@@ -58,22 +58,17 @@ def tile_attend_gex_x_kernel(tc, dyT, hT, ts, wm, offs, out):
         def listed(slots):
             return offsets[:, slots.start // LIST_ROWS : slots.stop // LIST_ROWS]
 
-        def load_wm(b):
-            nc.sync.dma_start(wm_raw[b][:], wm_rows[:, :, b * P : (b + 1) * P])
-
-        nc.sync.dma_start(offsets[:], offs)
         nc.sync.dma_start(ts_all[:], ts)
+        nc.sync.dma_start(offsets[:], offs)
         nc.sync.dma_start(h_all[0][:], h_rows[:, 0, :])
         for t in range(1, PACK):
             nc.sync.dma_start(h_all[t][:], h_rows[:, t, :])
             nc.sync.dma_start(dy_all[t - 1][:], dy_rows[:, t - 1, :])
-        load_wm(0)
+        nc.sync.dma_start(wm_raw[:], wm_rows)
         nc.sync.dma_start(dy_all[PACK - 1][:], dy_rows[:, PACK - 1, :])
-        for b in range(1, D_BLOCKS):
-            load_wm(b)
 
         for window in windows:
-            nc.vector.memset(window[:], 0.0)
+            nc.gpsimd.memset(window[:], 0.0)
 
         halves = [slice(0, HALF), slice(HALF, N)]
         whole = slice(0, N)
@@ -82,18 +77,23 @@ def tile_attend_gex_x_kernel(tc, dyT, hT, ts, wm, offs, out):
             nc.vector.tensor_tensor(h_scaled[t][:, slots], h_all[t][:].indirect(listed(slots)), ts_size[:, slots], MULT)
             nc.scalar.activation(slope[t][:, slots], h_scaled[t][:, slots], ACT.Relu)
 
+        def dz_rows(slots):
+            h = slots.start // HALF
+            first_row = (PACK - 1) * (1 - h)
+            return dz32[:, first_row : first_row + PACK, slots.start - h * HALF : slots.stop - h * HALF]
+
         def gather_dy(t, slots):
-            nc.vector.tensor_tensor(dz32[:, t, slots], dy_all[t][:].indirect(listed(slots)), slope[t][:, slots], MULT)
+            nc.vector.tensor_tensor(dz_rows(slots)[:, t, :], dy_all[t][:].indirect(listed(slots)), slope[t][:, slots], MULT)
 
         def interleaved(dst, src):
             return dst.rearrange("p (c i) t -> p c t i", i=4), src.rearrange("p t (c i) -> p c t i", i=4)
 
         def round_dz_scalar(slots):
-            dst, src = interleaved(dz16[:, slots, :], dz32[:, :, slots])
+            dst, src = interleaved(dz16[:, slots, :], dz_rows(slots))
             nc.scalar.activation(dst, src, ACT.Copy)
 
         def round_dz_vector(slots):
-            dst, src = interleaved(dz16[:, slots, :], dz32[:, :, slots])
+            dst, src = interleaved(dz16[:, slots, :], dz_rows(slots))
             nc.vector.tensor_copy(dst, src)
 
         def quantize_dz(slots):
@@ -104,7 +104,7 @@ def tile_attend_gex_x_kernel(tc, dyT, hT, ts, wm, offs, out):
             )
 
         def round_wm(b):
-            dst, src = interleaved(wm16[:, b * P : (b + 1) * P, :], wm_raw[b][:])
+            dst, src = interleaved(wm16[:, b * P : (b + 1) * P, :], wm_raw[:, :, b * P : (b + 1) * P])
             nc.scalar.activation(dst, src, ACT.Copy)
 
         def quantize_wm(first, last):
@@ -144,33 +144,28 @@ def tile_attend_gex_x_kernel(tc, dyT, hT, ts, wm, offs, out):
         nc.scalar.activation(ts_sign[:], ts_picked[:], ACT.Sign)
         for t in range(1, PACK):
             gather_h(t, whole)
-            gather_dy(t - 1, whole)
+            for slots in halves:
+                gather_dy(t - 1, slots)
 
-        round_wm(0)
+        for b in range(D_BLOCKS):
+            round_wm(b)
+        quantize_wm(0, 2)
         first, second = slice(0, QUARTER), slice(QUARTER, HALF)
         gather_dy(PACK - 1, first)
         round_dz_scalar(first)
         gather_dy(PACK - 1, second)
-        quantize_wm(0, 1)
+        quantize_wm(2, 4)
         round_dz_vector(second)
-        round_wm(1)
         quantize_dz(halves[0])
-        multiply(0, 0)
+        for b in range(D_BLOCKS):
+            multiply(b, 0)
         gather_dy(PACK - 1, halves[1])
-        quantize_wm(1, 2)
-        multiply(1, 0)
         round_dz_scalar(halves[1])
         scatter(0, 0)
-        quantize_dz(halves[1])
-        multiply(0, 1)
-        multiply(1, 1)
-        round_wm(2)
-        round_wm(3)
         scatter(1, 0)
-        quantize_wm(2, 4)
-        for b in (2, 3):
-            for h in (0, 1):
-                multiply(b, h)
+        quantize_dz(halves[1])
+        for b in range(D_BLOCKS):
+            multiply(b, 1)
         scatter(0, 1)
         store(0)
         scatter(1, 1)

@@ -22,6 +22,9 @@ QUARTER = 256
 LIST_ROWS = 16
 D_BLOCKS = D // P
 WINDOWS = 3
+TS_LOADED = 1024
+TS_RUN = (T - TS_LOADED) // P
+BANK_TURNS = 4
 
 
 def tile_attend_gex_x_kernel(tc, dyT, hT, ts, wm, offs, out):
@@ -34,7 +37,7 @@ def tile_attend_gex_x_kernel(tc, dyT, hT, ts, wm, offs, out):
         ts_all = keep.tile([P, T], F32, name="ts_all")
         h_all = [keep.tile([P, T], F32, name="h_all%d" % t) for t in range(PACK)]
         dy_all = [keep.tile([P, T], F32, name="dy_all%d" % t) for t in range(PACK)]
-        wm_raw = keep.tile([P, PACK, D], F32, name="wm_raw")
+        wm_raw = [keep.tile([P, PACK, 2 * P], F32, name="wm_raw%d" % u) for u in range(2)]
         windows = [keep.tile([P, T], F32, name="window%d" % w) for w in range(WINDOWS)]
 
         ts_picked = keep.tile([P, N], F32, name="ts_picked")
@@ -43,13 +46,19 @@ def tile_attend_gex_x_kernel(tc, dyT, hT, ts, wm, offs, out):
         h_scaled = [keep.tile([P, N], F32, name="h_scaled%d" % t) for t in range(PACK)]
         slope = [keep.tile([P, N], F32, name="slope%d" % t) for t in range(PACK)]
         dz32 = keep.tile([P, 2 * PACK - 1, HALF], F32, name="dz32")
-        dz16 = keep.tile([P, N, PACK], BF16, name="dz16", align_bytes=64)
-        dz_codes = keep.tile([P, N], U32, name="dz_codes", align_bytes=64)
+        dz16 = {0: keep.tile([P, HALF, PACK], BF16, name="dz16_first", align_bytes=64)}
+        dz_codes = [
+            keep.tile([P, HALF], U32, name="dz_codes_first", tag="codes_then_bf16", align_bytes=64),
+            keep.tile([P, HALF], U32, name="dz_codes_second", align_bytes=64),
+        ]
         dz_scales = keep.tile([P, N], U8, name="dz_scales", align_bytes=64)
         wm16 = keep.tile([P, D, PACK], BF16, name="wm16", align_bytes=64)
         wm_codes = keep.tile([P, D], U32, name="wm_codes", align_bytes=64)
         wm_scales = keep.tile([P, D], U8, name="wm_scales", align_bytes=64)
-        dx = [keep.tile([P, N], F32, name="dx%d" % b) for b in range(D_BLOCKS)]
+        dx_own = keep.tile([P, 6, HALF], F32, name="dx_own")
+        dx = {(0, 0): dx_own[:, 0, :], (1, 0): dx_own[:, 1, :], (2, 0): dz32[:, 0, :], (3, 0): dz32[:, 1, :]}
+        for b in range(D_BLOCKS):
+            dx[(b, 1)] = dx_own[:, 2 + b, :]
 
         h_rows = hT.rearrange("(p t) c -> p t c", t=PACK)
         dy_rows = dyT.rearrange("(p t) c -> p t c", t=PACK)
@@ -58,14 +67,18 @@ def tile_attend_gex_x_kernel(tc, dyT, hT, ts, wm, offs, out):
         def listed(slots):
             return offsets[:, slots.start // LIST_ROWS : slots.stop // LIST_ROWS]
 
+        def bank(b, h):
+            return psum.tile([P, HALF], F32, name="bank%d_%d" % (b, h), tag="bank%d" % (2 * b + h))
+
         nc.sync.dma_start(ts_all[:], ts)
         nc.sync.dma_start(offsets[:], offs)
         nc.sync.dma_start(h_all[0][:], h_rows[:, 0, :])
         for t in range(1, PACK):
             nc.sync.dma_start(h_all[t][:], h_rows[:, t, :])
             nc.sync.dma_start(dy_all[t - 1][:], dy_rows[:, t - 1, :])
-        nc.sync.dma_start(wm_raw[:], wm_rows)
+        nc.sync.dma_start(wm_raw[0][:], wm_rows[:, :, : 2 * P])
         nc.sync.dma_start(dy_all[PACK - 1][:], dy_rows[:, PACK - 1, :])
+        nc.sync.dma_start(wm_raw[1][:], wm_rows[:, :, 2 * P :])
 
         for window in windows:
             nc.gpsimd.memset(window[:], 0.0)
@@ -77,10 +90,14 @@ def tile_attend_gex_x_kernel(tc, dyT, hT, ts, wm, offs, out):
             nc.vector.tensor_tensor(h_scaled[t][:, slots], h_all[t][:].indirect(listed(slots)), ts_size[:, slots], MULT)
             nc.scalar.activation(slope[t][:, slots], h_scaled[t][:, slots], ACT.Relu)
 
-        def dz_rows(slots):
+        def within_half(slots):
             h = slots.start // HALF
+            return h, slice(slots.start - h * HALF, slots.stop - h * HALF)
+
+        def dz_rows(slots):
+            h, cols = within_half(slots)
             first_row = (PACK - 1) * (1 - h)
-            return dz32[:, first_row : first_row + PACK, slots.start - h * HALF : slots.stop - h * HALF]
+            return dz32[:, first_row : first_row + PACK, cols]
 
         def gather_dy(t, slots):
             nc.vector.tensor_tensor(dz_rows(slots)[:, t, :], dy_all[t][:].indirect(listed(slots)), slope[t][:, slots], MULT)
@@ -89,22 +106,24 @@ def tile_attend_gex_x_kernel(tc, dyT, hT, ts, wm, offs, out):
             return dst.rearrange("p (c i) t -> p c t i", i=4), src.rearrange("p t (c i) -> p c t i", i=4)
 
         def round_dz_scalar(slots):
-            dst, src = interleaved(dz16[:, slots, :], dz_rows(slots))
+            h, cols = within_half(slots)
+            dst, src = interleaved(dz16[h][:, cols, :], dz_rows(slots))
             nc.scalar.activation(dst, src, ACT.Copy)
 
         def round_dz_vector(slots):
-            dst, src = interleaved(dz16[:, slots, :], dz_rows(slots))
+            h, cols = within_half(slots)
+            dst, src = interleaved(dz16[h][:, cols, :], dz_rows(slots))
             nc.vector.tensor_copy(dst, src)
 
-        def quantize_dz(slots):
+        def quantize_dz(h):
             nc.vector.quantize_mx(
-                out=dz_codes[:, slots].bitcast(E5M2X4),
-                scales=dz_scales[:, slots],
-                in_=dz16[:, slots, :].rearrange("p c t -> p (c t)"),
+                out=dz_codes[h][:].bitcast(E5M2X4),
+                scales=dz_scales[:, halves[h]],
+                in_=dz16[h][:].rearrange("p c t -> p (c t)"),
             )
 
         def round_wm(b):
-            dst, src = interleaved(wm16[:, b * P : (b + 1) * P, :], wm_raw[:, :, b * P : (b + 1) * P])
+            dst, src = interleaved(wm16[:, b * P : (b + 1) * P, :], wm_raw[b // 2][:, :, (b % 2) * P : (b % 2 + 1) * P])
             nc.scalar.activation(dst, src, ACT.Copy)
 
         def quantize_wm(first, last):
@@ -117,21 +136,24 @@ def tile_attend_gex_x_kernel(tc, dyT, hT, ts, wm, offs, out):
 
         def multiply(b, h):
             cols = slice(b * P, (b + 1) * P)
-            acc = psum.tile([P, HALF], F32, name="acc%d_%d" % (b, h))
+            acc = bank(b, h)
             nc.tensor.matmul_mx(
                 out=acc[:],
                 lhsT=wm_codes[:, cols].bitcast(E4M3X4),
                 lhsT_scale=wm_scales[:, cols],
-                rhs=dz_codes[:, halves[h]].bitcast(E5M2X4),
+                rhs=dz_codes[h][:].bitcast(E5M2X4),
                 rhs_scale=dz_scales[:, halves[h]],
                 start=True,
                 stop=True,
             )
-            nc.scalar.activation(dx[b][:, halves[h]], acc[:], ACT.Copy)
+            return acc
+
+        def copy_out(b, h, acc):
+            nc.scalar.activation(dx[(b, h)], acc[:], ACT.Copy)
 
         def scatter(b, h):
             slots = halves[h]
-            nc.vector.tensor_tensor(windows[b % WINDOWS][:].indirect(listed(slots)), dx[b][:, slots], ts_sign[:, slots], MULT)
+            nc.vector.tensor_tensor(windows[b % WINDOWS][:].indirect(listed(slots)), dx[(b, h)], ts_sign[:, slots], MULT)
 
         def store(b):
             nc.sync.dma_start(out[b * P : (b + 1) * P, :], windows[b % WINDOWS][:])
@@ -147,30 +169,38 @@ def tile_attend_gex_x_kernel(tc, dyT, hT, ts, wm, offs, out):
             for slots in halves:
                 gather_dy(t - 1, slots)
 
-        for b in range(D_BLOCKS):
-            round_wm(b)
+        round_wm(0)
+        round_wm(1)
         quantize_wm(0, 2)
         first, second = slice(0, QUARTER), slice(QUARTER, HALF)
         gather_dy(PACK - 1, first)
         round_dz_scalar(first)
         gather_dy(PACK - 1, second)
-        quantize_wm(2, 4)
         round_dz_vector(second)
-        quantize_dz(halves[0])
-        for b in range(D_BLOCKS):
-            multiply(b, 0)
+        quantize_dz(0)
+        sums = {}
+        for b in (0, 1):
+            sums[b] = multiply(b, 0)
+            copy_out(b, 0, sums[b])
         gather_dy(PACK - 1, halves[1])
+        round_wm(2)
+        round_wm(3)
+        quantize_wm(2, 4)
+        for b in (2, 3):
+            sums[b] = multiply(b, 0)
+        dz16[1] = keep.tile([P, HALF, PACK], BF16, name="dz16_second", tag="codes_then_bf16", align_bytes=64)
         round_dz_scalar(halves[1])
+        for b in (2, 3):
+            copy_out(b, 0, sums[b])
         scatter(0, 0)
         scatter(1, 0)
-        quantize_dz(halves[1])
+        quantize_dz(1)
         for b in range(D_BLOCKS):
-            multiply(b, 1)
-        scatter(0, 1)
-        store(0)
-        scatter(1, 1)
-        store(1)
-        for b in (2, 3):
-            for h in (0, 1):
-                scatter(b, h)
+            copy_out(b, 1, multiply(b, 1))
+        scatter(2, 0)
+        for b in (0, 1, 2):
+            scatter(b, 1)
             store(b)
+        scatter(3, 0)
+        scatter(3, 1)
+        store(3)

@@ -17,14 +17,13 @@ MULT = mybir.AluOpType.mult
 
 P = 128
 PACK = 4
+LAST = PACK - 1
 HALF = 512
 QUARTER = 256
 LIST_ROWS = 16
 D_BLOCKS = D // P
-WINDOWS = 3
-TS_LOADED = 1024
-TS_RUN = (T - TS_LOADED) // P
-BANK_TURNS = 4
+LINE = 4
+MX_ALIGN = 64
 
 
 def tile_attend_gex_x_kernel(tc, dyT, hT, ts, wm, offs, out):
@@ -37,38 +36,39 @@ def tile_attend_gex_x_kernel(tc, dyT, hT, ts, wm, offs, out):
         ts_all = keep.tile([P, T], F32, name="ts_all")
         h_all = [keep.tile([P, T], F32, name="h_all%d" % t) for t in range(PACK)]
         dy_all = [keep.tile([P, T], F32, name="dy_all%d" % t) for t in range(PACK)]
-        wm_raw = [keep.tile([P, PACK, 2 * P], F32, name="wm_raw%d" % u) for u in range(2)]
-        windows = [keep.tile([P, T], F32, name="window%d" % w) for w in range(WINDOWS)]
+        wm_raw0 = keep.tile([P, PACK, P], F32, name="wm_raw0")
+        wm_raw1 = keep.tile([P, PACK, P], F32, name="wm_raw1")
+        out_rows = [keep.tile([P, T], F32, name="out_rows%d" % b) for b in range(D_BLOCKS)]
 
         ts_picked = keep.tile([P, N], F32, name="ts_picked")
         ts_size = keep.tile([P, N], F32, name="ts_size")
         ts_sign = keep.tile([P, N], F32, name="ts_sign")
         h_scaled = [keep.tile([P, N], F32, name="h_scaled%d" % t) for t in range(PACK)]
         slope = [keep.tile([P, N], F32, name="slope%d" % t) for t in range(PACK)]
-        dz32 = keep.tile([P, 2 * PACK - 1, HALF], F32, name="dz32")
-        dz16 = {0: keep.tile([P, HALF, PACK], BF16, name="dz16_first", align_bytes=64)}
+
+        shared = keep.tile([P, 6, HALF], F32, name="shared")
+        dz_early = keep.tile([P, 2, HALF], F32, name="dz_early")
+        dz16_first = keep.tile([P, HALF, PACK], BF16, name="dz16_first", align_bytes=MX_ALIGN)
         dz_codes = [
-            keep.tile([P, HALF], U32, name="dz_codes_first", tag="codes_then_bf16", align_bytes=64),
-            keep.tile([P, HALF], U32, name="dz_codes_second", align_bytes=64),
+            keep.tile([P, HALF], U32, name="dz_codes_first", tag="codes_then_bf16", align_bytes=MX_ALIGN),
+            keep.tile([P, HALF], U32, name="dz_codes_second", align_bytes=MX_ALIGN),
         ]
-        dz_scales = keep.tile([P, N], U8, name="dz_scales", align_bytes=64)
-        wm16 = keep.tile([P, D, PACK], BF16, name="wm16", align_bytes=64)
-        wm_codes = keep.tile([P, D], U32, name="wm_codes", align_bytes=64)
-        wm_scales = keep.tile([P, D], U8, name="wm_scales", align_bytes=64)
+        dz_scales = keep.tile([P, N], U8, name="dz_scales", align_bytes=MX_ALIGN)
+        wm16 = keep.tile([P, D, PACK], BF16, name="wm16", align_bytes=MX_ALIGN)
+        wm_codes = keep.tile([P, D], U32, name="wm_codes", align_bytes=MX_ALIGN)
+        wm_scales = keep.tile([P, D], U8, name="wm_scales", align_bytes=MX_ALIGN)
+
         dx_own = keep.tile([P, 6, HALF], F32, name="dx_own")
-        dx = {(0, 0): dx_own[:, 0, :], (1, 0): dx_own[:, 1, :], (2, 0): dz32[:, 0, :], (3, 0): dz32[:, 1, :]}
+        dx = {(0, 0): dx_own[:, 0, :], (1, 0): shared[:, 4, :], (2, 0): dx_own[:, 1, :], (3, 0): shared[:, 0, :]}
         for b in range(D_BLOCKS):
             dx[(b, 1)] = dx_own[:, 2 + b, :]
+
+        wm_late = shared[:, 4:6, :].rearrange("p r (u d) -> p (r u) d", u=2)
+        wm_raw = [wm_raw0[:], wm_raw1[:], wm_late[:, :, :P], wm_late[:, :, P:]]
 
         h_rows = hT.rearrange("(p t) c -> p t c", t=PACK)
         dy_rows = dyT.rearrange("(p t) c -> p t c", t=PACK)
         wm_rows = wm.rearrange("b (p t) d -> p (b t) d", t=PACK)
-
-        def listed(slots):
-            return offsets[:, slots.start // LIST_ROWS : slots.stop // LIST_ROWS]
-
-        def bank(b, h):
-            return psum.tile([P, HALF], F32, name="bank%d_%d" % (b, h), tag="bank%d" % (2 * b + h))
 
         nc.sync.dma_start(ts_all[:], ts)
         nc.sync.dma_start(offsets[:], offs)
@@ -76,58 +76,62 @@ def tile_attend_gex_x_kernel(tc, dyT, hT, ts, wm, offs, out):
         for t in range(1, PACK):
             nc.sync.dma_start(h_all[t][:], h_rows[:, t, :])
             nc.sync.dma_start(dy_all[t - 1][:], dy_rows[:, t - 1, :])
-        nc.sync.dma_start(wm_raw[0][:], wm_rows[:, :, : 2 * P])
-        nc.sync.dma_start(dy_all[PACK - 1][:], dy_rows[:, PACK - 1, :])
-        nc.sync.dma_start(wm_raw[1][:], wm_rows[:, :, 2 * P :])
+        nc.sync.dma_start(dy_all[LAST][:], dy_rows[:, LAST, :])
+        for b in (0, 1):
+            nc.sync.dma_start(wm_raw[b], wm_rows[:, :, b * P : (b + 1) * P])
 
-        for window in windows:
-            nc.gpsimd.memset(window[:], 0.0)
+        for rows in out_rows:
+            nc.gpsimd.memset(rows[:], 0.0)
 
         halves = [slice(0, HALF), slice(HALF, N)]
-        whole = slice(0, N)
+        quarters = [slice(0, QUARTER), slice(QUARTER, HALF)]
+
+        def listed(slots):
+            return offsets[:, slots.start // LIST_ROWS : slots.stop // LIST_ROWS]
+
+        def slope_at(t, slots):
+            if t == LAST and slots.start == 0:
+                return shared[:, 2, slots]
+            return slope[t][:, slots]
+
+        def first_half_pair(u, slots):
+            return dz_early[:, :, slots] if u == 0 else shared[:, 3:5, slots]
+
+        def dz_plane(t, slots):
+            if slots.start >= HALF:
+                return shared[:, t, slots.start - HALF : slots.stop - HALF]
+            return first_half_pair(t // 2, slots)[:, t % 2, :]
 
         def gather_h(t, slots):
             nc.vector.tensor_tensor(h_scaled[t][:, slots], h_all[t][:].indirect(listed(slots)), ts_size[:, slots], MULT)
-            nc.scalar.activation(slope[t][:, slots], h_scaled[t][:, slots], ACT.Relu)
-
-        def within_half(slots):
-            h = slots.start // HALF
-            return h, slice(slots.start - h * HALF, slots.stop - h * HALF)
-
-        def dz_rows(slots):
-            h, cols = within_half(slots)
-            first_row = (PACK - 1) * (1 - h)
-            return dz32[:, first_row : first_row + PACK, cols]
+            for piece in (quarters[0], slice(QUARTER, N)) if t == LAST else (slots,):
+                nc.scalar.activation(slope_at(t, piece), h_scaled[t][:, piece], ACT.Relu)
 
         def gather_dy(t, slots):
-            nc.vector.tensor_tensor(dz_rows(slots)[:, t, :], dy_all[t][:].indirect(listed(slots)), slope[t][:, slots], MULT)
+            nc.vector.tensor_tensor(dz_plane(t, slots), dy_all[t][:].indirect(listed(slots)), slope_at(t, slots), MULT)
 
-        def interleaved(dst, src):
-            return dst.rearrange("p (c i) t -> p c t i", i=4), src.rearrange("p t (c i) -> p c t i", i=4)
+        def round_and_interleave(dst, src):
+            nc.scalar.activation(
+                dst.rearrange("p (c i) t -> p c t i", i=LINE),
+                src.rearrange("p t (c i) -> p c t i", i=LINE),
+                ACT.Copy,
+            )
 
-        def round_dz_scalar(slots):
-            h, cols = within_half(slots)
-            dst, src = interleaved(dz16[h][:, cols, :], dz_rows(slots))
-            nc.scalar.activation(dst, src, ACT.Copy)
+        def round_first_half_pair(u, slots):
+            round_and_interleave(dz16_first[:, slots, 2 * u : 2 * u + 2], first_half_pair(u, slots))
 
-        def round_dz_vector(slots):
-            h, cols = within_half(slots)
-            dst, src = interleaved(dz16[h][:, cols, :], dz_rows(slots))
-            nc.vector.tensor_copy(dst, src)
+        def round_wm(b):
+            round_and_interleave(wm16[:, b * P : (b + 1) * P, :], wm_raw[b])
 
-        def quantize_dz(h):
+        def quantize_dz(h, dz16):
             nc.vector.quantize_mx(
                 out=dz_codes[h][:].bitcast(E5M2X4),
                 scales=dz_scales[:, halves[h]],
-                in_=dz16[h][:].rearrange("p c t -> p (c t)"),
+                in_=dz16[:].rearrange("p c t -> p (c t)"),
             )
 
-        def round_wm(b):
-            dst, src = interleaved(wm16[:, b * P : (b + 1) * P, :], wm_raw[b // 2][:, :, (b % 2) * P : (b % 2 + 1) * P])
-            nc.scalar.activation(dst, src, ACT.Copy)
-
-        def quantize_wm(first, last):
-            cols = slice(first * P, last * P)
+        def quantize_wm(from_block, to_block):
+            cols = slice(from_block * P, to_block * P)
             nc.vector.quantize_mx(
                 out=wm_codes[:, cols].bitcast(E4M3X4),
                 scales=wm_scales[:, cols],
@@ -136,7 +140,7 @@ def tile_attend_gex_x_kernel(tc, dyT, hT, ts, wm, offs, out):
 
         def multiply(b, h):
             cols = slice(b * P, (b + 1) * P)
-            acc = bank(b, h)
+            acc = psum.tile([P, HALF], F32, name="bank%d_%d" % (b, h), tag="bank%d" % (2 * b + h))
             nc.tensor.matmul_mx(
                 out=acc[:],
                 lhsT=wm_codes[:, cols].bitcast(E4M3X4),
@@ -153,10 +157,7 @@ def tile_attend_gex_x_kernel(tc, dyT, hT, ts, wm, offs, out):
 
         def scatter(b, h):
             slots = halves[h]
-            nc.vector.tensor_tensor(windows[b % WINDOWS][:].indirect(listed(slots)), dx[(b, h)], ts_sign[:, slots], MULT)
-
-        def store(b):
-            nc.sync.dma_start(out[b * P : (b + 1) * P, :], windows[b % WINDOWS][:])
+            nc.vector.tensor_tensor(out_rows[b][:].indirect(listed(slots)), dx[(b, h)], ts_sign[:, slots], MULT)
 
         for slots in halves:
             nc.vector.tensor_copy(ts_picked[:, slots], ts_all[:].indirect(listed(slots)))
@@ -165,42 +166,43 @@ def tile_attend_gex_x_kernel(tc, dyT, hT, ts, wm, offs, out):
             gather_h(0, slots)
         nc.scalar.activation(ts_sign[:], ts_picked[:], ACT.Sign)
         for t in range(1, PACK):
-            gather_h(t, whole)
-            for slots in halves:
+            gather_h(t, slice(0, N))
+            for slots in halves if t < LAST else halves[:1]:
                 gather_dy(t - 1, slots)
+            if t - 1 == 1:
+                round_first_half_pair(0, halves[0])
 
+        for slots in quarters:
+            gather_dy(LAST, slots)
+            round_first_half_pair(1, slots)
+        gather_dy(LAST - 1, halves[1])
         round_wm(0)
         round_wm(1)
-        quantize_wm(0, 2)
-        first, second = slice(0, QUARTER), slice(QUARTER, HALF)
-        gather_dy(PACK - 1, first)
-        round_dz_scalar(first)
-        gather_dy(PACK - 1, second)
-        round_dz_vector(second)
-        quantize_dz(0)
-        sums = {}
-        for b in (0, 1):
-            sums[b] = multiply(b, 0)
-            copy_out(b, 0, sums[b])
-        gather_dy(PACK - 1, halves[1])
+        nc.sync.dma_start(wm_late, wm_rows[:, :, 2 * P :])
+        quantize_dz(0, dz16_first)
+        quantize_wm(0, 1)
+        copy_out(0, 0, multiply(0, 0))
+        gather_dy(LAST, halves[1])
+        quantize_wm(1, 2)
+        acc1 = multiply(1, 0)
+        scatter(0, 0)
         round_wm(2)
         round_wm(3)
         quantize_wm(2, 4)
-        for b in (2, 3):
-            sums[b] = multiply(b, 0)
-        dz16[1] = keep.tile([P, HALF, PACK], BF16, name="dz16_second", tag="codes_then_bf16", align_bytes=64)
-        round_dz_scalar(halves[1])
-        for b in (2, 3):
-            copy_out(b, 0, sums[b])
-        scatter(0, 0)
+        copy_out(1, 0, acc1)
+        acc2 = multiply(2, 0)
+        acc3 = multiply(3, 0)
+        copy_out(2, 0, acc2)
+
+        dz16_second = keep.tile([P, HALF, PACK], BF16, name="dz16_second", tag="codes_then_bf16", align_bytes=MX_ALIGN)
+        round_and_interleave(dz16_second[:], shared[:, :PACK, :])
+        copy_out(3, 0, acc3)
         scatter(1, 0)
-        quantize_dz(1)
+        scatter(2, 0)
+        quantize_dz(1, dz16_second)
         for b in range(D_BLOCKS):
             copy_out(b, 1, multiply(b, 1))
-        scatter(2, 0)
-        for b in (0, 1, 2):
-            scatter(b, 1)
-            store(b)
         scatter(3, 0)
-        scatter(3, 1)
-        store(3)
+        for b in range(D_BLOCKS):
+            scatter(b, 1)
+            nc.sync.dma_start(out[b * P : (b + 1) * P, :], out_rows[b][:])

@@ -40,6 +40,7 @@ def tile_attend_gex_x_kernel(tc, dyT, hT, ts, wm, offs, out):
         wm_raw1 = keep.tile([P, PACK, P], F32, name="wm_raw1")
         out_rows = [keep.tile([P, T], F32, name="out_rows%d" % b) for b in range(D_BLOCKS)]
 
+        twos = keep.tile([P, HALF], F32, name="twos")
         ts_picked = keep.tile([P, N], F32, name="ts_picked")
         ts_size = keep.tile([P, N], F32, name="ts_size")
         ts_sign = keep.tile([P, N], F32, name="ts_sign")
@@ -80,6 +81,7 @@ def tile_attend_gex_x_kernel(tc, dyT, hT, ts, wm, offs, out):
         for b in (0, 1):
             nc.sync.dma_start(wm_raw[b], wm_rows[:, :, b * P : (b + 1) * P])
 
+        nc.gpsimd.memset(twos[:], 2.0)
         for rows in out_rows:
             nc.gpsimd.memset(rows[:], 0.0)
 
@@ -160,8 +162,8 @@ def tile_attend_gex_x_kernel(tc, dyT, hT, ts, wm, offs, out):
             nc.vector.tensor_tensor(out_rows[b][:].indirect(listed(slots)), dx[(b, h)], ts_sign[:, slots], MULT)
 
         for slots in halves:
-            nc.vector.tensor_copy(ts_picked[:, slots], ts_all[:].indirect(listed(slots)))
-            nc.scalar.activation(ts_size[:, slots], ts_picked[:, slots], ACT.Abs, scale=2.0)
+            nc.vector.tensor_tensor(ts_picked[:, slots], ts_all[:].indirect(listed(slots)), twos[:], MULT)
+            nc.scalar.activation(ts_size[:, slots], ts_picked[:, slots], ACT.Abs)
         for slots in halves:
             gather_h(0, slots)
         nc.scalar.activation(ts_sign[:], ts_picked[:], ACT.Sign)

@@ -1,6 +1,7 @@
 from contextlib import ExitStack
 
 import concourse.mybir as mybir
+from concourse.masks import make_identity
 
 N, T, D, DV = 1024, 2048, 512, 512
 FLOPS = 2 * N * D * DV
@@ -17,13 +18,15 @@ MULT = mybir.AluOpType.mult
 
 P = 128
 PACK = 4
-LAST = PACK - 1
 HALF = 512
 QUARTER = 256
 LIST_ROWS = 16
 D_BLOCKS = D // P
 LINE = 4
 MX_ALIGN = 64
+SPREAD_BANKS = 2
+SPREAD_COLS = 2
+SPREAD = SPREAD_BANKS * SPREAD_COLS * P
 
 
 def tile_attend_gex_x_kernel(tc, dyT, hT, ts, wm, offs, out):
@@ -34,83 +37,99 @@ def tile_attend_gex_x_kernel(tc, dyT, hT, ts, wm, offs, out):
 
         offsets = keep.tile([P, N // LIST_ROWS], U16, name="offsets")
         ts_all = keep.tile([P, T], F32, name="ts_all")
+        ts_tail = keep.tile([P, SPREAD_BANKS, SPREAD_COLS], F32, name="ts_tail")
+        identity = keep.tile([P, P], F32, name="identity")
+        twos = keep.tile([P, HALF], F32, name="twos")
         h_all = [keep.tile([P, T], F32, name="h_all%d" % t) for t in range(PACK)]
         dy_all = [keep.tile([P, T], F32, name="dy_all%d" % t) for t in range(PACK)]
-        wm_raw0 = keep.tile([P, PACK, P], F32, name="wm_raw0")
-        wm_raw1 = keep.tile([P, PACK, P], F32, name="wm_raw1")
+        wm_blocks = [slice(0, 1), slice(1, 3), slice(3, 4)]
         out_rows = [keep.tile([P, T], F32, name="out_rows%d" % b) for b in range(D_BLOCKS)]
+        dx = [keep.tile([P, N], F32, name="dx%d" % b) for b in range(D_BLOCKS)]
 
-        twos = keep.tile([P, HALF], F32, name="twos")
-        ts_picked = keep.tile([P, N], F32, name="ts_picked")
+        ts_twice = keep.tile([P, N], F32, name="ts_twice")
         ts_size = keep.tile([P, N], F32, name="ts_size")
-        ts_sign = keep.tile([P, N], F32, name="ts_sign")
         h_scaled = [keep.tile([P, N], F32, name="h_scaled%d" % t) for t in range(PACK)]
-        slope = [keep.tile([P, N], F32, name="slope%d" % t) for t in range(PACK)]
+        ts_sign = h_scaled[1]
+        slope = [keep.tile([P, N], F32, name="slope%d" % t) for t in range(PACK - 1)]
 
-        shared = keep.tile([P, 6, HALF], F32, name="shared")
-        dz_early = keep.tile([P, 2, HALF], F32, name="dz_early")
-        dz16_first = keep.tile([P, HALF, PACK], BF16, name="dz16_first", align_bytes=MX_ALIGN)
-        dz_codes = [
-            keep.tile([P, HALF], U32, name="dz_codes_first", tag="codes_then_bf16", align_bytes=MX_ALIGN),
-            keep.tile([P, HALF], U32, name="dz_codes_second", align_bytes=MX_ALIGN),
+        work = keep.tile([P, 13 * HALF], F32, name="work", align_bytes=MX_ALIGN)
+
+        def region(r, start=0, stop=HALF):
+            return work[:, r * HALF + start : r * HALF + stop]
+
+        def as_bf16(ap):
+            return ap.bitcast(BF16).rearrange("p (c t) -> p c t", t=PACK)
+
+        dz16 = [keep.tile([P, HALF, PACK], BF16, name="dz16_first", align_bytes=MX_ALIGN)[:], as_bf16(region(11, 0, N))]
+        wm16 = [as_bf16(region(0, 0, QUARTER)), as_bf16(region(11)), as_bf16(region(1, 0, QUARTER))]
+        wm_raw = [region(6, QUARTER, QUARTER + HALF).rearrange("p (t d) -> p t d", t=PACK)] + [
+            keep.tile([P, PACK, (g.stop - g.start) * P], F32, name="wm_raw%d" % g.start)[:] for g in wm_blocks[1:]
         ]
+        dz_codes = keep.tile([P, N], U32, name="dz_codes", align_bytes=MX_ALIGN)
         dz_scales = keep.tile([P, N], U8, name="dz_scales", align_bytes=MX_ALIGN)
-        wm16 = keep.tile([P, D, PACK], BF16, name="wm16", align_bytes=MX_ALIGN)
         wm_codes = keep.tile([P, D], U32, name="wm_codes", align_bytes=MX_ALIGN)
         wm_scales = keep.tile([P, D], U8, name="wm_scales", align_bytes=MX_ALIGN)
-
-        dx_own = keep.tile([P, 6, HALF], F32, name="dx_own")
-        dx = {(0, 0): dx_own[:, 0, :], (1, 0): shared[:, 4, :], (2, 0): dx_own[:, 1, :], (3, 0): shared[:, 0, :]}
-        for b in range(D_BLOCKS):
-            dx[(b, 1)] = dx_own[:, 2 + b, :]
-
-        wm_late = shared[:, 4:6, :].rearrange("p r (u d) -> p (r u) d", u=2)
-        wm_raw = [wm_raw0[:], wm_raw1[:], wm_late[:, :, :P], wm_late[:, :, P:]]
 
         h_rows = hT.rearrange("(p t) c -> p t c", t=PACK)
         dy_rows = dyT.rearrange("(p t) c -> p t c", t=PACK)
         wm_rows = wm.rearrange("b (p t) d -> p (b t) d", t=PACK)
 
-        nc.sync.dma_start(ts_all[:], ts)
+        def load_wm(g):
+            nc.sync.dma_start(wm_raw[g], wm_rows[:, :, wm_blocks[g].start * P : wm_blocks[g].stop * P])
+
+        nc.sync.dma_start(
+            ts_tail[:], ts[0:1, T - SPREAD :].rearrange("o (r p j) -> (o p) r j", r=SPREAD_BANKS, p=P)
+        )
+        nc.sync.dma_start(ts_all[:, : T - SPREAD], ts[:, : T - SPREAD])
         nc.sync.dma_start(offsets[:], offs)
         nc.sync.dma_start(h_all[0][:], h_rows[:, 0, :])
         for t in range(1, PACK):
             nc.sync.dma_start(h_all[t][:], h_rows[:, t, :])
             nc.sync.dma_start(dy_all[t - 1][:], dy_rows[:, t - 1, :])
-        nc.sync.dma_start(dy_all[LAST][:], dy_rows[:, LAST, :])
-        for b in (0, 1):
-            nc.sync.dma_start(wm_raw[b], wm_rows[:, :, b * P : (b + 1) * P])
+        load_wm(0)
+        nc.sync.dma_start(dy_all[3][:], dy_rows[:, 3, :])
+        load_wm(1)
+        load_wm(2)
 
+        make_identity(nc, identity[:])
+        for r in range(SPREAD_BANKS):
+            spread = psum.tile([P, SPREAD_COLS, P], F32, name="spread%d" % r, tag="bank%d" % (6 + r))
+            for j in range(SPREAD_COLS):
+                nc.tensor.transpose(spread[:, j, :], ts_tail[:, r, j : j + 1].to_broadcast([P, P]), identity[:])
+            first = T - SPREAD + r * SPREAD_COLS * P
+            nc.vector.tensor_copy(
+                ts_all[:, first : first + SPREAD_COLS * P].rearrange("p (n j) -> p n j", n=P),
+                spread[:].rearrange("p j n -> p n j"),
+            )
         nc.gpsimd.memset(twos[:], 2.0)
         for rows in out_rows:
             nc.gpsimd.memset(rows[:], 0.0)
 
+        whole = slice(0, N)
         halves = [slice(0, HALF), slice(HALF, N)]
-        quarters = [slice(0, QUARTER), slice(QUARTER, HALF)]
+        pieces = [slice(0, 128), slice(128, 256), slice(256, 512)]
 
         def listed(slots):
             return offsets[:, slots.start // LIST_ROWS : slots.stop // LIST_ROWS]
 
         def slope_at(t, slots):
-            if t == LAST and slots.start == 0:
-                return shared[:, 2, slots]
-            return slope[t][:, slots]
+            if t < 3:
+                return slope[t][:, slots]
+            return region(7 if slots.stop <= QUARTER else 5, slots.start, slots.stop)
 
-        def first_half_pair(u, slots):
-            return dz_early[:, :, slots] if u == 0 else shared[:, 3:5, slots]
-
-        def dz_plane(t, slots):
-            if slots.start >= HALF:
-                return shared[:, t, slots.start - HALF : slots.stop - HALF]
-            return first_half_pair(t // 2, slots)[:, t % 2, :]
+        def dz_at(t, slots):
+            if t >= 2 and slots.stop <= HALF:
+                return region(8 + t, slots.start, slots.stop)
+            return region(3 * t, slots.start, slots.stop)
 
         def gather_h(t, slots):
             nc.vector.tensor_tensor(h_scaled[t][:, slots], h_all[t][:].indirect(listed(slots)), ts_size[:, slots], MULT)
-            for piece in (quarters[0], slice(QUARTER, N)) if t == LAST else (slots,):
-                nc.scalar.activation(slope_at(t, piece), h_scaled[t][:, piece], ACT.Relu)
+
+        def relu(t, slots):
+            nc.scalar.activation(slope_at(t, slots), h_scaled[t][:, slots], ACT.Relu)
 
         def gather_dy(t, slots):
-            nc.vector.tensor_tensor(dz_plane(t, slots), dy_all[t][:].indirect(listed(slots)), slope_at(t, slots), MULT)
+            nc.vector.tensor_tensor(dz_at(t, slots), dy_all[t][:].indirect(listed(slots)), slope_at(t, slots), MULT)
 
         def round_and_interleave(dst, src):
             nc.scalar.activation(
@@ -119,25 +138,23 @@ def tile_attend_gex_x_kernel(tc, dyT, hT, ts, wm, offs, out):
                 ACT.Copy,
             )
 
-        def round_first_half_pair(u, slots):
-            round_and_interleave(dz16_first[:, slots, 2 * u : 2 * u + 2], first_half_pair(u, slots))
+        def round_wm(g):
+            round_and_interleave(wm16[g], wm_raw[g])
 
-        def round_wm(b):
-            round_and_interleave(wm16[:, b * P : (b + 1) * P, :], wm_raw[b])
-
-        def quantize_dz(h, dz16):
+        def quantize_dz(slots):
+            h = slots.start // HALF
             nc.vector.quantize_mx(
-                out=dz_codes[h][:].bitcast(E5M2X4),
-                scales=dz_scales[:, halves[h]],
-                in_=dz16[:].rearrange("p c t -> p (c t)"),
+                out=dz_codes[:, slots].bitcast(E5M2X4),
+                scales=dz_scales[:, slots],
+                in_=dz16[h][:, slots.start - h * HALF : slots.stop - h * HALF, :].rearrange("p c t -> p (c t)"),
             )
 
-        def quantize_wm(from_block, to_block):
-            cols = slice(from_block * P, to_block * P)
+        def quantize_wm(g):
+            cols = slice(wm_blocks[g].start * P, wm_blocks[g].stop * P)
             nc.vector.quantize_mx(
                 out=wm_codes[:, cols].bitcast(E4M3X4),
                 scales=wm_scales[:, cols],
-                in_=wm16[:, cols, :].rearrange("p c t -> p (c t)"),
+                in_=wm16[g].rearrange("p c t -> p (c t)"),
             )
 
         def multiply(b, h):
@@ -147,7 +164,7 @@ def tile_attend_gex_x_kernel(tc, dyT, hT, ts, wm, offs, out):
                 out=acc[:],
                 lhsT=wm_codes[:, cols].bitcast(E4M3X4),
                 lhsT_scale=wm_scales[:, cols],
-                rhs=dz_codes[h][:].bitcast(E5M2X4),
+                rhs=dz_codes[:, halves[h]].bitcast(E5M2X4),
                 rhs_scale=dz_scales[:, halves[h]],
                 start=True,
                 stop=True,
@@ -155,56 +172,67 @@ def tile_attend_gex_x_kernel(tc, dyT, hT, ts, wm, offs, out):
             return acc
 
         def copy_out(b, h, acc):
-            nc.scalar.activation(dx[(b, h)], acc[:], ACT.Copy)
+            nc.scalar.activation(dx[b][:, halves[h]], acc[:], ACT.Copy)
 
-        def scatter(b, h):
-            slots = halves[h]
-            nc.vector.tensor_tensor(out_rows[b][:].indirect(listed(slots)), dx[(b, h)], ts_sign[:, slots], MULT)
+        def scatter(b, slots):
+            nc.vector.tensor_tensor(out_rows[b][:].indirect(listed(slots)), dx[b][:, slots], ts_sign[:, slots], MULT)
+
+        def store(b):
+            nc.sync.dma_start(out[b * P : (b + 1) * P, :], out_rows[b][:])
 
         for slots in halves:
-            nc.vector.tensor_tensor(ts_picked[:, slots], ts_all[:].indirect(listed(slots)), twos[:], MULT)
-            nc.scalar.activation(ts_size[:, slots], ts_picked[:, slots], ACT.Abs)
+            nc.vector.tensor_tensor(ts_twice[:, slots], ts_all[:].indirect(listed(slots)), twos[:], MULT)
+            nc.scalar.activation(ts_size[:, slots], ts_twice[:, slots], ACT.Abs)
         for slots in halves:
             gather_h(0, slots)
-        nc.scalar.activation(ts_sign[:], ts_picked[:], ACT.Sign)
-        for t in range(1, PACK):
-            gather_h(t, slice(0, N))
-            for slots in halves if t < LAST else halves[:1]:
-                gather_dy(t - 1, slots)
-            if t - 1 == 1:
-                round_first_half_pair(0, halves[0])
-
-        for slots in quarters:
-            gather_dy(LAST, slots)
-            round_first_half_pair(1, slots)
-        gather_dy(LAST - 1, halves[1])
+            relu(0, slots)
+        gather_h(1, whole)
+        relu(1, whole)
+        nc.scalar.activation(ts_sign[:], ts_twice[:], ACT.Sign)
+        gather_dy(0, whole)
+        gather_h(2, whole)
+        relu(2, whole)
+        for slots in halves:
+            gather_dy(1, slots)
+        planes = work[:, : PACK * 3 * HALF].rearrange("p (t c) -> p t c", t=PACK)
+        round_and_interleave(dz16[0][:, :, 0:2], planes[:, 0:2, halves[0]])
         round_wm(0)
+        gather_h(3, whole)
+        relu(3, slice(0, QUARTER))
+        relu(3, slice(QUARTER, N))
+        gather_dy(2, halves[0])
+        quantize_wm(0)
+        late_pair = region(10, 0, N).rearrange("p (t c) -> p t c", t=2)
+        for slots in pieces:
+            gather_dy(3, slots)
+            round_and_interleave(dz16[0][:, slots, 2:4], late_pair[:, :, slots])
+        gather_dy(2, halves[1])
+        quantize_dz(halves[0])
+        acc00 = multiply(0, 0)
         round_wm(1)
-        nc.sync.dma_start(wm_late, wm_rows[:, :, 2 * P :])
-        quantize_dz(0, dz16_first)
-        quantize_wm(0, 1)
-        copy_out(0, 0, multiply(0, 0))
-        gather_dy(LAST, halves[1])
-        quantize_wm(1, 2)
-        acc1 = multiply(1, 0)
-        scatter(0, 0)
+        copy_out(0, 0, acc00)
+        gather_dy(3, halves[1])
+        quantize_wm(1)
+        acc10 = multiply(1, 0)
+        acc20 = multiply(2, 0)
+        scatter(0, halves[0])
+        round_and_interleave(dz16[1], planes[:, :, halves[1]])
+        copy_out(1, 0, acc10)
+        quantize_dz(halves[1])
+        scatter(1, halves[0])
         round_wm(2)
-        round_wm(3)
-        quantize_wm(2, 4)
-        copy_out(1, 0, acc1)
-        acc2 = multiply(2, 0)
-        acc3 = multiply(3, 0)
-        copy_out(2, 0, acc2)
-
-        dz16_second = keep.tile([P, HALF, PACK], BF16, name="dz16_second", tag="codes_then_bf16", align_bytes=MX_ALIGN)
-        round_and_interleave(dz16_second[:], shared[:, :PACK, :])
-        copy_out(3, 0, acc3)
-        scatter(1, 0)
-        scatter(2, 0)
-        quantize_dz(1, dz16_second)
-        for b in range(D_BLOCKS):
-            copy_out(b, 1, multiply(b, 1))
-        scatter(3, 0)
-        for b in range(D_BLOCKS):
-            scatter(b, 1)
-            nc.sync.dma_start(out[b * P : (b + 1) * P, :], out_rows[b][:])
+        quantize_wm(2)
+        copy_out(0, 1, multiply(0, 1))
+        scatter(0, halves[1])
+        store(0)
+        copy_out(2, 0, acc20)
+        copy_out(2, 1, multiply(2, 1))
+        scatter(2, whole)
+        store(2)
+        copy_out(1, 1, multiply(1, 1))
+        scatter(1, halves[1])
+        store(1)
+        for h in range(2):
+            copy_out(3, h, multiply(3, h))
+        scatter(3, whole)
+        store(3)

@@ -19,14 +19,19 @@ MULT = mybir.AluOpType.mult
 P = 128
 PACK = 4
 HALF = 512
-QUARTER = 256
+QUARTER = HALF // 2
 LIST_ROWS = 16
 D_BLOCKS = D // P
+PSUM_BANKS = 8
 LINE = 4
 MX_ALIGN = 64
-SPREAD_BANKS = 2
-SPREAD_COLS = 2
-SPREAD = SPREAD_BANKS * SPREAD_COLS * P
+
+SPREAD_BANKS = 3
+SPREAD_TURNS = 2
+SPREAD = SPREAD_BANKS * SPREAD_TURNS * P
+
+HELD = 256
+PITCH = 2 * N + QUARTER - HELD
 
 
 def tile_attend_gex_x_kernel(tc, dyT, hT, ts, wm, offs, out):
@@ -37,12 +42,11 @@ def tile_attend_gex_x_kernel(tc, dyT, hT, ts, wm, offs, out):
 
         offsets = keep.tile([P, N // LIST_ROWS], U16, name="offsets")
         ts_all = keep.tile([P, T], F32, name="ts_all")
-        ts_tail = keep.tile([P, SPREAD_BANKS, SPREAD_COLS], F32, name="ts_tail")
+        ts_tail = keep.tile([P, SPREAD_BANKS, SPREAD_TURNS], F32, name="ts_tail")
         identity = keep.tile([P, P], F32, name="identity")
         twos = keep.tile([P, HALF], F32, name="twos")
         h_all = [keep.tile([P, T], F32, name="h_all%d" % t) for t in range(PACK)]
         dy_all = [keep.tile([P, T], F32, name="dy_all%d" % t) for t in range(PACK)]
-        wm_blocks = [slice(0, 1), slice(1, 3), slice(3, 4)]
         out_rows = [keep.tile([P, T], F32, name="out_rows%d" % b) for b in range(D_BLOCKS)]
         dx = [keep.tile([P, N], F32, name="dx%d" % b) for b in range(D_BLOCKS)]
 
@@ -52,19 +56,30 @@ def tile_attend_gex_x_kernel(tc, dyT, hT, ts, wm, offs, out):
         ts_sign = h_scaled[1]
         slope = [keep.tile([P, N], F32, name="slope%d" % t) for t in range(PACK - 1)]
 
-        work = keep.tile([P, 13 * HALF], F32, name="work", align_bytes=MX_ALIGN)
+        work = keep.tile([P, PACK * PITCH], F32, name="work", align_bytes=MX_ALIGN)
+        planes = work[:].rearrange("p (t c) -> p t c", t=PACK)
+        dz16_first_at = PITCH + N - HELD
+        slope3_second_at = dz16_first_at + N
+        slope3_first_at = slope3_second_at + HALF
+        late_pair_at = 3 * PITCH + HALF
 
-        def region(r, start=0, stop=HALF):
-            return work[:, r * HALF + start : r * HALF + stop]
+        def columns(first, count):
+            return work[:, first : first + count]
 
-        def as_bf16(ap):
-            return ap.bitcast(BF16).rearrange("p (c t) -> p c t", t=PACK)
+        def as_bf16(cols):
+            return cols.bitcast(BF16).rearrange("p (c t) -> p c t", t=PACK)
 
-        dz16 = [keep.tile([P, HALF, PACK], BF16, name="dz16_first", align_bytes=MX_ALIGN)[:], as_bf16(region(11, 0, N))]
-        wm16 = [as_bf16(region(0, 0, QUARTER)), as_bf16(region(11)), as_bf16(region(1, 0, QUARTER))]
-        wm_raw = [region(6, QUARTER, QUARTER + HALF).rearrange("p (t d) -> p t d", t=PACK)] + [
-            keep.tile([P, PACK, (g.stop - g.start) * P], F32, name="wm_raw%d" % g.start)[:] for g in wm_blocks[1:]
+        late_pair = columns(late_pair_at, N).rearrange("p (t c) -> p t c", t=2)
+        dz16 = [as_bf16(columns(dz16_first_at, N)), as_bf16(columns(late_pair_at + HALF, N))]
+
+        wm_cols = [slice(0, P), slice(P, 3 * P), slice(3 * P, D)]
+        wm_raw = [
+            columns(slope3_first_at - QUARTER, HALF).rearrange("p (t d) -> p t d", t=PACK),
+            keep.tile([P, PACK, 2 * P], F32, name="wm_raw1")[:],
+            keep.tile([P, PACK, P], F32, name="wm_raw3")[:],
         ]
+        wm16 = [as_bf16(columns(0, QUARTER)), as_bf16(columns(late_pair_at + HALF, HALF)), as_bf16(columns(HALF, QUARTER))]
+
         dz_codes = keep.tile([P, N], U32, name="dz_codes", align_bytes=MX_ALIGN)
         dz_scales = keep.tile([P, N], U8, name="dz_scales", align_bytes=MX_ALIGN)
         wm_codes = keep.tile([P, D], U32, name="wm_codes", align_bytes=MX_ALIGN)
@@ -75,11 +90,9 @@ def tile_attend_gex_x_kernel(tc, dyT, hT, ts, wm, offs, out):
         wm_rows = wm.rearrange("b (p t) d -> p (b t) d", t=PACK)
 
         def load_wm(g):
-            nc.sync.dma_start(wm_raw[g], wm_rows[:, :, wm_blocks[g].start * P : wm_blocks[g].stop * P])
+            nc.sync.dma_start(wm_raw[g], wm_rows[:, :, wm_cols[g]])
 
-        nc.sync.dma_start(
-            ts_tail[:], ts[0:1, T - SPREAD :].rearrange("o (r p j) -> (o p) r j", r=SPREAD_BANKS, p=P)
-        )
+        nc.sync.dma_start(ts_tail[:], ts[0:1, T - SPREAD :].rearrange("o (r p j) -> (o p) r j", r=SPREAD_BANKS, p=P))
         nc.sync.dma_start(ts_all[:, : T - SPREAD], ts[:, : T - SPREAD])
         nc.sync.dma_start(offsets[:], offs)
         nc.sync.dma_start(h_all[0][:], h_rows[:, 0, :])
@@ -93,13 +106,15 @@ def tile_attend_gex_x_kernel(tc, dyT, hT, ts, wm, offs, out):
 
         make_identity(nc, identity[:])
         for r in range(SPREAD_BANKS):
-            spread = psum.tile([P, SPREAD_COLS, P], F32, name="spread%d" % r, tag="bank%d" % (6 + r))
-            for j in range(SPREAD_COLS):
+            bank = PSUM_BANKS - SPREAD_BANKS + r
+            spread = psum.tile([P, SPREAD_TURNS, P], F32, name="spread%d" % r, tag="bank%d" % bank)
+            for j in range(SPREAD_TURNS):
                 nc.tensor.transpose(spread[:, j, :], ts_tail[:, r, j : j + 1].to_broadcast([P, P]), identity[:])
-            first = T - SPREAD + r * SPREAD_COLS * P
-            nc.vector.tensor_copy(
-                ts_all[:, first : first + SPREAD_COLS * P].rearrange("p (n j) -> p n j", n=P),
+            first = T - SPREAD + r * SPREAD_TURNS * P
+            nc.scalar.activation(
+                ts_all[:, first : first + SPREAD_TURNS * P].rearrange("p (n j) -> p n j", n=P),
                 spread[:].rearrange("p j n -> p n j"),
+                ACT.Copy,
             )
         nc.gpsimd.memset(twos[:], 2.0)
         for rows in out_rows:
@@ -107,7 +122,6 @@ def tile_attend_gex_x_kernel(tc, dyT, hT, ts, wm, offs, out):
 
         whole = slice(0, N)
         halves = [slice(0, HALF), slice(HALF, N)]
-        pieces = [slice(0, 128), slice(128, 256), slice(256, 512)]
 
         def listed(slots):
             return offsets[:, slots.start // LIST_ROWS : slots.stop // LIST_ROWS]
@@ -115,12 +129,13 @@ def tile_attend_gex_x_kernel(tc, dyT, hT, ts, wm, offs, out):
         def slope_at(t, slots):
             if t < 3:
                 return slope[t][:, slots]
-            return region(7 if slots.stop <= QUARTER else 5, slots.start, slots.stop)
+            first = slope3_first_at if slots.stop <= HALF else slope3_second_at - HALF
+            return columns(first + slots.start, slots.stop - slots.start)
 
         def dz_at(t, slots):
             if t >= 2 and slots.stop <= HALF:
-                return region(8 + t, slots.start, slots.stop)
-            return region(3 * t, slots.start, slots.stop)
+                return late_pair[:, t - 2, slots]
+            return planes[:, t, slots]
 
         def gather_h(t, slots):
             nc.vector.tensor_tensor(h_scaled[t][:, slots], h_all[t][:].indirect(listed(slots)), ts_size[:, slots], MULT)
@@ -150,10 +165,9 @@ def tile_attend_gex_x_kernel(tc, dyT, hT, ts, wm, offs, out):
             )
 
         def quantize_wm(g):
-            cols = slice(wm_blocks[g].start * P, wm_blocks[g].stop * P)
             nc.vector.quantize_mx(
-                out=wm_codes[:, cols].bitcast(E4M3X4),
-                scales=wm_scales[:, cols],
+                out=wm_codes[:, wm_cols[g]].bitcast(E4M3X4),
+                scales=wm_scales[:, wm_cols[g]],
                 in_=wm16[g].rearrange("p c t -> p (c t)"),
             )
 
@@ -192,29 +206,30 @@ def tile_attend_gex_x_kernel(tc, dyT, hT, ts, wm, offs, out):
         gather_dy(0, whole)
         gather_h(2, whole)
         relu(2, whole)
-        for slots in halves:
-            gather_dy(1, slots)
-        planes = work[:, : PACK * 3 * HALF].rearrange("p (t c) -> p t c", t=PACK)
+        gather_dy(1, slice(0, N - HELD))
         round_and_interleave(dz16[0][:, :, 0:2], planes[:, 0:2, halves[0]])
         round_wm(0)
         gather_h(3, whole)
-        relu(3, slice(0, QUARTER))
-        relu(3, slice(QUARTER, N))
+        for slots in halves:
+            relu(3, slots)
         gather_dy(2, halves[0])
         quantize_wm(0)
-        late_pair = region(10, 0, N).rearrange("p (t c) -> p t c", t=2)
-        for slots in pieces:
+
+        for slots in (slice(QUARTER, QUARTER + P), slice(QUARTER + P, HALF), slice(0, QUARTER)):
             gather_dy(3, slots)
             round_and_interleave(dz16[0][:, slots, 2:4], late_pair[:, :, slots])
         gather_dy(2, halves[1])
-        quantize_dz(halves[0])
+        quantize_dz(slice(QUARTER, HALF))
+        quantize_dz(slice(0, QUARTER))
         acc00 = multiply(0, 0)
         round_wm(1)
         copy_out(0, 0, acc00)
         gather_dy(3, halves[1])
+        gather_dy(1, slice(N - HELD, N))
         quantize_wm(1)
         acc10 = multiply(1, 0)
         acc20 = multiply(2, 0)
+
         scatter(0, halves[0])
         round_and_interleave(dz16[1], planes[:, :, halves[1]])
         copy_out(1, 0, acc10)

@@ -24,9 +24,10 @@ LIST_ROWS = 16
 D_BLOCKS = D // P
 PSUM_BANKS = 8
 LINE = 4
+BLOCK = 8
 MX_ALIGN = 64
 
-SPREAD_BANKS = 3
+SPREAD_BANKS = 5
 SPREAD_TURNS = 2
 SPREAD = SPREAD_BANKS * SPREAD_TURNS * P
 
@@ -42,7 +43,7 @@ def tile_attend_gex_x_kernel(tc, dyT, hT, ts, wm, offs, out):
 
         offsets = keep.tile([P, N // LIST_ROWS], U16, name="offsets")
         ts_all = keep.tile([P, T], F32, name="ts_all")
-        ts_tail = keep.tile([P, SPREAD_BANKS, SPREAD_TURNS], F32, name="ts_tail")
+        ts_tail = keep.tile([P, SPREAD_BANKS, BLOCK], F32, name="ts_tail")
         identity = keep.tile([P, P], F32, name="identity")
         twos = keep.tile([P, HALF], F32, name="twos")
         h_all = [keep.tile([P, T], F32, name="h_all%d" % t) for t in range(PACK)]
@@ -92,7 +93,7 @@ def tile_attend_gex_x_kernel(tc, dyT, hT, ts, wm, offs, out):
         def load_wm(g):
             nc.sync.dma_start(wm_raw[g], wm_rows[:, :, wm_cols[g]])
 
-        nc.sync.dma_start(ts_tail[:], ts[0:1, T - SPREAD :].rearrange("o (r p j) -> (o p) r j", r=SPREAD_BANKS, p=P))
+        nc.sync.dma_start(ts_tail[:, :, :SPREAD_TURNS], ts[0:1, T - SPREAD :].rearrange("o (r p j) -> (o p) r j", r=SPREAD_BANKS, p=P))
         nc.sync.dma_start(ts_all[:, : T - SPREAD], ts[:, : T - SPREAD])
         nc.sync.dma_start(offsets[:], offs)
         nc.sync.dma_start(h_all[0][:], h_rows[:, 0, :])
@@ -111,11 +112,11 @@ def tile_attend_gex_x_kernel(tc, dyT, hT, ts, wm, offs, out):
             for j in range(SPREAD_TURNS):
                 nc.tensor.transpose(spread[:, j, :], ts_tail[:, r, j : j + 1].to_broadcast([P, P]), identity[:])
             first = T - SPREAD + r * SPREAD_TURNS * P
-            nc.scalar.activation(
-                ts_all[:, first : first + SPREAD_TURNS * P].rearrange("p (n j) -> p n j", n=P),
-                spread[:].rearrange("p j n -> p n j"),
-                ACT.Copy,
-            )
+            dst = ts_all[:, first : first + SPREAD_TURNS * P].rearrange("p (n j) -> p n j", n=P)
+            if r % 2:
+                nc.vector.tensor_copy(dst, spread[:].rearrange("p j n -> p n j"))
+            else:
+                nc.scalar.activation(dst, spread[:].rearrange("p j n -> p n j"), ACT.Copy)
         nc.gpsimd.memset(twos[:], 2.0)
         for rows in out_rows:
             nc.gpsimd.memset(rows[:], 0.0)

@@ -27,7 +27,7 @@ LINE = 4
 BLOCK = 8
 MX_ALIGN = 64
 
-SPREAD_BANKS = 5
+SPREAD_BANKS = 4
 SPREAD_TURNS = 2
 SPREAD = SPREAD_BANKS * SPREAD_TURNS * P
 
@@ -75,11 +75,12 @@ def tile_attend_gex_x_kernel(tc, dyT, hT, ts, wm, offs, out):
 
         wm_cols = [slice(0, P), slice(P, 3 * P), slice(3 * P, D)]
         wm_raw = [
-            columns(slope3_first_at - QUARTER, HALF).rearrange("p (t d) -> p t d", t=PACK),
+            keep.tile([P, PACK, P], F32, name="wm_raw0")[:],
             keep.tile([P, PACK, 2 * P], F32, name="wm_raw1")[:],
             keep.tile([P, PACK, P], F32, name="wm_raw3")[:],
         ]
-        wm16 = [as_bf16(columns(0, QUARTER)), as_bf16(columns(late_pair_at + HALF, HALF)), as_bf16(columns(HALF, QUARTER))]
+        wm16_first = keep.tile([P, QUARTER], F32, name="wm16_first", align_bytes=MX_ALIGN)
+        wm16 = [as_bf16(wm16_first[:]), as_bf16(columns(late_pair_at + HALF, HALF)), as_bf16(columns(HALF, QUARTER))]
 
         dz_codes = keep.tile([P, N], U32, name="dz_codes", align_bytes=MX_ALIGN)
         dz_scales = keep.tile([P, N], U8, name="dz_scales", align_bytes=MX_ALIGN)
@@ -94,13 +95,13 @@ def tile_attend_gex_x_kernel(tc, dyT, hT, ts, wm, offs, out):
             nc.sync.dma_start(wm_raw[g], wm_rows[:, :, wm_cols[g]])
 
         nc.sync.dma_start(ts_tail[:, :, :SPREAD_TURNS], ts[0:1, T - SPREAD :].rearrange("o (r p j) -> (o p) r j", r=SPREAD_BANKS, p=P))
+        load_wm(0)
         nc.sync.dma_start(ts_all[:, : T - SPREAD], ts[:, : T - SPREAD])
         nc.sync.dma_start(offsets[:], offs)
         nc.sync.dma_start(h_all[0][:], h_rows[:, 0, :])
         for t in range(1, PACK):
             nc.sync.dma_start(h_all[t][:], h_rows[:, t, :])
             nc.sync.dma_start(dy_all[t - 1][:], dy_rows[:, t - 1, :])
-        load_wm(0)
         nc.sync.dma_start(dy_all[3][:], dy_rows[:, 3, :])
         load_wm(1)
         load_wm(2)
@@ -113,10 +114,7 @@ def tile_attend_gex_x_kernel(tc, dyT, hT, ts, wm, offs, out):
                 nc.tensor.transpose(spread[:, j, :], ts_tail[:, r, j : j + 1].to_broadcast([P, P]), identity[:])
             first = T - SPREAD + r * SPREAD_TURNS * P
             dst = ts_all[:, first : first + SPREAD_TURNS * P].rearrange("p (n j) -> p n j", n=P)
-            if r % 2:
-                nc.vector.tensor_copy(dst, spread[:].rearrange("p j n -> p n j"))
-            else:
-                nc.scalar.activation(dst, spread[:].rearrange("p j n -> p n j"), ACT.Copy)
+            nc.scalar.activation(dst, spread[:].rearrange("p j n -> p n j"), ACT.Copy)
         nc.gpsimd.memset(twos[:], 2.0)
         for rows in out_rows:
             nc.gpsimd.memset(rows[:], 0.0)
@@ -195,6 +193,10 @@ def tile_attend_gex_x_kernel(tc, dyT, hT, ts, wm, offs, out):
         def store(b):
             nc.sync.dma_start(out[b * P : (b + 1) * P, :], out_rows[b][:])
 
+        nc.vector.tensor_copy(
+            wm16[0].rearrange("p (c i) t -> p c t i", i=LINE), wm_raw[0].rearrange("p t (c i) -> p c t i", i=LINE)
+        )
+        quantize_wm(0)
         for slots in halves:
             nc.vector.tensor_tensor(ts_twice[:, slots], ts_all[:].indirect(listed(slots)), twos[:], MULT)
             nc.scalar.activation(ts_size[:, slots], ts_twice[:, slots], ACT.Abs)
@@ -209,12 +211,10 @@ def tile_attend_gex_x_kernel(tc, dyT, hT, ts, wm, offs, out):
         relu(2, whole)
         gather_dy(1, slice(0, N - HELD))
         round_and_interleave(dz16[0][:, :, 0:2], planes[:, 0:2, halves[0]])
-        round_wm(0)
         gather_h(3, whole)
         for slots in halves:
             relu(3, slots)
         gather_dy(2, halves[0])
-        quantize_wm(0)
 
         for slots in (slice(QUARTER, QUARTER + P), slice(QUARTER + P, HALF), slice(0, QUARTER)):
             gather_dy(3, slots)

@@ -9,6 +9,7 @@ FLOPS = 2 * N * D * DV
 F32 = mybir.dt.float32
 BF16 = mybir.dt.bfloat16
 U32 = mybir.dt.uint32
+I32 = mybir.dt.int32
 U16 = mybir.dt.uint16
 U8 = mybir.dt.uint8
 E4M3X4 = mybir.dt.float8_e4m3fn_x4
@@ -29,6 +30,7 @@ MX_ALIGN = 64
 
 SPREAD_BANKS = 4
 SPREAD_TURNS = 2
+TURNS = QUARTER // P
 SPREAD = SPREAD_BANKS * SPREAD_TURNS * P
 
 HELD = 256
@@ -43,17 +45,17 @@ def tile_attend_gex_x_kernel(tc, dyT, hT, ts, wm, offs, out):
 
         offsets = keep.tile([P, N // LIST_ROWS], U16, name="offsets")
         ts_all = keep.tile([P, T], F32, name="ts_all")
-        ts_tail = keep.tile([P, SPREAD_BANKS, BLOCK], F32, name="ts_tail")
+        ts_down = [keep.tile([P, TURNS], F32, name="ts_down%d" % q) for q in range(N // QUARTER)]
         identity = keep.tile([P, P], F32, name="identity")
-        twos = keep.tile([P, HALF], F32, name="twos")
-        h_all = [keep.tile([P, T], F32, name="h_all%d" % t) for t in range(PACK)]
-        dy_all = [keep.tile([P, T], F32, name="dy_all%d" % t) for t in range(PACK)]
-        out_rows = [keep.tile([P, T], F32, name="out_rows%d" % b) for b in range(D_BLOCKS)]
+        twos = keep.tile([P, QUARTER], F32, name="twos")
+        h_all = [keep.tile([P, T], F32, name="h_all%d" % t, tag="h_all%d" % t) for t in range(PACK)]
+        dy_all = [keep.tile([P, T], F32, name="dy_all%d" % t, tag="dy_all%d" % t) for t in range(PACK)]
         dx = [keep.tile([P, N], F32, name="dx%d" % b) for b in range(D_BLOCKS)]
 
         ts_twice = keep.tile([P, N], F32, name="ts_twice")
         ts_size = keep.tile([P, N], F32, name="ts_size")
-        h_scaled = [keep.tile([P, N], F32, name="h_scaled%d" % t) for t in range(PACK)]
+        h_scaled = [keep.tile([P, N], F32, name="h_scaled%d" % t) for t in (0, 1, 3)]
+        h_scaled = [h_scaled[0], h_scaled[1], h_scaled[0], h_scaled[2]]
         ts_sign = h_scaled[1]
         slope = [keep.tile([P, N], F32, name="slope%d" % t) for t in range(PACK - 1)]
 
@@ -94,10 +96,9 @@ def tile_attend_gex_x_kernel(tc, dyT, hT, ts, wm, offs, out):
         def load_wm(g):
             nc.sync.dma_start(wm_raw[g], wm_rows[:, :, wm_cols[g]])
 
-        nc.sync.dma_start(ts_tail[:, :, :SPREAD_TURNS], ts[0:1, T - SPREAD :].rearrange("o (r p j) -> (o p) r j", r=SPREAD_BANKS, p=P))
-        load_wm(0)
-        nc.sync.dma_start(ts_all[:, : T - SPREAD], ts[:, : T - SPREAD])
         nc.sync.dma_start(offsets[:], offs)
+        nc.sync.dma_start(ts_all[P - 1 :, :], ts[0:1, :])
+        load_wm(0)
         nc.sync.dma_start(h_all[0][:], h_rows[:, 0, :])
         for t in range(1, PACK):
             nc.sync.dma_start(h_all[t][:], h_rows[:, t, :])
@@ -106,18 +107,15 @@ def tile_attend_gex_x_kernel(tc, dyT, hT, ts, wm, offs, out):
         load_wm(1)
         load_wm(2)
 
-        make_identity(nc, identity[:])
-        for r in range(SPREAD_BANKS):
-            bank = PSUM_BANKS - SPREAD_BANKS + r
-            spread = psum.tile([P, SPREAD_TURNS, P], F32, name="spread%d" % r, tag="bank%d" % bank)
-            for j in range(SPREAD_TURNS):
-                nc.tensor.transpose(spread[:, j, :], ts_tail[:, r, j : j + 1].to_broadcast([P, P]), identity[:])
-            first = T - SPREAD + r * SPREAD_TURNS * P
-            dst = ts_all[:, first : first + SPREAD_TURNS * P].rearrange("p (n j) -> p n j", n=P)
-            nc.scalar.activation(dst, spread[:].rearrange("p j n -> p n j"), ACT.Copy)
         nc.gpsimd.memset(twos[:], 2.0)
-        for rows in out_rows:
-            nc.gpsimd.memset(rows[:], 0.0)
+        nc.vector.memset(ts_all[: P - 1, :].bitcast(I32), 0)
+        make_identity(nc, identity[:])
+        out_rows = []
+
+        def zero_next_block():
+            b = len(out_rows)
+            out_rows.append(keep.tile([P, T], F32, name="out_rows%d" % b, tag=("h_all0", "h_all1", "dy_all0", "h_all2")[b]))
+            nc.gpsimd.memset(out_rows[b][:], 0.0)
 
         whole = slice(0, N)
         halves = [slice(0, HALF), slice(HALF, N)]
@@ -193,22 +191,33 @@ def tile_attend_gex_x_kernel(tc, dyT, hT, ts, wm, offs, out):
         def store(b):
             nc.sync.dma_start(out[b * P : (b + 1) * P, :], out_rows[b][:])
 
-        nc.vector.tensor_copy(
-            wm16[0].rearrange("p (c i) t -> p c t i", i=LINE), wm_raw[0].rearrange("p t (c i) -> p c t i", i=LINE)
-        )
-        quantize_wm(0)
-        for slots in halves:
+        quarters = [slice(q * QUARTER, (q + 1) * QUARTER) for q in range(N // QUARTER)]
+        spread = []
+        for q, slots in enumerate(quarters):
             nc.vector.tensor_tensor(ts_twice[:, slots], ts_all[:].indirect(listed(slots)), twos[:], MULT)
-            nc.scalar.activation(ts_size[:, slots], ts_twice[:, slots], ACT.Abs)
-        for slots in halves:
+            turned = psum.tile([P, TURNS, P], F32, name="turned%d" % q, tag="bank%d" % (q % 2))
+            for j in range(TURNS):
+                first = slots.start + j * P
+                nc.tensor.transpose(turned[:, j, :], ts_twice[:, first : first + P], identity[:])
+            nc.scalar.activation(ts_down[q][:], turned[:, :, P - 1], ACT.Copy)
+            spread.append(psum.tile([P, QUARTER], F32, name="spread%d" % q, tag="bank%d" % (PSUM_BANKS - 4 + q)))
+            for j in range(TURNS):
+                nc.tensor.transpose(spread[q][:, j * P : (j + 1) * P], ts_down[q][:, j : j + 1].to_broadcast([P, P]), identity[:])
+            nc.scalar.activation(ts_size[:, slots], spread[q][:], ACT.Abs)
+        round_wm(0)
+        quantize_wm(0)
+        for slots in quarters:
             gather_h(0, slots)
-            relu(0, slots)
+        relu(0, whole)
         gather_h(1, whole)
         relu(1, whole)
-        nc.scalar.activation(ts_sign[:], ts_twice[:], ACT.Sign)
+        for q, slots in enumerate(quarters):
+            nc.scalar.activation(ts_sign[:, slots], spread[q][:], ACT.Sign)
         gather_dy(0, whole)
         gather_h(2, whole)
         relu(2, whole)
+        for b in range(D_BLOCKS):
+            zero_next_block()
         gather_dy(1, slice(0, N - HELD))
         round_and_interleave(dz16[0][:, :, 0:2], planes[:, 0:2, halves[0]])
         gather_h(3, whole)

@@ -96,8 +96,8 @@ def tile_attend_gex_x_kernel(tc, dyT, hT, ts, wm, offs, out):
         def load_wm(g):
             nc.sync.dma_start(wm_raw[g], wm_rows[:, :, wm_cols[g]])
 
-        nc.sync.dma_start(offsets[:], offs)
         nc.sync.dma_start(ts_all[P - 1 :, :], ts[0:1, :])
+        nc.sync.dma_start(offsets[:], offs)
         load_wm(0)
         nc.sync.dma_start(h_all[0][:], h_rows[:, 0, :])
         for t in range(1, PACK):
@@ -107,7 +107,7 @@ def tile_attend_gex_x_kernel(tc, dyT, hT, ts, wm, offs, out):
         load_wm(1)
         load_wm(2)
 
-        nc.gpsimd.memset(twos[:], 2.0)
+        nc.vector.memset(twos[:], 2.0)
         nc.vector.memset(ts_all[: P - 1, :].bitcast(I32), 0)
         make_identity(nc, identity[:])
         out_rows = []

@@ -20,18 +20,16 @@ MULT = mybir.AluOpType.mult
 P = 128
 PACK = 4
 HALF = 512
-QUARTER = HALF // 2
+QUARTER = 256
 LIST_ROWS = 16
 D_BLOCKS = D // P
-PSUM_BANKS = 8
 LINE = 4
-BLOCK = 8
 MX_ALIGN = 64
-
-SPREAD_BANKS = 4
-SPREAD_TURNS = 2
-TURNS = QUARTER // P
-SPREAD = SPREAD_BANKS * SPREAD_TURNS * P
+TURNS = HALF // P
+PSUM_BANKS = 8
+LINE2 = 4
+BLOCK = 8
+MX2 = 64
 
 HELD = 256
 PITCH = 2 * N + QUARTER - HELD
@@ -45,18 +43,16 @@ def tile_attend_gex_x_kernel(tc, dyT, hT, ts, wm, offs, out):
 
         offsets = keep.tile([P, N // LIST_ROWS], U16, name="offsets")
         ts_all = keep.tile([P, T], F32, name="ts_all")
-        ts_down = [keep.tile([P, TURNS], F32, name="ts_down%d" % q) for q in range(N // QUARTER)]
         identity = keep.tile([P, P], F32, name="identity")
-        twos = keep.tile([P, QUARTER], F32, name="twos")
+        twos = keep.tile([P, HALF], F32, name="twos")
         h_all = [keep.tile([P, T], F32, name="h_all%d" % t, tag="h_all%d" % t) for t in range(PACK)]
         dy_all = [keep.tile([P, T], F32, name="dy_all%d" % t, tag="dy_all%d" % t) for t in range(PACK)]
         dx = [keep.tile([P, N], F32, name="dx%d" % b) for b in range(D_BLOCKS)]
 
         ts_twice = keep.tile([P, N], F32, name="ts_twice")
         ts_size = keep.tile([P, N], F32, name="ts_size")
-        h_scaled = [keep.tile([P, N], F32, name="h_scaled%d" % t) for t in (0, 1, 3)]
-        h_scaled = [h_scaled[0], h_scaled[1], h_scaled[0], h_scaled[2]]
-        ts_sign = h_scaled[1]
+        h_scaled = [keep.tile([P, N], F32, name="h_scaled%d" % t) for t in range(PACK)]
+        ts_sign = h_scaled[0]
         slope = [keep.tile([P, N], F32, name="slope%d" % t) for t in range(PACK - 1)]
 
         work = keep.tile([P, PACK * PITCH], F32, name="work", align_bytes=MX_ALIGN)
@@ -98,12 +94,12 @@ def tile_attend_gex_x_kernel(tc, dyT, hT, ts, wm, offs, out):
 
         nc.sync.dma_start(ts_all[P - 1 :, :], ts[0:1, :])
         nc.sync.dma_start(offsets[:], offs)
+        for tiles, rows, t in (
+            (h_all, h_rows, 1), (h_all, h_rows, 0), (h_all, h_rows, 2), (dy_all, dy_rows, 0),
+            (dy_all, dy_rows, 1), (h_all, h_rows, 3), (dy_all, dy_rows, 2), (dy_all, dy_rows, 3),
+        ):
+            nc.sync.dma_start(tiles[t][:], rows[:, t, :])
         load_wm(0)
-        nc.sync.dma_start(h_all[0][:], h_rows[:, 0, :])
-        for t in range(1, PACK):
-            nc.sync.dma_start(h_all[t][:], h_rows[:, t, :])
-            nc.sync.dma_start(dy_all[t - 1][:], dy_rows[:, t - 1, :])
-        nc.sync.dma_start(dy_all[3][:], dy_rows[:, 3, :])
         load_wm(1)
         load_wm(2)
 
@@ -114,7 +110,7 @@ def tile_attend_gex_x_kernel(tc, dyT, hT, ts, wm, offs, out):
 
         def zero_next_block():
             b = len(out_rows)
-            out_rows.append(keep.tile([P, T], F32, name="out_rows%d" % b, tag=("h_all0", "h_all1", "dy_all0", "h_all2")[b]))
+            out_rows.append(keep.tile([P, T], F32, name="out_rows%d" % b, tag=("h_all1", "h_all0", "h_all2", "dy_all0")[b]))
             nc.gpsimd.memset(out_rows[b][:], 0.0)
 
         whole = slice(0, N)
@@ -170,7 +166,7 @@ def tile_attend_gex_x_kernel(tc, dyT, hT, ts, wm, offs, out):
 
         def multiply(b, h):
             cols = slice(b * P, (b + 1) * P)
-            acc = psum.tile([P, HALF], F32, name="bank%d_%d" % (b, h), tag="bank%d" % (2 * b + h))
+            acc = psum.tile([P, HALF], F32, name="bank%d_%d" % (b, h), tag="bank%d" % ((2 * b + h) % 7))
             nc.tensor.matmul_mx(
                 out=acc[:],
                 lhsT=wm_codes[:, cols].bitcast(E4M3X4),
@@ -191,31 +187,45 @@ def tile_attend_gex_x_kernel(tc, dyT, hT, ts, wm, offs, out):
         def store(b):
             nc.sync.dma_start(out[b * P : (b + 1) * P, :], out_rows[b][:])
 
-        quarters = [slice(q * QUARTER, (q + 1) * QUARTER) for q in range(N // QUARTER)]
-        spread = []
-        for q, slots in enumerate(quarters):
+        def bank(shape, name, k):
+            return psum.tile(shape, F32, name=name, tag="bank%d" % k)
+
+        def turn(dst, src):
+            for j in range(TURNS):
+                nc.tensor.transpose(dst[:, j, :], src(j), identity[:])
+
+        spread, size_down = [], []
+        for h, slots in enumerate(halves):
             nc.vector.tensor_tensor(ts_twice[:, slots], ts_all[:].indirect(listed(slots)), twos[:], MULT)
-            turned = psum.tile([P, TURNS, P], F32, name="turned%d" % q, tag="bank%d" % (q % 2))
-            for j in range(TURNS):
-                first = slots.start + j * P
-                nc.tensor.transpose(turned[:, j, :], ts_twice[:, first : first + P], identity[:])
-            nc.scalar.activation(ts_down[q][:], turned[:, :, P - 1], ACT.Copy)
-            spread.append(psum.tile([P, QUARTER], F32, name="spread%d" % q, tag="bank%d" % (PSUM_BANKS - 4 + q)))
-            for j in range(TURNS):
-                nc.tensor.transpose(spread[q][:, j * P : (j + 1) * P], ts_down[q][:, j : j + 1].to_broadcast([P, P]), identity[:])
-            nc.scalar.activation(ts_size[:, slots], spread[q][:], ACT.Abs)
-        round_wm(0)
-        quantize_wm(0)
-        for slots in quarters:
+            turned = bank([P, TURNS, P], "ts_turned%d" % h, 0)
+            turn(turned, lambda j: ts_twice[:, slots.start + j * P : slots.start + (j + 1) * P])
+            ts_down = keep.tile([P, TURNS], F32, name="ts_down%d" % h)
+            nc.scalar.activation(ts_down[:], turned[:, :, P - 1], ACT.Copy)
+            spread.append(bank([P, TURNS, P], "spread%d" % h, 5 + h))
+            turn(spread[h], lambda j: ts_down[:, j : j + 1].to_broadcast([P, P]))
+            nc.scalar.activation(ts_size[:, slots], spread[h][:].rearrange("p j s -> p (j s)"), ACT.Abs)
+            size_down.append(keep.tile([P, TURNS], F32, name="size_down%d" % h))
+            nc.scalar.activation(size_down[h][:], ts_down[:], ACT.Abs, scale=0.5)
+        for slots in halves:
+            nc.vector.tensor_tensor(h_scaled[1][:, slots], h_all[1][:].indirect(listed(slots)), twos[:], MULT)
+        for slots in halves:
             gather_h(0, slots)
+        h_turned = bank([P, 2, TURNS, P], "h_turned", 0)
+        for h, slots in enumerate(halves):
+            turned = h_turned[:, h]
+            turn(turned, lambda j: h_scaled[1][:, slots.start + j * P : slots.start + (j + 1) * P])
+            slope_down = keep.tile([P, TURNS, P], F32, name="slope_down%d" % h)
+            for j in range(TURNS):
+                nc.scalar.activation(slope_down[:, j, :], turned[:, j, :], ACT.Relu, scale=size_down[h][:, j : j + 1])
+            back = bank([P, TURNS, P], "slope_back%d" % h, 3 + h)
+            turn(back, lambda j: slope_down[:, j, :])
+            nc.scalar.activation(slope[1][:, slots], back[:].rearrange("p j s -> p (j s)"), ACT.Copy)
         relu(0, whole)
-        gather_h(1, whole)
-        relu(1, whole)
-        for q, slots in enumerate(quarters):
-            nc.scalar.activation(ts_sign[:, slots], spread[q][:], ACT.Sign)
-        gather_dy(0, whole)
         gather_h(2, whole)
         relu(2, whole)
+        for h, slots in enumerate(halves):
+            nc.scalar.activation(ts_sign[:, slots], spread[h][:].rearrange("p j s -> p (j s)"), ACT.Sign)
+        gather_dy(0, whole)
         for b in range(D_BLOCKS):
             zero_next_block()
         gather_dy(1, slice(0, N - HELD))
@@ -227,9 +237,12 @@ def tile_attend_gex_x_kernel(tc, dyT, hT, ts, wm, offs, out):
 
         for slots in (slice(QUARTER, QUARTER + P), slice(QUARTER + P, HALF), slice(0, QUARTER)):
             gather_dy(3, slots)
+            if slots.start == 0:
+                round_wm(0)
             round_and_interleave(dz16[0][:, slots, 2:4], late_pair[:, :, slots])
         gather_dy(2, halves[1])
         quantize_dz(slice(QUARTER, HALF))
+        quantize_wm(0)
         quantize_dz(slice(0, QUARTER))
         acc00 = multiply(0, 0)
         round_wm(1)

@@ -31,7 +31,7 @@ LINE2 = 4
 BLOCK = 8
 MX2 = 64
 
-HELD = 256
+HELD = 192
 PITCH = 2 * N + QUARTER - HELD
 
 
@@ -194,20 +194,23 @@ def tile_attend_gex_x_kernel(tc, dyT, hT, ts, wm, offs, out):
             for j in range(TURNS):
                 nc.tensor.transpose(dst[:, j, :], src(j), identity[:])
 
-        spread, size_down = [], []
-        for h, slots in enumerate(halves):
-            nc.vector.tensor_tensor(ts_twice[:, slots], ts_all[:].indirect(listed(slots)), twos[:], MULT)
-            turned = bank([P, TURNS, P], "ts_turned%d" % h, 0)
-            turn(turned, lambda j: ts_twice[:, slots.start + j * P : slots.start + (j + 1) * P])
-            ts_down = keep.tile([P, TURNS], F32, name="ts_down%d" % h)
-            nc.scalar.activation(ts_down[:], turned[:, :, P - 1], ACT.Copy)
-            spread.append(bank([P, TURNS, P], "spread%d" % h, 5 + h))
-            turn(spread[h], lambda j: ts_down[:, j : j + 1].to_broadcast([P, P]))
-            nc.scalar.activation(ts_size[:, slots], spread[h][:].rearrange("p j s -> p (j s)"), ACT.Abs)
-            size_down.append(keep.tile([P, TURNS], F32, name="size_down%d" % h))
-            nc.scalar.activation(size_down[h][:], ts_down[:], ACT.Abs, scale=0.5)
-        for slots in halves:
-            nc.vector.tensor_tensor(h_scaled[1][:, slots], h_all[1][:].indirect(listed(slots)), twos[:], MULT)
+        spread = [bank([P, TURNS, P], "spread%d" % h, 5 + h) for h in range(2)]
+        ts_down = keep.tile([P, N // P], F32, name="ts_down")
+        size_down = keep.tile([P, N // P], F32, name="size_down")
+        for k, first, count in ((0, 0, 2), (3, 2, 2), (0, 4, 4)):
+            slots = slice(first * P, (first + count) * P)
+            nc.vector.tensor_tensor(ts_twice[:, slots], ts_all[:].indirect(listed(slots)), twos[:, : count * P], MULT)
+            turned = bank([P, count, P], "ts_turned%d" % first, k)
+            for j in range(count):
+                nc.tensor.transpose(turned[:, j, :], ts_twice[:, (first + j) * P : (first + j + 1) * P], identity[:])
+            nc.scalar.activation(ts_down[:, first : first + count], turned[:, :, P - 1], ACT.Copy)
+            for j in range(first, first + count):
+                nc.tensor.transpose(spread[j // TURNS][:, j % TURNS, :], ts_down[:, j : j + 1].to_broadcast([P, P]), identity[:])
+            if first:
+                h = first // TURNS
+                nc.scalar.activation(ts_size[:, halves[h]], spread[h][:].rearrange("p j s -> p (j s)"), ACT.Abs)
+        nc.scalar.activation(size_down[:], ts_down[:], ACT.Abs)
+        nc.vector.tensor_copy(h_scaled[1][:], h_all[1][:].indirect(listed(whole)))
         for slots in halves:
             gather_h(0, slots)
         h_turned = bank([P, 2, TURNS, P], "h_turned", 0)
@@ -216,7 +219,7 @@ def tile_attend_gex_x_kernel(tc, dyT, hT, ts, wm, offs, out):
             turn(turned, lambda j: h_scaled[1][:, slots.start + j * P : slots.start + (j + 1) * P])
             slope_down = keep.tile([P, TURNS, P], F32, name="slope_down%d" % h)
             for j in range(TURNS):
-                nc.scalar.activation(slope_down[:, j, :], turned[:, j, :], ACT.Relu, scale=size_down[h][:, j : j + 1])
+                nc.scalar.activation(slope_down[:, j, :], turned[:, j, :], ACT.Relu, scale=size_down[:, h * TURNS + j : h * TURNS + j + 1])
             back = bank([P, TURNS, P], "slope_back%d" % h, 3 + h)
             turn(back, lambda j: slope_down[:, j, :])
             nc.scalar.activation(slope[1][:, slots], back[:].rearrange("p j s -> p (j s)"), ACT.Copy)

@@ -16,6 +16,7 @@ E4M3X4 = mybir.dt.float8_e4m3fn_x4
 E5M2X4 = mybir.dt.float8_e5m2_x4
 ACT = mybir.ActivationFunctionType
 MULT = mybir.AluOpType.mult
+MAX = mybir.AluOpType.max
 
 P = 128
 PACK = 4
@@ -26,13 +27,6 @@ D_BLOCKS = D // P
 LINE = 4
 MX_ALIGN = 64
 TURNS = HALF // P
-PSUM_BANKS = 8
-LINE2 = 4
-BLOCK = 8
-MX2 = 64
-
-HELD = 192
-PITCH = 2 * N + QUARTER - HELD
 
 
 def tile_attend_gex_x_kernel(tc, dyT, hT, ts, wm, offs, out):
@@ -45,43 +39,20 @@ def tile_attend_gex_x_kernel(tc, dyT, hT, ts, wm, offs, out):
         ts_all = keep.tile([P, T], F32, name="ts_all")
         identity = keep.tile([P, P], F32, name="identity")
         twos = keep.tile([P, HALF], F32, name="twos")
-        h_all = [keep.tile([P, T], F32, name="h_all%d" % t, tag="h_all%d" % t) for t in range(PACK)]
-        dy_all = [keep.tile([P, T], F32, name="dy_all%d" % t, tag="dy_all%d" % t) for t in range(PACK)]
+        h_all = [keep.tile([P, T], F32, name="h_all%d" % t) for t in range(PACK)]
+        dy_all = [keep.tile([P, T], F32, name="dy_all%d" % t) for t in range(PACK)]
+        out_rows = [keep.tile([P, T], F32, name="out_rows%d" % b) for b in range(D_BLOCKS)]
         dx = [keep.tile([P, N], F32, name="dx%d" % b) for b in range(D_BLOCKS)]
-
         ts_twice = keep.tile([P, N], F32, name="ts_twice")
-        ts_size = keep.tile([P, N], F32, name="ts_size")
-        h_scaled = [keep.tile([P, N], F32, name="h_scaled%d" % t) for t in range(PACK)]
-        ts_sign = h_scaled[0]
-        slope = [keep.tile([P, N], F32, name="slope%d" % t) for t in range(PACK - 1)]
-
-        work = keep.tile([P, PACK * PITCH], F32, name="work", align_bytes=MX_ALIGN)
-        planes = work[:].rearrange("p (t c) -> p t c", t=PACK)
-        dz16_first_at = PITCH + N - HELD
-        slope3_second_at = dz16_first_at + N
-        slope3_first_at = slope3_second_at + HALF
-        late_pair_at = 3 * PITCH + HALF
-
-        def columns(first, count):
-            return work[:, first : first + count]
-
-        def as_bf16(cols):
-            return cols.bitcast(BF16).rearrange("p (c t) -> p c t", t=PACK)
-
-        late_pair = columns(late_pair_at, N).rearrange("p (t c) -> p t c", t=2)
-        dz16 = [as_bf16(columns(dz16_first_at, N)), as_bf16(columns(late_pair_at + HALF, N))]
-
-        wm_cols = [slice(0, P), slice(P, 3 * P), slice(3 * P, D)]
-        wm_raw = [
-            keep.tile([P, PACK, P], F32, name="wm_raw0")[:],
-            keep.tile([P, PACK, 2 * P], F32, name="wm_raw1")[:],
-            keep.tile([P, PACK, P], F32, name="wm_raw3")[:],
-        ]
-        wm16_first = keep.tile([P, QUARTER], F32, name="wm16_first", align_bytes=MX_ALIGN)
-        wm16 = [as_bf16(wm16_first[:]), as_bf16(columns(late_pair_at + HALF, HALF)), as_bf16(columns(HALF, QUARTER))]
-
+        ts_down = keep.tile([P, N // P], F32, name="ts_down")
+        h_listed = [keep.tile([P, N], F32, name="h_listed%d" % t) for t in range(PACK)]
+        slope = [keep.tile([P, N], F32, name="slope%d" % t) for t in range(PACK)]
+        dz = keep.tile([P, PACK, N], F32, name="dz")
+        dz16 = keep.tile([P, N * PACK], BF16, name="dz16", align_bytes=MX_ALIGN)
         dz_codes = keep.tile([P, N], U32, name="dz_codes", align_bytes=MX_ALIGN)
         dz_scales = keep.tile([P, N], U8, name="dz_scales", align_bytes=MX_ALIGN)
+        wm_raw = [keep.tile([P, PACK, P], F32, name="wm_raw%d" % b) for b in range(D_BLOCKS)]
+        wm16 = [keep.tile([P, P * PACK], BF16, name="wm16_%d" % b, align_bytes=MX_ALIGN) for b in range(D_BLOCKS)]
         wm_codes = keep.tile([P, D], U32, name="wm_codes", align_bytes=MX_ALIGN)
         wm_scales = keep.tile([P, D], U8, name="wm_scales", align_bytes=MX_ALIGN)
 
@@ -89,191 +60,152 @@ def tile_attend_gex_x_kernel(tc, dyT, hT, ts, wm, offs, out):
         dy_rows = dyT.rearrange("(p t) c -> p t c", t=PACK)
         wm_rows = wm.rearrange("b (p t) d -> p (b t) d", t=PACK)
 
-        def load_wm(g):
-            nc.sync.dma_start(wm_raw[g], wm_rows[:, :, wm_cols[g]])
-
         nc.sync.dma_start(ts_all[P - 1 :, :], ts[0:1, :])
         nc.sync.dma_start(offsets[:], offs)
         for tiles, rows, t in (
-            (h_all, h_rows, 1), (h_all, h_rows, 0), (h_all, h_rows, 2), (dy_all, dy_rows, 0),
+            (h_all, h_rows, 0), (h_all, h_rows, 1), (dy_all, dy_rows, 0), (h_all, h_rows, 2),
             (dy_all, dy_rows, 1), (h_all, h_rows, 3), (dy_all, dy_rows, 2), (dy_all, dy_rows, 3),
         ):
             nc.sync.dma_start(tiles[t][:], rows[:, t, :])
-        load_wm(0)
-        load_wm(1)
-        load_wm(2)
+        for b in range(D_BLOCKS):
+            nc.sync.dma_start(wm_raw[b][:], wm_rows[:, :, b * P : (b + 1) * P])
 
         nc.vector.memset(twos[:], 2.0)
         nc.vector.memset(ts_all[: P - 1, :].bitcast(I32), 0)
         make_identity(nc, identity[:])
-        out_rows = []
-
-        def zero_next_block():
-            b = len(out_rows)
-            out_rows.append(keep.tile([P, T], F32, name="out_rows%d" % b, tag=("h_all1", "h_all0", "h_all2", "dy_all0")[b]))
+        for b in range(D_BLOCKS):
             nc.gpsimd.memset(out_rows[b][:], 0.0)
 
         whole = slice(0, N)
         halves = [slice(0, HALF), slice(HALF, N)]
+        quarters = [slice(q * QUARTER, (q + 1) * QUARTER) for q in range(4)]
 
         def listed(slots):
             return offsets[:, slots.start // LIST_ROWS : slots.stop // LIST_ROWS]
 
-        def slope_at(t, slots):
-            if t < 3:
-                return slope[t][:, slots]
-            first = slope3_first_at if slots.stop <= HALF else slope3_second_at - HALF
-            return columns(first + slots.start, slots.stop - slots.start)
+        def bank(shape, name, k):
+            return psum.tile(shape, F32, name=name, tag="bank%d" % k)
 
-        def dz_at(t, slots):
-            if t >= 2 and slots.stop <= HALF:
-                return late_pair[:, t - 2, slots]
-            return planes[:, t, slots]
+        spread = [bank([P, TURNS, P], "spread%d" % h, 6 + h) for h in range(2)]
+        for h, slots in enumerate(halves):
+            nc.vector.tensor_tensor(ts_twice[:, slots], ts_all[:].indirect(listed(slots)), twos[:], MULT)
+            turned = bank([P, TURNS, P], "ts_turned%d" % h, h)
+            for j in range(TURNS):
+                nc.tensor.transpose(turned[:, j, :], ts_twice[:, slots.start + j * P : slots.start + (j + 1) * P], identity[:])
+            nc.scalar.activation(ts_down[:, h * TURNS : (h + 1) * TURNS], turned[:, :, P - 1], ACT.Copy)
+            for j in range(TURNS):
+                col = h * TURNS + j
+                nc.tensor.transpose(spread[h][:, j, :], ts_down[:, col : col + 1].to_broadcast([P, P]), identity[:])
 
         def gather_h(t, slots):
-            nc.vector.tensor_tensor(h_scaled[t][:, slots], h_all[t][:].indirect(listed(slots)), ts_size[:, slots], MULT)
+            nc.scalar.activation(h_listed[t][:, slots], h_all[t][:].indirect(listed(slots)), ACT.Copy)
 
-        def relu(t, slots):
-            nc.scalar.activation(slope_at(t, slots), h_scaled[t][:, slots], ACT.Relu)
+        def make_slope(t, h):
+            nc.vector.scalar_tensor_tensor(
+                slope[t][:, halves[h]], h_listed[t][:, halves[h]], 0.0,
+                spread[h][:].rearrange("p j s -> p (j s)"), MAX, MULT,
+            )
 
         def gather_dy(t, slots):
-            nc.vector.tensor_tensor(dz_at(t, slots), dy_all[t][:].indirect(listed(slots)), slope_at(t, slots), MULT)
+            nc.vector.tensor_tensor(dz[:, t, slots], dy_all[t][:].indirect(listed(slots)), slope[t][:, slots], MULT)
 
-        def round_and_interleave(dst, src):
+        def words(tile16, slots):
+            return tile16[:, PACK * slots.start : PACK * slots.stop]
+
+        def round_dz(slots):
+            nc.vector.tensor_copy(
+                words(dz16, slots).rearrange("p (c i t) -> p c t i", i=LINE, t=PACK),
+                dz[:, :, slots].rearrange("p t (c i) -> p c t i", i=LINE),
+            )
+
+        def round_wm(b):
             nc.scalar.activation(
-                dst.rearrange("p (c i) t -> p c t i", i=LINE),
-                src.rearrange("p t (c i) -> p c t i", i=LINE),
+                wm16[b][:].rearrange("p (c i t) -> p c t i", i=LINE, t=PACK),
+                wm_raw[b][:].rearrange("p t (c i) -> p c t i", i=LINE),
                 ACT.Copy,
             )
 
-        def round_wm(g):
-            round_and_interleave(wm16[g], wm_raw[g])
-
         def quantize_dz(slots):
-            h = slots.start // HALF
-            nc.vector.quantize_mx(
-                out=dz_codes[:, slots].bitcast(E5M2X4),
-                scales=dz_scales[:, slots],
-                in_=dz16[h][:, slots.start - h * HALF : slots.stop - h * HALF, :].rearrange("p c t -> p (c t)"),
-            )
+            nc.vector.quantize_mx(out=dz_codes[:, slots].bitcast(E5M2X4), scales=dz_scales[:, slots], in_=words(dz16, slots))
 
-        def quantize_wm(g):
-            nc.vector.quantize_mx(
-                out=wm_codes[:, wm_cols[g]].bitcast(E4M3X4),
-                scales=wm_scales[:, wm_cols[g]],
-                in_=wm16[g].rearrange("p c t -> p (c t)"),
-            )
-
-        def multiply(b, h):
+        def quantize_wm(b):
             cols = slice(b * P, (b + 1) * P)
-            acc = psum.tile([P, HALF], F32, name="bank%d_%d" % (b, h), tag="bank%d" % ((2 * b + h) % 7))
+            nc.vector.quantize_mx(out=wm_codes[:, cols].bitcast(E4M3X4), scales=wm_scales[:, cols], in_=wm16[b][:])
+
+        def multiply(b, slots, k):
+            cols = slice(b * P, (b + 1) * P)
+            acc = bank([P, slots.stop - slots.start], "acc%d_%d" % (b, slots.start), k)
             nc.tensor.matmul_mx(
                 out=acc[:],
                 lhsT=wm_codes[:, cols].bitcast(E4M3X4),
                 lhsT_scale=wm_scales[:, cols],
-                rhs=dz_codes[:, halves[h]].bitcast(E5M2X4),
-                rhs_scale=dz_scales[:, halves[h]],
+                rhs=dz_codes[:, slots].bitcast(E5M2X4),
+                rhs_scale=dz_scales[:, slots],
                 start=True,
                 stop=True,
             )
-            return acc
+            nc.scalar.activation(dx[b][:, slots], acc[:], ACT.Copy)
 
-        def copy_out(b, h, acc):
-            nc.scalar.activation(dx[b][:, halves[h]], acc[:], ACT.Copy)
+        def scatter_s(b, slots):
+            nc.scalar.activation(out_rows[b][:].indirect(listed(slots)), dx[b][:, slots], ACT.Copy)
 
-        def scatter(b, slots):
-            nc.vector.tensor_tensor(out_rows[b][:].indirect(listed(slots)), dx[b][:, slots], ts_sign[:, slots], MULT)
+        def scatter_v(b, slots):
+            nc.vector.tensor_copy(out_rows[b][:].indirect(listed(slots)), dx[b][:, slots])
 
         def store(b):
             nc.sync.dma_start(out[b * P : (b + 1) * P, :], out_rows[b][:])
 
-        def bank(shape, name, k):
-            return psum.tile(shape, F32, name=name, tag="bank%d" % k)
+        def prepare(t):
+            for h in range(2):
+                gather_h(t, halves[h])
+                make_slope(t, h)
 
-        def turn(dst, src):
-            for j in range(TURNS):
-                nc.tensor.transpose(dst[:, j, :], src(j), identity[:])
-
-        spread = [bank([P, TURNS, P], "spread%d" % h, 5 + h) for h in range(2)]
-        ts_down = keep.tile([P, N // P], F32, name="ts_down")
-        size_down = keep.tile([P, N // P], F32, name="size_down")
-        for k, first, count in ((0, 0, 2), (3, 2, 2), (0, 4, 4)):
-            slots = slice(first * P, (first + count) * P)
-            nc.vector.tensor_tensor(ts_twice[:, slots], ts_all[:].indirect(listed(slots)), twos[:, : count * P], MULT)
-            turned = bank([P, count, P], "ts_turned%d" % first, k)
-            for j in range(count):
-                nc.tensor.transpose(turned[:, j, :], ts_twice[:, (first + j) * P : (first + j + 1) * P], identity[:])
-            nc.scalar.activation(ts_down[:, first : first + count], turned[:, :, P - 1], ACT.Copy)
-            for j in range(first, first + count):
-                nc.tensor.transpose(spread[j // TURNS][:, j % TURNS, :], ts_down[:, j : j + 1].to_broadcast([P, P]), identity[:])
-            if first:
-                h = first // TURNS
-                nc.scalar.activation(ts_size[:, halves[h]], spread[h][:].rearrange("p j s -> p (j s)"), ACT.Abs)
-        nc.scalar.activation(size_down[:], ts_down[:], ACT.Abs)
-        nc.vector.tensor_copy(h_scaled[1][:], h_all[1][:].indirect(listed(whole)))
-        for slots in halves:
-            gather_h(0, slots)
-        h_turned = bank([P, 2, TURNS, P], "h_turned", 0)
-        for h, slots in enumerate(halves):
-            turned = h_turned[:, h]
-            turn(turned, lambda j: h_scaled[1][:, slots.start + j * P : slots.start + (j + 1) * P])
-            slope_down = keep.tile([P, TURNS, P], F32, name="slope_down%d" % h)
-            for j in range(TURNS):
-                nc.scalar.activation(slope_down[:, j, :], turned[:, j, :], ACT.Relu, scale=size_down[:, h * TURNS + j : h * TURNS + j + 1])
-            back = bank([P, TURNS, P], "slope_back%d" % h, 3 + h)
-            turn(back, lambda j: slope_down[:, j, :])
-            nc.scalar.activation(slope[1][:, slots], back[:].rearrange("p j s -> p (j s)"), ACT.Copy)
-        relu(0, whole)
-        gather_h(2, whole)
-        relu(2, whole)
-        for h, slots in enumerate(halves):
-            nc.scalar.activation(ts_sign[:, slots], spread[h][:].rearrange("p j s -> p (j s)"), ACT.Sign)
+        prepare(0)
+        prepare(1)
         gather_dy(0, whole)
-        for b in range(D_BLOCKS):
-            zero_next_block()
-        gather_dy(1, slice(0, N - HELD))
-        round_and_interleave(dz16[0][:, :, 0:2], planes[:, 0:2, halves[0]])
-        gather_h(3, whole)
-        for slots in halves:
-            relu(3, slots)
-        gather_dy(2, halves[0])
+        prepare(2)
+        gather_dy(1, whole)
+        prepare(3)
+        gather_dy(2, whole)
 
-        for slots in (slice(QUARTER, QUARTER + P), slice(QUARTER + P, HALF), slice(0, QUARTER)):
-            gather_dy(3, slots)
-            if slots.start == 0:
-                round_wm(0)
-            round_and_interleave(dz16[0][:, slots, 2:4], late_pair[:, :, slots])
-        gather_dy(2, halves[1])
-        quantize_dz(slice(QUARTER, HALF))
+        gather_dy(3, quarters[0])
+        gather_dy(3, quarters[1])
+        round_wm(0)
+        round_dz(quarters[0])
         quantize_wm(0)
-        quantize_dz(slice(0, QUARTER))
-        acc00 = multiply(0, 0)
+        quantize_dz(quarters[0])
         round_wm(1)
-        copy_out(0, 0, acc00)
-        gather_dy(3, halves[1])
-        gather_dy(1, slice(N - HELD, N))
         quantize_wm(1)
-        acc10 = multiply(1, 0)
-        acc20 = multiply(2, 0)
-
-        scatter(0, halves[0])
-        round_and_interleave(dz16[1], planes[:, :, halves[1]])
-        copy_out(1, 0, acc10)
-        quantize_dz(halves[1])
-        scatter(1, halves[0])
+        multiply(0, quarters[0], 0)
+        multiply(1, quarters[0], 1)
+        round_dz(quarters[1])
+        gather_dy(3, halves[1])
+        quantize_dz(quarters[1])
+        scatter_s(0, quarters[0])
         round_wm(2)
+        round_wm(3)
         quantize_wm(2)
-        copy_out(0, 1, multiply(0, 1))
-        scatter(0, halves[1])
+        round_dz(halves[1])
+        quantize_wm(3)
+        quantize_dz(halves[1])
+        multiply(2, halves[0], 2)
+        multiply(0, quarters[1], 3)
+        scatter_s(1, quarters[0])
+        scatter_v(2, halves[0])
+        multiply(3, halves[0], 4)
+        multiply(0, halves[1], 5)
+        scatter_s(0, slice(256, 640))
+        scatter_v(3, halves[0])
+        multiply(2, halves[1], 6)
+        scatter_s(0, slice(640, N))
         store(0)
-        copy_out(2, 0, acc20)
-        copy_out(2, 1, multiply(2, 1))
-        scatter(2, whole)
+        scatter_v(2, halves[1])
         store(2)
-        copy_out(1, 1, multiply(1, 1))
-        scatter(1, halves[1])
-        store(1)
-        for h in range(2):
-            copy_out(3, h, multiply(3, h))
-        scatter(3, whole)
+        multiply(1, quarters[1], 7)
+        multiply(1, halves[1], 0)
+        multiply(3, halves[1], 1)
+        scatter_s(1, slice(256, 640))
+        scatter_v(3, halves[1])
         store(3)
+        scatter_s(1, slice(640, N))
+        store(1)

@@ -36,23 +36,24 @@ def tile_attend_gex_x_kernel(tc, dyT, hT, ts, wm, offs, out):
         psum = ctx.enter_context(tc.psum_pool(name="psum", bufs=1))
 
         offsets = keep.tile([P, N // LIST_ROWS], U16, name="offsets")
-        ts_all = keep.tile([P, T], F32, name="ts_all")
+        ts_all = keep.tile([P, T], F32, name="ts_all", tag="ts_all")
         identity = keep.tile([P, P], F32, name="identity")
-        twos = keep.tile([P, HALF], F32, name="twos")
-        h_all = [keep.tile([P, T], F32, name="h_all%d" % t) for t in range(PACK)]
-        dy_all = [keep.tile([P, T], F32, name="dy_all%d" % t) for t in range(PACK)]
-        out_rows = [keep.tile([P, T], F32, name="out_rows%d" % b) for b in range(D_BLOCKS)]
+        h_all = [keep.tile([P, T], F32, name="h_all%d" % t, tag="h_all%d" % t) for t in range(PACK)]
+        dy_all = [keep.tile([P, T], F32, name="dy_all%d" % t, tag="dy_all%d" % t) for t in range(PACK)]
         dx = [keep.tile([P, N], F32, name="dx%d" % b) for b in range(D_BLOCKS)]
-        ts_twice = keep.tile([P, N], F32, name="ts_twice")
+        ts_listed = keep.tile([P, N], F32, name="ts_listed")
+        dy_listed = [keep.tile([P, HALF], F32, name="dy_listed%d" % t) for t in range(2)]
         ts_down = keep.tile([P, N // P], F32, name="ts_down")
         h_listed = [keep.tile([P, N], F32, name="h_listed%d" % t) for t in range(PACK)]
         slope = [keep.tile([P, N], F32, name="slope%d" % t) for t in range(PACK)]
-        dz = keep.tile([P, PACK, N], F32, name="dz")
-        dz16 = keep.tile([P, N * PACK], BF16, name="dz16", align_bytes=MX_ALIGN)
+        dz = keep.tile([P, PACK, N], F32, name="dz", align_bytes=MX_ALIGN)
+        dz16_first = keep.tile([P, QUARTER * PACK], BF16, name="dz16_first", align_bytes=MX_ALIGN)
+        dz16_second = keep.tile([P, HALF * PACK], BF16, name="dz16_second", align_bytes=MX_ALIGN)
         dz_codes = keep.tile([P, N], U32, name="dz_codes", align_bytes=MX_ALIGN)
         dz_scales = keep.tile([P, N], U8, name="dz_scales", align_bytes=MX_ALIGN)
         wm_raw = [keep.tile([P, PACK, P], F32, name="wm_raw%d" % b) for b in range(D_BLOCKS)]
-        wm16 = [keep.tile([P, P * PACK], BF16, name="wm16_%d" % b, align_bytes=MX_ALIGN) for b in range(D_BLOCKS)]
+        wm16 = [dz[:, PACK - 1, HALF + b * QUARTER : HALF + (b + 1) * QUARTER].bitcast(BF16) for b in range(2)]
+        wm16 += [keep.tile([P, P * PACK], BF16, name="wm16_%d" % b, align_bytes=MX_ALIGN)[:] for b in range(2, D_BLOCKS)]
         wm_codes = keep.tile([P, D], U32, name="wm_codes", align_bytes=MX_ALIGN)
         wm_scales = keep.tile([P, D], U8, name="wm_scales", align_bytes=MX_ALIGN)
 
@@ -63,18 +64,15 @@ def tile_attend_gex_x_kernel(tc, dyT, hT, ts, wm, offs, out):
         nc.sync.dma_start(ts_all[P - 1 :, :], ts[0:1, :])
         nc.sync.dma_start(offsets[:], offs)
         for tiles, rows, t in (
-            (h_all, h_rows, 0), (h_all, h_rows, 1), (dy_all, dy_rows, 0), (h_all, h_rows, 2),
-            (dy_all, dy_rows, 1), (h_all, h_rows, 3), (dy_all, dy_rows, 2), (dy_all, dy_rows, 3),
+            (h_all, h_rows, 0), (dy_all, dy_rows, 0), (h_all, h_rows, 1), (h_all, h_rows, 2),
+            (h_all, h_rows, 3), (dy_all, dy_rows, 1), (dy_all, dy_rows, 2), (dy_all, dy_rows, 3),
         ):
             nc.sync.dma_start(tiles[t][:], rows[:, t, :])
         for b in range(D_BLOCKS):
             nc.sync.dma_start(wm_raw[b][:], wm_rows[:, :, b * P : (b + 1) * P])
 
-        nc.vector.memset(twos[:], 2.0)
         nc.vector.memset(ts_all[: P - 1, :].bitcast(I32), 0)
         make_identity(nc, identity[:])
-        for b in range(D_BLOCKS):
-            nc.gpsimd.memset(out_rows[b][:], 0.0)
 
         whole = slice(0, N)
         halves = [slice(0, HALF), slice(HALF, N)]
@@ -88,11 +86,11 @@ def tile_attend_gex_x_kernel(tc, dyT, hT, ts, wm, offs, out):
 
         spread = [bank([P, TURNS, P], "spread%d" % h, 6 + h) for h in range(2)]
         for h, slots in enumerate(halves):
-            nc.vector.tensor_tensor(ts_twice[:, slots], ts_all[:].indirect(listed(slots)), twos[:], MULT)
+            nc.vector.tensor_copy(ts_listed[:, slots], ts_all[:].indirect(listed(slots)))
             turned = bank([P, TURNS, P], "ts_turned%d" % h, h)
             for j in range(TURNS):
-                nc.tensor.transpose(turned[:, j, :], ts_twice[:, slots.start + j * P : slots.start + (j + 1) * P], identity[:])
-            nc.scalar.activation(ts_down[:, h * TURNS : (h + 1) * TURNS], turned[:, :, P - 1], ACT.Copy)
+                nc.tensor.transpose(turned[:, j, :], ts_listed[:, slots.start + j * P : slots.start + (j + 1) * P], identity[:])
+            nc.vector.tensor_scalar_mul(ts_down[:, h * TURNS : (h + 1) * TURNS], turned[:, :, P - 1], 2.0)
             for j in range(TURNS):
                 col = h * TURNS + j
                 nc.tensor.transpose(spread[h][:, j, :], ts_down[:, col : col + 1].to_broadcast([P, P]), identity[:])
@@ -109,28 +107,28 @@ def tile_attend_gex_x_kernel(tc, dyT, hT, ts, wm, offs, out):
         def gather_dy(t, slots):
             nc.vector.tensor_tensor(dz[:, t, slots], dy_all[t][:].indirect(listed(slots)), slope[t][:, slots], MULT)
 
-        def words(tile16, slots):
-            return tile16[:, PACK * slots.start : PACK * slots.stop]
+        def dz16(slots):
+            return dz16_first[:] if slots.stop <= HALF else dz16_second[:]
 
         def round_dz(slots):
             nc.vector.tensor_copy(
-                words(dz16, slots).rearrange("p (c i t) -> p c t i", i=LINE, t=PACK),
+                dz16(slots).rearrange("p (c i t) -> p c t i", i=LINE, t=PACK),
                 dz[:, :, slots].rearrange("p t (c i) -> p c t i", i=LINE),
             )
 
         def round_wm(b):
             nc.scalar.activation(
-                wm16[b][:].rearrange("p (c i t) -> p c t i", i=LINE, t=PACK),
+                wm16[b].rearrange("p (c i t) -> p c t i", i=LINE, t=PACK),
                 wm_raw[b][:].rearrange("p t (c i) -> p c t i", i=LINE),
                 ACT.Copy,
             )
 
         def quantize_dz(slots):
-            nc.vector.quantize_mx(out=dz_codes[:, slots].bitcast(E5M2X4), scales=dz_scales[:, slots], in_=words(dz16, slots))
+            nc.vector.quantize_mx(out=dz_codes[:, slots].bitcast(E5M2X4), scales=dz_scales[:, slots], in_=dz16(slots))
 
         def quantize_wm(b):
             cols = slice(b * P, (b + 1) * P)
-            nc.vector.quantize_mx(out=wm_codes[:, cols].bitcast(E4M3X4), scales=wm_scales[:, cols], in_=wm16[b][:])
+            nc.vector.quantize_mx(out=wm_codes[:, cols].bitcast(E4M3X4), scales=wm_scales[:, cols], in_=wm16[b])
 
         def multiply(b, slots, k):
             cols = slice(b * P, (b + 1) * P)
@@ -144,13 +142,24 @@ def tile_attend_gex_x_kernel(tc, dyT, hT, ts, wm, offs, out):
                 start=True,
                 stop=True,
             )
-            nc.scalar.activation(dx[b][:, slots], acc[:], ACT.Copy)
+            return acc
+
+        def sums_at(b, slots):
+            if b == 2 and slots.stop <= HALF:
+                return dz[:, 0, HALF + slots.start : HALF + slots.stop]
+            return dx[b][:, slots]
+
+        def product_s(b, slots, k):
+            nc.scalar.activation(sums_at(b, slots), multiply(b, slots, k)[:], ACT.Copy)
+
+        def product_v(b, slots, k):
+            nc.vector.tensor_copy(sums_at(b, slots), multiply(b, slots, k)[:])
 
         def scatter_s(b, slots):
-            nc.scalar.activation(out_rows[b][:].indirect(listed(slots)), dx[b][:, slots], ACT.Copy)
+            nc.scalar.activation(out_rows[b][:].indirect(listed(slots)), sums_at(b, slots), ACT.Copy)
 
         def scatter_v(b, slots):
-            nc.vector.tensor_copy(out_rows[b][:].indirect(listed(slots)), dx[b][:, slots])
+            nc.vector.tensor_copy(out_rows[b][:].indirect(listed(slots)), sums_at(b, slots))
 
         def store(b):
             nc.sync.dma_start(out[b * P : (b + 1) * P, :], out_rows[b][:])
@@ -160,52 +169,62 @@ def tile_attend_gex_x_kernel(tc, dyT, hT, ts, wm, offs, out):
                 gather_h(t, halves[h])
                 make_slope(t, h)
 
+        def gather_dy_shared(t):
+            picked = dy_listed[t - 1]
+            nc.scalar.activation(picked[:], dy_all[t][:].indirect(listed(halves[1])), ACT.Copy)
+            gather_dy(t, halves[0])
+            nc.vector.tensor_tensor(dz[:, t, halves[1]], picked[:], slope[t][:, halves[1]], MULT)
+
         prepare(0)
-        prepare(1)
         gather_dy(0, whole)
+        prepare(1)
+        out_rows = []
+        for b, tag in enumerate(("ts_all", "h_all0", "h_all1", "dy_all0")):
+            out_rows.append(keep.tile([P, T], F32, name="out_rows%d" % b, tag=tag))
+            nc.gpsimd.memset(out_rows[b][:], 0.0)
         prepare(2)
-        gather_dy(1, whole)
         prepare(3)
-        gather_dy(2, whole)
+        gather_dy_shared(1)
+        gather_dy_shared(2)
 
         gather_dy(3, quarters[0])
         gather_dy(3, quarters[1])
         round_wm(0)
+        round_wm(1)
         round_dz(quarters[0])
         quantize_wm(0)
         quantize_dz(quarters[0])
-        round_wm(1)
         quantize_wm(1)
-        multiply(0, quarters[0], 0)
-        multiply(1, quarters[0], 1)
+        round_wm(2)
+        round_wm(3)
+        product_s(0, quarters[0], 0)
+        product_s(1, quarters[0], 1)
         round_dz(quarters[1])
         gather_dy(3, halves[1])
         quantize_dz(quarters[1])
-        scatter_s(0, quarters[0])
-        round_wm(2)
-        round_wm(3)
         quantize_wm(2)
-        round_dz(halves[1])
-        quantize_wm(3)
-        quantize_dz(halves[1])
-        multiply(2, halves[0], 2)
-        multiply(0, quarters[1], 3)
+        scatter_s(0, quarters[0])
+        product_s(0, quarters[1], 2)
+        product_s(1, quarters[1], 3)
         scatter_s(1, quarters[0])
+        round_dz(halves[1])
+        product_v(2, halves[0], 4)
+        quantize_dz(halves[1])
+        quantize_wm(3)
         scatter_v(2, halves[0])
-        multiply(3, halves[0], 4)
-        multiply(0, halves[1], 5)
-        scatter_s(0, slice(256, 640))
-        scatter_v(3, halves[0])
-        multiply(2, halves[1], 6)
-        scatter_s(0, slice(640, N))
-        store(0)
+        scatter_s(0, quarters[1])
+        product_s(0, halves[1], 5)
+        product_s(1, halves[1], 6)
+        product_v(2, halves[1], 7)
+        product_v(3, halves[1], 0)
+        product_s(3, halves[0], 1)
+        scatter_s(0, quarters[2])
         scatter_v(2, halves[1])
         store(2)
-        multiply(1, quarters[1], 7)
-        multiply(1, halves[1], 0)
-        multiply(3, halves[1], 1)
         scatter_s(1, slice(256, 640))
-        scatter_v(3, halves[1])
-        store(3)
+        scatter_s(0, quarters[3])
+        store(0)
         scatter_s(1, slice(640, N))
         store(1)
+        scatter_v(3, whole)
+        store(3)

@@ -42,7 +42,7 @@ def tile_attend_gex_x_kernel(tc, dyT, hT, ts, wm, offs, out):
         dy_all = [keep.tile([P, T], F32, name="dy_all%d" % t, tag="dy_all%d" % t) for t in range(PACK)]
         dx = [keep.tile([P, N], F32, name="dx%d" % b) for b in range(D_BLOCKS)]
         ts_listed = keep.tile([P, N], F32, name="ts_listed")
-        dy_listed = [keep.tile([P, HALF], F32, name="dy_listed%d" % t) for t in range(2)]
+        dy_listed = [keep.tile([P, HALF], F32, name="dy_listed%d" % t) for t in range(3)]
         ts_down = keep.tile([P, N // P], F32, name="ts_down")
         h_listed = [keep.tile([P, N], F32, name="h_listed%d" % t) for t in range(PACK)]
         slope = [keep.tile([P, N], F32, name="slope%d" % t) for t in range(PACK)]
@@ -53,7 +53,8 @@ def tile_attend_gex_x_kernel(tc, dyT, hT, ts, wm, offs, out):
         dz_scales = keep.tile([P, N], U8, name="dz_scales", align_bytes=MX_ALIGN)
         wm_raw = [keep.tile([P, PACK, P], F32, name="wm_raw%d" % b) for b in range(D_BLOCKS)]
         wm16 = [dz[:, PACK - 1, HALF + b * QUARTER : HALF + (b + 1) * QUARTER].bitcast(BF16) for b in range(2)]
-        wm16 += [keep.tile([P, P * PACK], BF16, name="wm16_%d" % b, align_bytes=MX_ALIGN)[:] for b in range(2, D_BLOCKS)]
+        wm16.append(keep.tile([P, P * PACK], BF16, name="wm16_2", align_bytes=MX_ALIGN)[:])
+        wm16.append(dz16_first[:, : P * PACK])
         wm_codes = keep.tile([P, D], U32, name="wm_codes", align_bytes=MX_ALIGN)
         wm_scales = keep.tile([P, D], U8, name="wm_scales", align_bytes=MX_ALIGN)
 
@@ -61,10 +62,11 @@ def tile_attend_gex_x_kernel(tc, dyT, hT, ts, wm, offs, out):
         dy_rows = dyT.rearrange("(p t) c -> p t c", t=PACK)
         wm_rows = wm.rearrange("b (p t) d -> p (b t) d", t=PACK)
 
-        nc.sync.dma_start(ts_all[P - 1 :, :], ts[0:1, :])
+        nc.sync.dma_start(h_all[0][:], h_rows[:, 0, :])
         nc.sync.dma_start(offsets[:], offs)
+        nc.sync.dma_start(ts_all[P - 1 :, :], ts[0:1, :])
         for tiles, rows, t in (
-            (h_all, h_rows, 0), (dy_all, dy_rows, 0), (h_all, h_rows, 1), (h_all, h_rows, 2),
+            (dy_all, dy_rows, 0), (h_all, h_rows, 1), (h_all, h_rows, 2),
             (h_all, h_rows, 3), (dy_all, dy_rows, 1), (dy_all, dy_rows, 2), (dy_all, dy_rows, 3),
         ):
             nc.sync.dma_start(tiles[t][:], rows[:, t, :])
@@ -117,11 +119,12 @@ def tile_attend_gex_x_kernel(tc, dyT, hT, ts, wm, offs, out):
             )
 
         def round_wm(b):
-            nc.scalar.activation(
-                wm16[b].rearrange("p (c i t) -> p c t i", i=LINE, t=PACK),
-                wm_raw[b][:].rearrange("p t (c i) -> p c t i", i=LINE),
-                ACT.Copy,
-            )
+            dst = wm16[b].rearrange("p (c i t) -> p c t i", i=LINE, t=PACK)
+            src = wm_raw[b][:].rearrange("p t (c i) -> p c t i", i=LINE)
+            if b == D_BLOCKS - 1:
+                nc.vector.tensor_copy(dst, src)
+            else:
+                nc.scalar.activation(dst, src, ACT.Copy)
 
         def quantize_dz(slots):
             nc.vector.quantize_mx(out=dz_codes[:, slots].bitcast(E5M2X4), scales=dz_scales[:, slots], in_=dz16(slots))
@@ -169,11 +172,11 @@ def tile_attend_gex_x_kernel(tc, dyT, hT, ts, wm, offs, out):
                 gather_h(t, halves[h])
                 make_slope(t, h)
 
-        def gather_dy_shared(t):
-            picked = dy_listed[t - 1]
-            nc.scalar.activation(picked[:], dy_all[t][:].indirect(listed(halves[1])), ACT.Copy)
-            gather_dy(t, halves[0])
-            nc.vector.tensor_tensor(dz[:, t, halves[1]], picked[:], slope[t][:, halves[1]], MULT)
+        def pick_dy(t):
+            nc.scalar.activation(dy_listed[t - 1][:], dy_all[t][:].indirect(listed(halves[1])), ACT.Copy)
+
+        def multiply_picked(t):
+            nc.vector.tensor_tensor(dz[:, t, halves[1]], dy_listed[t - 1][:], slope[t][:, halves[1]], MULT)
 
         prepare(0)
         gather_dy(0, whole)
@@ -184,8 +187,11 @@ def tile_attend_gex_x_kernel(tc, dyT, hT, ts, wm, offs, out):
             nc.gpsimd.memset(out_rows[b][:], 0.0)
         prepare(2)
         prepare(3)
-        gather_dy_shared(1)
-        gather_dy_shared(2)
+        for t in (1, 2):
+            pick_dy(t)
+            gather_dy(t, halves[0])
+            multiply_picked(t)
+        pick_dy(3)
 
         gather_dy(3, quarters[0])
         gather_dy(3, quarters[1])
@@ -196,11 +202,10 @@ def tile_attend_gex_x_kernel(tc, dyT, hT, ts, wm, offs, out):
         quantize_dz(quarters[0])
         quantize_wm(1)
         round_wm(2)
-        round_wm(3)
         product_s(0, quarters[0], 0)
         product_s(1, quarters[0], 1)
         round_dz(quarters[1])
-        gather_dy(3, halves[1])
+        multiply_picked(3)
         quantize_dz(quarters[1])
         quantize_wm(2)
         scatter_s(0, quarters[0])
@@ -208,6 +213,7 @@ def tile_attend_gex_x_kernel(tc, dyT, hT, ts, wm, offs, out):
         product_s(1, quarters[1], 3)
         scatter_s(1, quarters[0])
         round_dz(halves[1])
+        round_wm(3)
         product_v(2, halves[0], 4)
         quantize_dz(halves[1])
         quantize_wm(3)

@@ -223,7 +223,8 @@ def tile_attend_gex_x_kernel(tc, dyT, hT, ts, wm, offs, out):
         product_s(1, halves[1], 6)
         product_v(2, halves[1], 7)
         product_v(3, halves[1], 0)
-        product_s(3, halves[0], 1)
+        product_v(3, quarters[1], 2)
+        product_s(3, quarters[0], 1)
         scatter_s(0, quarters[2])
         scatter_v(2, halves[1])
         store(2)

@@ -45,7 +45,8 @@ def tile_attend_gex_x_kernel(tc, dyT, hT, ts, wm, offs, out):
         dy_listed = [keep.tile([P, HALF], F32, name="dy_listed%d" % t) for t in range(3)]
         ts_down = keep.tile([P, N // P], F32, name="ts_down")
         h_listed = [keep.tile([P, N], F32, name="h_listed%d" % t) for t in range(PACK)]
-        slope = [keep.tile([P, N], F32, name="slope%d" % t) for t in range(PACK)]
+        slope = [[keep.tile([P, HALF], F32, name="slope%d_%d" % (t, h)) for h in range(2)] for t in range(PACK - 1)]
+        slope.append([keep.tile([P, HALF], F32, name="slope3_0"), slope[1][0]])
         dz = keep.tile([P, PACK, N], F32, name="dz", align_bytes=MX_ALIGN)
         dz16_first = keep.tile([P, QUARTER * PACK], BF16, name="dz16_first", align_bytes=MX_ALIGN)
         dz16_second = keep.tile([P, HALF * PACK], BF16, name="dz16_second", align_bytes=MX_ALIGN)
@@ -102,12 +103,14 @@ def tile_attend_gex_x_kernel(tc, dyT, hT, ts, wm, offs, out):
 
         def make_slope(t, h):
             nc.vector.scalar_tensor_tensor(
-                slope[t][:, halves[h]], h_listed[t][:, halves[h]], 0.0,
+                slope[t][h][:], h_listed[t][:, halves[h]], 0.0,
                 spread[h][:].rearrange("p j s -> p (j s)"), MAX, MULT,
             )
 
         def gather_dy(t, slots):
-            nc.vector.tensor_tensor(dz[:, t, slots], dy_all[t][:].indirect(listed(slots)), slope[t][:, slots], MULT)
+            h = slots.start // HALF
+            part = slope[t][h][:, slots.start - h * HALF : slots.stop - h * HALF]
+            nc.vector.tensor_tensor(dz[:, t, slots], dy_all[t][:].indirect(listed(slots)), part, MULT)
 
         def dz16(slots):
             return dz16_first[:] if slots.stop <= HALF else dz16_second[:]
@@ -176,21 +179,27 @@ def tile_attend_gex_x_kernel(tc, dyT, hT, ts, wm, offs, out):
             nc.scalar.activation(dy_listed[t - 1][:], dy_all[t][:].indirect(listed(halves[1])), ACT.Copy)
 
         def multiply_picked(t):
-            nc.vector.tensor_tensor(dz[:, t, halves[1]], dy_listed[t - 1][:], slope[t][:, halves[1]], MULT)
+            nc.vector.tensor_tensor(dz[:, t, halves[1]], dy_listed[t - 1][:], slope[t][1][:], MULT)
 
-        prepare(0)
-        gather_dy(0, whole)
+        for h in range(2):
+            gather_h(0, halves[h])
+            make_slope(0, h)
+            gather_dy(0, halves[h])
         prepare(1)
         out_rows = []
         for b, tag in enumerate(("ts_all", "h_all0", "h_all1", "dy_all0")):
             out_rows.append(keep.tile([P, T], F32, name="out_rows%d" % b, tag=tag))
             nc.gpsimd.memset(out_rows[b][:], 0.0)
         prepare(2)
-        prepare(3)
+        gather_h(3, halves[0])
+        make_slope(3, 0)
+        gather_h(3, halves[1])
         for t in (1, 2):
             pick_dy(t)
             gather_dy(t, halves[0])
             multiply_picked(t)
+            if t == 1:
+                make_slope(3, 1)
         pick_dy(3)
 
         gather_dy(3, quarters[0])

@@ -37,16 +37,15 @@ def tile_attend_gex_x_kernel(tc, dyT, hT, ts, wm, offs, out):
 
         offsets = keep.tile([P, N // LIST_ROWS], U16, name="offsets")
         ts_all = keep.tile([P, T], F32, name="ts_all", tag="ts_all")
-        identity = keep.tile([P, P], F32, name="identity")
+        identity = keep.tile([P, P], F32, name="identity", tag="identity")
         h_all = [keep.tile([P, T], F32, name="h_all%d" % t, tag="h_all%d" % t) for t in range(PACK)]
         dy_all = [keep.tile([P, T], F32, name="dy_all%d" % t, tag="dy_all%d" % t) for t in range(PACK)]
         dx = [keep.tile([P, N], F32, name="dx%d" % b) for b in range(D_BLOCKS)]
-        ts_listed = keep.tile([P, N], F32, name="ts_listed")
-        dy_listed = [keep.tile([P, HALF], F32, name="dy_listed%d" % t) for t in range(3)]
+        ts_listed = keep.tile([P, N], F32, name="ts_listed", tag="ts_listed")
+        dy_listed = [keep.tile([P, HALF], F32, name="dy_listed%d" % t) for t in range(PACK)]
         ts_down = keep.tile([P, N // P], F32, name="ts_down")
         h_listed = [keep.tile([P, N], F32, name="h_listed%d" % t) for t in range(PACK)]
-        slope = [[keep.tile([P, HALF], F32, name="slope%d_%d" % (t, h)) for h in range(2)] for t in range(PACK - 1)]
-        slope.append([keep.tile([P, HALF], F32, name="slope3_0"), slope[1][0]])
+        slope = [[keep.tile([P, HALF], F32, name="slope%d_%d" % (t, h)) for h in range(2)] for t in range(PACK)]
         dz = keep.tile([P, PACK, N], F32, name="dz", align_bytes=MX_ALIGN)
         dz16_first = keep.tile([P, QUARTER * PACK], BF16, name="dz16_first", align_bytes=MX_ALIGN)
         dz16_second = keep.tile([P, HALF * PACK], BF16, name="dz16_second", align_bytes=MX_ALIGN)
@@ -63,12 +62,12 @@ def tile_attend_gex_x_kernel(tc, dyT, hT, ts, wm, offs, out):
         dy_rows = dyT.rearrange("(p t) c -> p t c", t=PACK)
         wm_rows = wm.rearrange("b (p t) d -> p (b t) d", t=PACK)
 
-        nc.sync.dma_start(h_all[0][:], h_rows[:, 0, :])
-        nc.sync.dma_start(offsets[:], offs)
         nc.sync.dma_start(ts_all[P - 1 :, :], ts[0:1, :])
+        nc.sync.dma_start(offsets[:], offs)
+        nc.sync.dma_start(h_all[0][:], h_rows[:, 0, :])
         for tiles, rows, t in (
-            (dy_all, dy_rows, 0), (h_all, h_rows, 1), (h_all, h_rows, 2),
-            (h_all, h_rows, 3), (dy_all, dy_rows, 1), (dy_all, dy_rows, 2), (dy_all, dy_rows, 3),
+            (h_all, h_rows, 1), (h_all, h_rows, 2), (h_all, h_rows, 3),
+            (dy_all, dy_rows, 0), (dy_all, dy_rows, 1), (dy_all, dy_rows, 2), (dy_all, dy_rows, 3),
         ):
             nc.sync.dma_start(tiles[t][:], rows[:, t, :])
         for b in range(D_BLOCKS):
@@ -171,35 +170,29 @@ def tile_attend_gex_x_kernel(tc, dyT, hT, ts, wm, offs, out):
             nc.sync.dma_start(out[b * P : (b + 1) * P, :], out_rows[b][:])
 
         def prepare(t):
+            gather_h(t, halves[0])
+            nc.vector.tensor_copy(h_listed[t][:, quarters[3]], h_all[t][:].indirect(listed(quarters[3])))
+            gather_h(t, quarters[2])
             for h in range(2):
-                gather_h(t, halves[h])
                 make_slope(t, h)
 
         def pick_dy(t):
-            nc.scalar.activation(dy_listed[t - 1][:], dy_all[t][:].indirect(listed(halves[1])), ACT.Copy)
+            nc.scalar.activation(dy_listed[t][:], dy_all[t][:].indirect(listed(halves[1])), ACT.Copy)
 
         def multiply_picked(t):
-            nc.vector.tensor_tensor(dz[:, t, halves[1]], dy_listed[t - 1][:], slope[t][1][:], MULT)
+            nc.vector.tensor_tensor(dz[:, t, halves[1]], dy_listed[t][:], slope[t][1][:], MULT)
 
-        for h in range(2):
-            gather_h(0, halves[h])
-            make_slope(0, h)
-            gather_dy(0, halves[h])
-        prepare(1)
+        prepare(0)
         out_rows = []
-        for b, tag in enumerate(("ts_all", "h_all0", "h_all1", "dy_all0")):
+        for b, tag in enumerate(("ts_all", "ts_listed", "identity", "h_all0")):
             out_rows.append(keep.tile([P, T], F32, name="out_rows%d" % b, tag=tag))
             nc.gpsimd.memset(out_rows[b][:], 0.0)
-        prepare(2)
-        gather_h(3, halves[0])
-        make_slope(3, 0)
-        gather_h(3, halves[1])
-        for t in (1, 2):
+        for t in range(1, PACK):
+            prepare(t)
+        for t in range(PACK - 1):
             pick_dy(t)
             gather_dy(t, halves[0])
             multiply_picked(t)
-            if t == 1:
-                make_slope(3, 1)
         pick_dy(3)
 
         gather_dy(3, quarters[0])

@@ -45,14 +45,16 @@ def tile_attend_gex_x_kernel(tc, dyT, hT, ts, wm, offs, out):
         dy_listed = [keep.tile([P, HALF], F32, name="dy_listed%d" % t) for t in range(PACK)]
         ts_down = keep.tile([P, N // P], F32, name="ts_down")
         h_listed = [keep.tile([P, N], F32, name="h_listed%d" % t) for t in range(PACK)]
-        slope = [[keep.tile([P, HALF], F32, name="slope%d_%d" % (t, h)) for h in range(2)] for t in range(PACK)]
-        dz = keep.tile([P, PACK, N], F32, name="dz", align_bytes=MX_ALIGN)
+        slope = [[keep.tile([P, HALF], F32, name="slope%d_%d" % (t, h))[:] for h in range(2)] for t in range(PACK)]
+        dz_halves = [keep.tile([P, PACK, HALF], F32, name="dz%d" % h, align_bytes=MX_ALIGN) for h in range(2)]
         dz16_first = keep.tile([P, QUARTER * PACK], BF16, name="dz16_first", align_bytes=MX_ALIGN)
-        dz16_second = keep.tile([P, HALF * PACK], BF16, name="dz16_second", align_bytes=MX_ALIGN)
+        second_words = keep.tile([P, N], F32, name="second_words", align_bytes=MX_ALIGN)
+        dz16_second = second_words[:].bitcast(BF16)
+        slope[2][1] = second_words[:, HALF:]
         dz_codes = keep.tile([P, N], U32, name="dz_codes", align_bytes=MX_ALIGN)
         dz_scales = keep.tile([P, N], U8, name="dz_scales", align_bytes=MX_ALIGN)
         wm_raw = [keep.tile([P, PACK, P], F32, name="wm_raw%d" % b) for b in range(D_BLOCKS)]
-        wm16 = [dz[:, PACK - 1, HALF + b * QUARTER : HALF + (b + 1) * QUARTER].bitcast(BF16) for b in range(2)]
+        wm16 = [dz_halves[1][:, PACK - 1, b * QUARTER : (b + 1) * QUARTER].bitcast(BF16) for b in range(2)]
         wm16.append(keep.tile([P, P * PACK], BF16, name="wm16_2", align_bytes=MX_ALIGN)[:])
         wm16.append(dz16_first[:, : P * PACK])
         wm_codes = keep.tile([P, D], U32, name="wm_codes", align_bytes=MX_ALIGN)
@@ -88,7 +90,11 @@ def tile_attend_gex_x_kernel(tc, dyT, hT, ts, wm, offs, out):
 
         spread = [bank([P, TURNS, P], "spread%d" % h, 6 + h) for h in range(2)]
         for h, slots in enumerate(halves):
-            nc.vector.tensor_copy(ts_listed[:, slots], ts_all[:].indirect(listed(slots)))
+            if h == 0:
+                nc.vector.tensor_copy(ts_listed[:, slots], ts_all[:].indirect(listed(slots)))
+            else:
+                nc.vector.tensor_copy(ts_listed[:, quarters[2]], ts_all[:].indirect(listed(quarters[2])))
+                nc.scalar.activation(ts_listed[:, quarters[3]], ts_all[:].indirect(listed(quarters[3])), ACT.Copy)
             turned = bank([P, TURNS, P], "ts_turned%d" % h, h)
             for j in range(TURNS):
                 nc.tensor.transpose(turned[:, j, :], ts_listed[:, slots.start + j * P : slots.start + (j + 1) * P], identity[:])
@@ -102,23 +108,35 @@ def tile_attend_gex_x_kernel(tc, dyT, hT, ts, wm, offs, out):
 
         def make_slope(t, h):
             nc.vector.scalar_tensor_tensor(
-                slope[t][h][:], h_listed[t][:, halves[h]], 0.0,
+                slope[t][h], h_listed[t][:, halves[h]], 0.0,
                 spread[h][:].rearrange("p j s -> p (j s)"), MAX, MULT,
             )
+
+        def dz(planes, slots):
+            h = slots.start // HALF
+            return dz_halves[h][:, planes, slots.start - h * HALF : slots.stop - h * HALF]
 
         def gather_dy(t, slots):
             h = slots.start // HALF
             part = slope[t][h][:, slots.start - h * HALF : slots.stop - h * HALF]
-            nc.vector.tensor_tensor(dz[:, t, slots], dy_all[t][:].indirect(listed(slots)), part, MULT)
+            nc.vector.tensor_tensor(dz(t, slots), dy_all[t][:].indirect(listed(slots)), part, MULT)
 
         def dz16(slots):
-            return dz16_first[:] if slots.stop <= HALF else dz16_second[:]
+            if slots.stop <= HALF:
+                return dz16_first[:]
+            return dz16_second[:, PACK * (slots.start - HALF) : PACK * (slots.stop - HALF)]
 
-        def round_dz(slots):
-            nc.vector.tensor_copy(
-                dz16(slots).rearrange("p (c i t) -> p c t i", i=LINE, t=PACK),
-                dz[:, :, slots].rearrange("p t (c i) -> p c t i", i=LINE),
+        def rounding(slots, planes):
+            return (
+                dz16(slots).rearrange("p (c i t) -> p c t i", i=LINE, t=PACK)[:, :, planes, :],
+                dz(planes, slots).rearrange("p t (c i) -> p c t i", i=LINE),
             )
+
+        def round_dz(slots, planes=slice(0, PACK)):
+            nc.vector.tensor_copy(*rounding(slots, planes))
+
+        def round_dz_early(slots):
+            nc.scalar.activation(*rounding(slots, slice(0, 2)), ACT.Copy)
 
         def round_wm(b):
             dst = wm16[b].rearrange("p (c i t) -> p c t i", i=LINE, t=PACK)
@@ -151,7 +169,7 @@ def tile_attend_gex_x_kernel(tc, dyT, hT, ts, wm, offs, out):
 
         def sums_at(b, slots):
             if b == 2 and slots.stop <= HALF:
-                return dz[:, 0, HALF + slots.start : HALF + slots.stop]
+                return dz_halves[1][:, 2, slots]
             return dx[b][:, slots]
 
         def product_s(b, slots, k):
@@ -176,11 +194,11 @@ def tile_attend_gex_x_kernel(tc, dyT, hT, ts, wm, offs, out):
             for h in range(2):
                 make_slope(t, h)
 
-        def pick_dy(t):
-            nc.scalar.activation(dy_listed[t][:], dy_all[t][:].indirect(listed(halves[1])), ACT.Copy)
+        def pick_dy(t, h):
+            nc.scalar.activation(dy_listed[t][:], dy_all[t][:].indirect(listed(halves[h])), ACT.Copy)
 
-        def multiply_picked(t):
-            nc.vector.tensor_tensor(dz[:, t, halves[1]], dy_listed[t][:], slope[t][1][:], MULT)
+        def multiply_picked(t, h):
+            nc.vector.tensor_tensor(dz(t, halves[h]), dy_listed[t][:], slope[t][h], MULT)
 
         prepare(0)
         out_rows = []
@@ -190,10 +208,12 @@ def tile_attend_gex_x_kernel(tc, dyT, hT, ts, wm, offs, out):
         for t in range(1, PACK):
             prepare(t)
         for t in range(PACK - 1):
-            pick_dy(t)
-            gather_dy(t, halves[0])
-            multiply_picked(t)
-        pick_dy(3)
+            pick_dy(t, 0)
+            gather_dy(t, halves[1])
+            multiply_picked(t, 0)
+            if t:
+                round_dz_early(quarters[1 + t])
+        pick_dy(3, 1)
 
         gather_dy(3, quarters[0])
         gather_dy(3, quarters[1])
@@ -207,14 +227,14 @@ def tile_attend_gex_x_kernel(tc, dyT, hT, ts, wm, offs, out):
         product_s(0, quarters[0], 0)
         product_s(1, quarters[0], 1)
         round_dz(quarters[1])
-        multiply_picked(3)
+        multiply_picked(3, 1)
         quantize_dz(quarters[1])
         quantize_wm(2)
         scatter_s(0, quarters[0])
         product_s(0, quarters[1], 2)
         product_s(1, quarters[1], 3)
         scatter_s(1, quarters[0])
-        round_dz(halves[1])
+        round_dz(halves[1], slice(2, PACK))
         round_wm(3)
         product_v(2, halves[0], 4)
         quantize_dz(halves[1])
@@ -225,8 +245,7 @@ def tile_attend_gex_x_kernel(tc, dyT, hT, ts, wm, offs, out):
         product_s(1, halves[1], 6)
         product_v(2, halves[1], 7)
         product_v(3, halves[1], 0)
-        product_v(3, quarters[1], 2)
-        product_s(3, quarters[0], 1)
+        product_v(3, halves[0], 1)
         scatter_s(0, quarters[2])
         scatter_v(2, halves[1])
         store(2)

@@ -27,6 +27,8 @@ D_BLOCKS = D // P
 LINE = 4
 MX_ALIGN = 64
 TURNS = HALF // P
+SPREAD_BANK = 6
+BLOCK1_CUT = QUARTER + (N - QUARTER) // 2
 
 
 def tile_attend_gex_x_kernel(tc, dyT, hT, ts, wm, offs, out):
@@ -45,18 +47,28 @@ def tile_attend_gex_x_kernel(tc, dyT, hT, ts, wm, offs, out):
         dy_listed = [keep.tile([P, HALF], F32, name="dy_listed%d" % t) for t in range(PACK)]
         ts_down = keep.tile([P, N // P], F32, name="ts_down")
         h_listed = [keep.tile([P, N], F32, name="h_listed%d" % t) for t in range(PACK)]
-        slope = [[keep.tile([P, HALF], F32, name="slope%d_%d" % (t, h))[:] for h in range(2)] for t in range(PACK)]
+        slope = {
+            (t, h): keep.tile([P, HALF], F32, name="slope%d_%d" % (t, h))[:]
+            for t in range(PACK)
+            for h in range(2)
+            if (t, h) != (2, 1)
+        }
         dz_halves = [keep.tile([P, PACK, HALF], F32, name="dz%d" % h, align_bytes=MX_ALIGN) for h in range(2)]
-        dz16_first = keep.tile([P, QUARTER * PACK], BF16, name="dz16_first", align_bytes=MX_ALIGN)
+
+        dz16_first = keep.tile([P, HALF * PACK], BF16, name="dz16_first", align_bytes=MX_ALIGN)
         second_words = keep.tile([P, N], F32, name="second_words", align_bytes=MX_ALIGN)
         dz16_second = second_words[:].bitcast(BF16)
-        slope[2][1] = second_words[:, HALF:]
+        slope[2, 1] = second_words[:, HALF:]
         dz_codes = keep.tile([P, N], U32, name="dz_codes", align_bytes=MX_ALIGN)
         dz_scales = keep.tile([P, N], U8, name="dz_scales", align_bytes=MX_ALIGN)
         wm_raw = [keep.tile([P, PACK, P], F32, name="wm_raw%d" % b) for b in range(D_BLOCKS)]
-        wm16 = [dz_halves[1][:, PACK - 1, b * QUARTER : (b + 1) * QUARTER].bitcast(BF16) for b in range(2)]
-        wm16.append(keep.tile([P, P * PACK], BF16, name="wm16_2", align_bytes=MX_ALIGN)[:])
-        wm16.append(dz16_first[:, : P * PACK])
+        on_quarter1 = dz16_first[:, QUARTER * PACK : QUARTER * PACK + P * PACK]
+        wm16 = [
+            on_quarter1,
+            dz_halves[1][:, PACK - 1, :QUARTER].bitcast(BF16),
+            keep.tile([P, P * PACK], BF16, name="wm16_2", align_bytes=MX_ALIGN)[:],
+            on_quarter1,
+        ]
         wm_codes = keep.tile([P, D], U32, name="wm_codes", align_bytes=MX_ALIGN)
         wm_scales = keep.tile([P, D], U8, name="wm_scales", align_bytes=MX_ALIGN)
 
@@ -66,12 +78,9 @@ def tile_attend_gex_x_kernel(tc, dyT, hT, ts, wm, offs, out):
 
         nc.sync.dma_start(ts_all[P - 1 :, :], ts[0:1, :])
         nc.sync.dma_start(offsets[:], offs)
-        nc.sync.dma_start(h_all[0][:], h_rows[:, 0, :])
-        for tiles, rows, t in (
-            (h_all, h_rows, 1), (h_all, h_rows, 2), (h_all, h_rows, 3),
-            (dy_all, dy_rows, 0), (dy_all, dy_rows, 1), (dy_all, dy_rows, 2), (dy_all, dy_rows, 3),
-        ):
-            nc.sync.dma_start(tiles[t][:], rows[:, t, :])
+        for tiles, rows in ((h_all, h_rows), (dy_all, dy_rows)):
+            for t in range(PACK):
+                nc.sync.dma_start(tiles[t][:], rows[:, t, :])
         for b in range(D_BLOCKS):
             nc.sync.dma_start(wm_raw[b][:], wm_rows[:, :, b * P : (b + 1) * P])
 
@@ -80,71 +89,88 @@ def tile_attend_gex_x_kernel(tc, dyT, hT, ts, wm, offs, out):
 
         whole = slice(0, N)
         halves = [slice(0, HALF), slice(HALF, N)]
-        quarters = [slice(q * QUARTER, (q + 1) * QUARTER) for q in range(4)]
+        quarters = [slice(q * QUARTER, (q + 1) * QUARTER) for q in range(N // QUARTER)]
+        all_planes, early_planes, late_planes = slice(0, PACK), slice(0, 2), slice(2, PACK)
 
         def listed(slots):
             return offsets[:, slots.start // LIST_ROWS : slots.stop // LIST_ROWS]
 
+        def in_half(slots):
+            h = slots.start // HALF
+            return h, slice(slots.start - h * HALF, slots.stop - h * HALF)
+
         def bank(shape, name, k):
             return psum.tile(shape, F32, name=name, tag="bank%d" % k)
 
-        spread = [bank([P, TURNS, P], "spread%d" % h, 6 + h) for h in range(2)]
+        def gather_on_vector(dst, window, slots):
+            nc.vector.tensor_copy(dst, window[:].indirect(listed(slots)))
+
+        def gather_on_scalar(dst, window, slots):
+            nc.scalar.activation(dst, window[:].indirect(listed(slots)), ACT.Copy)
+
+        spread = [bank([P, TURNS, P], "spread%d" % h, SPREAD_BANK + h) for h in range(2)]
         for h, slots in enumerate(halves):
             if h == 0:
-                nc.vector.tensor_copy(ts_listed[:, slots], ts_all[:].indirect(listed(slots)))
+                gather_on_vector(ts_listed[:, slots], ts_all, slots)
             else:
-                nc.vector.tensor_copy(ts_listed[:, quarters[2]], ts_all[:].indirect(listed(quarters[2])))
-                nc.scalar.activation(ts_listed[:, quarters[3]], ts_all[:].indirect(listed(quarters[3])), ACT.Copy)
+                gather_on_vector(ts_listed[:, quarters[2]], ts_all, quarters[2])
+                gather_on_scalar(ts_listed[:, quarters[3]], ts_all, quarters[3])
             turned = bank([P, TURNS, P], "ts_turned%d" % h, h)
             for j in range(TURNS):
-                nc.tensor.transpose(turned[:, j, :], ts_listed[:, slots.start + j * P : slots.start + (j + 1) * P], identity[:])
+                first = slots.start + j * P
+                nc.tensor.transpose(turned[:, j, :], ts_listed[:, first : first + P], identity[:])
             nc.vector.tensor_scalar_mul(ts_down[:, h * TURNS : (h + 1) * TURNS], turned[:, :, P - 1], 2.0)
             for j in range(TURNS):
                 col = h * TURNS + j
                 nc.tensor.transpose(spread[h][:, j, :], ts_down[:, col : col + 1].to_broadcast([P, P]), identity[:])
 
-        def gather_h(t, slots):
-            nc.scalar.activation(h_listed[t][:, slots], h_all[t][:].indirect(listed(slots)), ACT.Copy)
-
-        def make_slope(t, h):
-            nc.vector.scalar_tensor_tensor(
-                slope[t][h], h_listed[t][:, halves[h]], 0.0,
-                spread[h][:].rearrange("p j s -> p (j s)"), MAX, MULT,
-            )
+        def make_slopes(t):
+            gather_on_scalar(h_listed[t][:, halves[0]], h_all[t], halves[0])
+            gather_on_vector(h_listed[t][:, quarters[3]], h_all[t], quarters[3])
+            gather_on_scalar(h_listed[t][:, quarters[2]], h_all[t], quarters[2])
+            for h in range(2):
+                nc.vector.scalar_tensor_tensor(
+                    slope[t, h], h_listed[t][:, halves[h]], 0.0,
+                    spread[h][:].rearrange("p j s -> p (j s)"), MAX, MULT,
+                )
 
         def dz(planes, slots):
-            h = slots.start // HALF
-            return dz_halves[h][:, planes, slots.start - h * HALF : slots.stop - h * HALF]
+            h, cols = in_half(slots)
+            return dz_halves[h][:, planes, cols]
 
-        def gather_dy(t, slots):
-            h = slots.start // HALF
-            part = slope[t][h][:, slots.start - h * HALF : slots.stop - h * HALF]
-            nc.vector.tensor_tensor(dz(t, slots), dy_all[t][:].indirect(listed(slots)), part, MULT)
+        def gather_times_slope(t, slots):
+            h, cols = in_half(slots)
+            nc.vector.tensor_tensor(dz(t, slots), dy_all[t][:].indirect(listed(slots)), slope[t, h][:, cols], MULT)
+
+        def pick_dy(t, h):
+            gather_on_scalar(dy_listed[t][:], dy_all[t], halves[h])
+
+        def picked_times_slope(t, h):
+            nc.vector.tensor_tensor(dz(t, halves[h]), dy_listed[t][:], slope[t, h], MULT)
 
         def dz16(slots):
-            if slots.stop <= HALF:
-                return dz16_first[:]
-            return dz16_second[:, PACK * (slots.start - HALF) : PACK * (slots.stop - HALF)]
+            h, cols = in_half(slots)
+            return (dz16_first[:], dz16_second)[h][:, PACK * cols.start : PACK * cols.stop]
 
-        def rounding(slots, planes):
+        def interleaved(dst, src):
             return (
-                dz16(slots).rearrange("p (c i t) -> p c t i", i=LINE, t=PACK)[:, :, planes, :],
-                dz(planes, slots).rearrange("p t (c i) -> p c t i", i=LINE),
+                dst.rearrange("p (c i t) -> p c t i", i=LINE, t=PACK),
+                src.rearrange("p t (c i) -> p c t i", i=LINE),
             )
 
-        def round_dz(slots, planes=slice(0, PACK)):
-            nc.vector.tensor_copy(*rounding(slots, planes))
+        def round_dz_on_vector(slots, planes):
+            dst, src = interleaved(dz16(slots), dz(planes, slots))
+            nc.vector.tensor_copy(dst[:, :, planes, :], src)
 
-        def round_dz_early(slots):
-            nc.scalar.activation(*rounding(slots, slice(0, 2)), ACT.Copy)
+        def round_dz_on_scalar(slots, planes):
+            dst, src = interleaved(dz16(slots), dz(planes, slots))
+            nc.scalar.activation(dst[:, :, planes, :], src, ACT.Copy)
 
-        def round_wm(b):
-            dst = wm16[b].rearrange("p (c i t) -> p c t i", i=LINE, t=PACK)
-            src = wm_raw[b][:].rearrange("p t (c i) -> p c t i", i=LINE)
-            if b == D_BLOCKS - 1:
-                nc.vector.tensor_copy(dst, src)
-            else:
-                nc.scalar.activation(dst, src, ACT.Copy)
+        def round_wm_on_vector(b):
+            nc.vector.tensor_copy(*interleaved(wm16[b], wm_raw[b][:]))
+
+        def round_wm_on_scalar(b):
+            nc.scalar.activation(*interleaved(wm16[b], wm_raw[b][:]), ACT.Copy)
 
         def quantize_dz(slots):
             nc.vector.quantize_mx(out=dz_codes[:, slots].bitcast(E5M2X4), scales=dz_scales[:, slots], in_=dz16(slots))
@@ -172,87 +198,77 @@ def tile_attend_gex_x_kernel(tc, dyT, hT, ts, wm, offs, out):
                 return dz_halves[1][:, 2, slots]
             return dx[b][:, slots]
 
-        def product_s(b, slots, k):
+        def product_via_scalar(b, slots, k):
             nc.scalar.activation(sums_at(b, slots), multiply(b, slots, k)[:], ACT.Copy)
 
-        def product_v(b, slots, k):
+        def product_via_vector(b, slots, k):
             nc.vector.tensor_copy(sums_at(b, slots), multiply(b, slots, k)[:])
 
-        def scatter_s(b, slots):
+        def scatter_on_scalar(b, slots):
             nc.scalar.activation(out_rows[b][:].indirect(listed(slots)), sums_at(b, slots), ACT.Copy)
 
-        def scatter_v(b, slots):
+        def scatter_on_vector(b, slots):
             nc.vector.tensor_copy(out_rows[b][:].indirect(listed(slots)), sums_at(b, slots))
 
-        def store(b):
-            nc.sync.dma_start(out[b * P : (b + 1) * P, :], out_rows[b][:])
+        def store(b, queue=nc.sync):
+            queue.dma_start(out[b * P : (b + 1) * P, :], out_rows[b][:])
 
-        def prepare(t):
-            gather_h(t, halves[0])
-            nc.vector.tensor_copy(h_listed[t][:, quarters[3]], h_all[t][:].indirect(listed(quarters[3])))
-            gather_h(t, quarters[2])
-            for h in range(2):
-                make_slope(t, h)
-
-        def pick_dy(t, h):
-            nc.scalar.activation(dy_listed[t][:], dy_all[t][:].indirect(listed(halves[h])), ACT.Copy)
-
-        def multiply_picked(t, h):
-            nc.vector.tensor_tensor(dz(t, halves[h]), dy_listed[t][:], slope[t][h], MULT)
-
-        prepare(0)
+        make_slopes(0)
         out_rows = []
         for b, tag in enumerate(("ts_all", "ts_listed", "identity", "h_all0")):
             out_rows.append(keep.tile([P, T], F32, name="out_rows%d" % b, tag=tag))
             nc.gpsimd.memset(out_rows[b][:], 0.0)
         for t in range(1, PACK):
-            prepare(t)
+            make_slopes(t)
+
         for t in range(PACK - 1):
             pick_dy(t, 0)
-            gather_dy(t, halves[1])
-            multiply_picked(t, 0)
-            if t:
-                round_dz_early(quarters[1 + t])
-        pick_dy(3, 1)
+            gather_times_slope(t, halves[1])
+            picked_times_slope(t, 0)
+            if t > 0:
+                round_dz_on_scalar(quarters[1 + t], early_planes)
 
-        gather_dy(3, quarters[0])
-        gather_dy(3, quarters[1])
-        round_wm(0)
-        round_wm(1)
-        round_dz(quarters[0])
+        pick_dy(PACK - 1, 1)
+        gather_times_slope(PACK - 1, quarters[0])
+        gather_times_slope(PACK - 1, quarters[1])
+        round_wm_on_scalar(0)
+        round_wm_on_scalar(1)
+        round_dz_on_vector(quarters[0], all_planes)
         quantize_wm(0)
         quantize_dz(quarters[0])
         quantize_wm(1)
-        round_wm(2)
-        product_s(0, quarters[0], 0)
-        product_s(1, quarters[0], 1)
-        round_dz(quarters[1])
-        multiply_picked(3, 1)
+        round_wm_on_scalar(2)
+        product_via_scalar(0, quarters[0], 0)
+        product_via_scalar(1, quarters[0], 1)
+        round_dz_on_vector(quarters[1], all_planes)
+        picked_times_slope(PACK - 1, 1)
         quantize_dz(quarters[1])
         quantize_wm(2)
-        scatter_s(0, quarters[0])
-        product_s(0, quarters[1], 2)
-        product_s(1, quarters[1], 3)
-        scatter_s(1, quarters[0])
-        round_dz(halves[1], slice(2, PACK))
-        round_wm(3)
-        product_v(2, halves[0], 4)
+
+        scatter_on_scalar(0, quarters[0])
+        product_via_scalar(0, quarters[1], 2)
+        product_via_scalar(1, quarters[1], 3)
+        scatter_on_scalar(1, quarters[0])
+        round_dz_on_vector(halves[1], late_planes)
+        round_wm_on_vector(3)
+        product_via_vector(2, halves[0], 4)
         quantize_dz(halves[1])
         quantize_wm(3)
-        scatter_v(2, halves[0])
-        scatter_s(0, quarters[1])
-        product_s(0, halves[1], 5)
-        product_s(1, halves[1], 6)
-        product_v(2, halves[1], 7)
-        product_v(3, halves[1], 0)
-        product_v(3, halves[0], 1)
-        scatter_s(0, quarters[2])
-        scatter_v(2, halves[1])
+        scatter_on_vector(2, halves[0])
+        scatter_on_scalar(0, quarters[1])
+        product_via_scalar(0, halves[1], 5)
+        product_via_scalar(1, halves[1], 6)
+        product_via_vector(2, halves[1], 7)
+        product_via_vector(3, halves[1], 0)
+        product_via_vector(3, halves[0], 1)
+
+        scatter_on_scalar(0, quarters[2])
+        scatter_on_vector(2, halves[1])
         store(2)
-        scatter_s(1, slice(256, 640))
-        scatter_s(0, quarters[3])
+        scatter_on_scalar(1, slice(QUARTER, BLOCK1_CUT))
+        scatter_on_scalar(0, quarters[3])
         store(0)
-        scatter_s(1, slice(640, N))
-        store(1)
-        scatter_v(3, whole)
+        scatter_on_scalar(1, slice(BLOCK1_CUT, N))
+        store(1, nc.scalar)
+        scatter_on_vector(3, whole)
         store(3)

@@ -55,20 +55,17 @@ def tile_attend_gex_x_kernel(tc, dyT, hT, ts, wm, offs, out):
         }
         dz_halves = [keep.tile([P, PACK, HALF], F32, name="dz%d" % h, align_bytes=MX_ALIGN) for h in range(2)]
 
-        dz16_first = keep.tile([P, HALF * PACK], BF16, name="dz16_first", align_bytes=MX_ALIGN)
-        second_words = keep.tile([P, N], F32, name="second_words", align_bytes=MX_ALIGN)
-        dz16_second = second_words[:].bitcast(BF16)
-        slope[2, 1] = second_words[:, HALF:]
+        words = keep.tile([P, 2 * N], F32, name="words", align_bytes=MX_ALIGN)
+        dz16_second = words[:, :N].bitcast(BF16)
+        dz16_quarter1 = words[:, N : N + HALF].bitcast(BF16)
+        dz16_quarter0 = words[:, N + HALF :].bitcast(BF16)
+        slope[2, 1] = words[:, N - QUARTER : N + QUARTER]
         dz_codes = keep.tile([P, N], U32, name="dz_codes", align_bytes=MX_ALIGN)
         dz_scales = keep.tile([P, N], U8, name="dz_scales", align_bytes=MX_ALIGN)
         wm_raw = [keep.tile([P, PACK, P], F32, name="wm_raw%d" % b) for b in range(D_BLOCKS)]
-        on_quarter1 = dz16_first[:, QUARTER * PACK : QUARTER * PACK + P * PACK]
-        wm16 = [
-            on_quarter1,
-            dz_halves[1][:, PACK - 1, :QUARTER].bitcast(BF16),
-            keep.tile([P, P * PACK], BF16, name="wm16_2", align_bytes=MX_ALIGN)[:],
-            on_quarter1,
-        ]
+        wm16 = [dz_halves[1][:, PACK - 1, b * QUARTER : (b + 1) * QUARTER].bitcast(BF16) for b in range(2)]
+        wm16.append(keep.tile([P, P * PACK], BF16, name="wm16_2", align_bytes=MX_ALIGN)[:])
+        wm16.append(dz16_quarter1[:, : P * PACK])
         wm_codes = keep.tile([P, D], U32, name="wm_codes", align_bytes=MX_ALIGN)
         wm_scales = keep.tile([P, D], U8, name="wm_scales", align_bytes=MX_ALIGN)
 
@@ -150,7 +147,9 @@ def tile_attend_gex_x_kernel(tc, dyT, hT, ts, wm, offs, out):
 
         def dz16(slots):
             h, cols = in_half(slots)
-            return (dz16_first[:], dz16_second)[h][:, PACK * cols.start : PACK * cols.stop]
+            if h:
+                return dz16_second[:, PACK * cols.start : PACK * cols.stop]
+            return dz16_quarter1 if cols.start else dz16_quarter0
 
         def interleaved(dst, src):
             return (
@@ -227,6 +226,7 @@ def tile_attend_gex_x_kernel(tc, dyT, hT, ts, wm, offs, out):
             picked_times_slope(t, 0)
             if t > 0:
                 round_dz_on_scalar(quarters[1 + t], early_planes)
+        round_dz_on_vector(quarters[1], early_planes)
 
         pick_dy(PACK - 1, 1)
         gather_times_slope(PACK - 1, quarters[0])
@@ -234,13 +234,13 @@ def tile_attend_gex_x_kernel(tc, dyT, hT, ts, wm, offs, out):
         round_wm_on_scalar(0)
         round_wm_on_scalar(1)
         round_dz_on_vector(quarters[0], all_planes)
+        round_dz_on_vector(quarters[1], late_planes)
         quantize_wm(0)
         quantize_dz(quarters[0])
         quantize_wm(1)
         round_wm_on_scalar(2)
         product_via_scalar(0, quarters[0], 0)
         product_via_scalar(1, quarters[0], 1)
-        round_dz_on_vector(quarters[1], all_planes)
         picked_times_slope(PACK - 1, 1)
         quantize_dz(quarters[1])
         quantize_wm(2)

@@ -16,10 +16,12 @@ E4M3X4 = mybir.dt.float8_e4m3fn_x4
 E5M2X4 = mybir.dt.float8_e5m2_x4
 ACT = mybir.ActivationFunctionType
 MULT = mybir.AluOpType.mult
+ADD = mybir.AluOpType.add
 MAX = mybir.AluOpType.max
 
 P = 128
 PACK = 4
+LAST = PACK - 1
 HALF = 512
 QUARTER = 256
 LIST_ROWS = 16
@@ -28,7 +30,8 @@ LINE = 4
 MX_ALIGN = 64
 TURNS = HALF // P
 SPREAD_BANK = 6
-BLOCK1_CUT = QUARTER + (N - QUARTER) // 2
+COVER = 448
+LONG = 384
 
 
 def tile_attend_gex_x_kernel(tc, dyT, hT, ts, wm, offs, out):
@@ -37,37 +40,41 @@ def tile_attend_gex_x_kernel(tc, dyT, hT, ts, wm, offs, out):
         keep = ctx.enter_context(tc.tile_pool(name="keep", bufs=1))
         psum = ctx.enter_context(tc.psum_pool(name="psum", bufs=1))
 
+        whole = slice(0, N)
+        halves = [slice(0, HALF), slice(HALF, N)]
+        quarters = [slice(q * QUARTER, (q + 1) * QUARTER) for q in range(N // QUARTER)]
+        all_planes, early_planes, late_planes = slice(0, PACK), slice(0, 2), slice(2, PACK)
+
         offsets = keep.tile([P, N // LIST_ROWS], U16, name="offsets")
         ts_all = keep.tile([P, T], F32, name="ts_all", tag="ts_all")
         identity = keep.tile([P, P], F32, name="identity", tag="identity")
         h_all = [keep.tile([P, T], F32, name="h_all%d" % t, tag="h_all%d" % t) for t in range(PACK)]
         dy_all = [keep.tile([P, T], F32, name="dy_all%d" % t, tag="dy_all%d" % t) for t in range(PACK)]
-        dx = [keep.tile([P, N], F32, name="dx%d" % b) for b in range(D_BLOCKS)]
         ts_listed = keep.tile([P, N], F32, name="ts_listed", tag="ts_listed")
-        dy_listed = [keep.tile([P, HALF], F32, name="dy_listed%d" % t) for t in range(PACK)]
         ts_down = keep.tile([P, N // P], F32, name="ts_down")
         h_listed = [keep.tile([P, N], F32, name="h_listed%d" % t) for t in range(PACK)]
+        dy_listed = [keep.tile([P, HALF], F32, name="dy_listed%d" % t) for t in range(PACK)]
+        dz_halves = [keep.tile([P, PACK * HALF], F32, name="dz%d" % h, align_bytes=MX_ALIGN) for h in range(2)]
+        dz16_quarter0 = keep.tile([P, PACK * QUARTER], BF16, name="dz16_quarter0", align_bytes=MX_ALIGN)
+        dz_codes = keep.tile([P, N], U32, name="dz_codes", align_bytes=MX_ALIGN)
+        dz_scales = keep.tile([P, N], U8, name="dz_scales", align_bytes=MX_ALIGN)
+        wm_raw = [keep.tile([P, PACK, P], F32, name="wm_raw%d" % b) for b in range(D_BLOCKS)]
+        wm_codes = keep.tile([P, D], U32, name="wm_codes", align_bytes=MX_ALIGN)
+        wm_scales = keep.tile([P, D], U8, name="wm_scales", align_bytes=MX_ALIGN)
+
+        late_bytes = dz_halves[1][:, LAST * HALF :].bitcast(BF16)
+        shared = keep.tile([P, N], F32, name="shared", align_bytes=MX_ALIGN)
+        dz16_second = shared[:].bitcast(BF16)
+        wm16 = [keep.tile([P, P * PACK], BF16, name="wm16_%d" % b, align_bytes=MX_ALIGN)[:] for b in range(LAST)]
+        wm16.append(late_bytes[:, : P * PACK])
+        sums = [keep.tile([P, N], F32, name="sums%d" % b) for b in range(D_BLOCKS - 1)] + [shared]
         slope = {
             (t, h): keep.tile([P, HALF], F32, name="slope%d_%d" % (t, h))[:]
             for t in range(PACK)
             for h in range(2)
             if (t, h) != (2, 1)
         }
-        dz_halves = [keep.tile([P, PACK, HALF], F32, name="dz%d" % h, align_bytes=MX_ALIGN) for h in range(2)]
-
-        words = keep.tile([P, 2 * N], F32, name="words", align_bytes=MX_ALIGN)
-        dz16_second = words[:, :N].bitcast(BF16)
-        dz16_quarter1 = words[:, N : N + HALF].bitcast(BF16)
-        dz16_quarter0 = words[:, N + HALF :].bitcast(BF16)
-        slope[2, 1] = words[:, N - QUARTER : N + QUARTER]
-        dz_codes = keep.tile([P, N], U32, name="dz_codes", align_bytes=MX_ALIGN)
-        dz_scales = keep.tile([P, N], U8, name="dz_scales", align_bytes=MX_ALIGN)
-        wm_raw = [keep.tile([P, PACK, P], F32, name="wm_raw%d" % b) for b in range(D_BLOCKS)]
-        wm16 = [dz_halves[1][:, PACK - 1, b * QUARTER : (b + 1) * QUARTER].bitcast(BF16) for b in range(2)]
-        wm16.append(keep.tile([P, P * PACK], BF16, name="wm16_2", align_bytes=MX_ALIGN)[:])
-        wm16.append(dz16_quarter1[:, : P * PACK])
-        wm_codes = keep.tile([P, D], U32, name="wm_codes", align_bytes=MX_ALIGN)
-        wm_scales = keep.tile([P, D], U8, name="wm_scales", align_bytes=MX_ALIGN)
+        slope[2, 1] = shared[:, halves[1]]
 
         h_rows = hT.rearrange("(p t) c -> p t c", t=PACK)
         dy_rows = dyT.rearrange("(p t) c -> p t c", t=PACK)
@@ -83,11 +90,6 @@ def tile_attend_gex_x_kernel(tc, dyT, hT, ts, wm, offs, out):
 
         nc.vector.memset(ts_all[: P - 1, :].bitcast(I32), 0)
         make_identity(nc, identity[:])
-
-        whole = slice(0, N)
-        halves = [slice(0, HALF), slice(HALF, N)]
-        quarters = [slice(q * QUARTER, (q + 1) * QUARTER) for q in range(N // QUARTER)]
-        all_planes, early_planes, late_planes = slice(0, PACK), slice(0, 2), slice(2, PACK)
 
         def listed(slots):
             return offsets[:, slots.start // LIST_ROWS : slots.stop // LIST_ROWS]
@@ -133,7 +135,7 @@ def tile_attend_gex_x_kernel(tc, dyT, hT, ts, wm, offs, out):
 
         def dz(planes, slots):
             h, cols = in_half(slots)
-            return dz_halves[h][:, planes, cols]
+            return dz_halves[h][:].rearrange("p (t c) -> p t c", t=PACK)[:, planes, cols]
 
         def gather_times_slope(t, slots):
             h, cols = in_half(slots)
@@ -142,14 +144,14 @@ def tile_attend_gex_x_kernel(tc, dyT, hT, ts, wm, offs, out):
         def pick_dy(t, h):
             gather_on_scalar(dy_listed[t][:], dy_all[t], halves[h])
 
-        def picked_times_slope(t, h):
-            nc.vector.tensor_tensor(dz(t, halves[h]), dy_listed[t][:], slope[t, h], MULT)
+        def picked_times_slope(engine, t, h):
+            engine.tensor_tensor(dz(t, halves[h]), dy_listed[t][:], slope[t, h], MULT)
 
         def dz16(slots):
             h, cols = in_half(slots)
             if h:
                 return dz16_second[:, PACK * cols.start : PACK * cols.stop]
-            return dz16_quarter1 if cols.start else dz16_quarter0
+            return late_bytes if cols.start else dz16_quarter0[:]
 
         def interleaved(dst, src):
             return (
@@ -157,13 +159,9 @@ def tile_attend_gex_x_kernel(tc, dyT, hT, ts, wm, offs, out):
                 src.rearrange("p t (c i) -> p c t i", i=LINE),
             )
 
-        def round_dz_on_vector(slots, planes):
+        def dz_views(slots, planes):
             dst, src = interleaved(dz16(slots), dz(planes, slots))
-            nc.vector.tensor_copy(dst[:, :, planes, :], src)
-
-        def round_dz_on_scalar(slots, planes):
-            dst, src = interleaved(dz16(slots), dz(planes, slots))
-            nc.scalar.activation(dst[:, :, planes, :], src, ACT.Copy)
+            return dst[:, :, planes, :], src
 
         def round_wm_on_vector(b):
             nc.vector.tensor_copy(*interleaved(wm16[b], wm_raw[b][:]))
@@ -192,22 +190,17 @@ def tile_attend_gex_x_kernel(tc, dyT, hT, ts, wm, offs, out):
             )
             return acc
 
-        def sums_at(b, slots):
-            if b == 2 and slots.stop <= HALF:
-                return dz_halves[1][:, 2, slots]
-            return dx[b][:, slots]
-
         def product_via_scalar(b, slots, k):
-            nc.scalar.activation(sums_at(b, slots), multiply(b, slots, k)[:], ACT.Copy)
+            nc.scalar.activation(sums[b][:, slots], multiply(b, slots, k)[:], ACT.Copy)
 
         def product_via_vector(b, slots, k):
-            nc.vector.tensor_copy(sums_at(b, slots), multiply(b, slots, k)[:])
+            nc.vector.tensor_copy(sums[b][:, slots], multiply(b, slots, k)[:])
 
         def scatter_on_scalar(b, slots):
-            nc.scalar.activation(out_rows[b][:].indirect(listed(slots)), sums_at(b, slots), ACT.Copy)
+            nc.scalar.activation(out_rows[b][:].indirect(listed(slots)), sums[b][:, slots], ACT.Copy)
 
         def scatter_on_vector(b, slots):
-            nc.vector.tensor_copy(out_rows[b][:].indirect(listed(slots)), sums_at(b, slots))
+            nc.vector.tensor_copy(out_rows[b][:].indirect(listed(slots)), sums[b][:, slots])
 
         def store(b, queue=nc.sync):
             queue.dma_start(out[b * P : (b + 1) * P, :], out_rows[b][:])
@@ -220,55 +213,59 @@ def tile_attend_gex_x_kernel(tc, dyT, hT, ts, wm, offs, out):
         for t in range(1, PACK):
             make_slopes(t)
 
-        for t in range(PACK - 1):
+        for t in range(LAST):
             pick_dy(t, 0)
             gather_times_slope(t, halves[1])
-            picked_times_slope(t, 0)
+            picked_times_slope(nc.vector, t, 0)
             if t > 0:
-                round_dz_on_scalar(quarters[1 + t], early_planes)
-        round_dz_on_vector(quarters[1], early_planes)
+                nc.scalar.activation(*dz_views(quarters[1 + t], early_planes), ACT.Copy)
+        nc.vector.tensor_copy(*dz_views(quarters[1], early_planes))
 
-        pick_dy(PACK - 1, 1)
-        gather_times_slope(PACK - 1, quarters[0])
-        gather_times_slope(PACK - 1, quarters[1])
+        pick_dy(LAST, 1)
+        gather_times_slope(LAST, quarters[0])
+        gather_times_slope(LAST, quarters[1])
         round_wm_on_scalar(0)
         round_wm_on_scalar(1)
-        round_dz_on_vector(quarters[0], all_planes)
-        round_dz_on_vector(quarters[1], late_planes)
+        round_wm_on_scalar(2)
+        nc.vector.tensor_copy(*dz_views(quarters[0], all_planes))
         quantize_wm(0)
         quantize_dz(quarters[0])
-        quantize_wm(1)
-        round_wm_on_scalar(2)
         product_via_scalar(0, quarters[0], 0)
-        product_via_scalar(1, quarters[0], 1)
-        picked_times_slope(PACK - 1, 1)
+        nc.vector.tensor_copy(*dz_views(quarters[1], late_planes))
+        quantize_wm(1)
         quantize_dz(quarters[1])
         quantize_wm(2)
+        round_wm_on_vector(3)
+        product_via_vector(1, quarters[0], 1)
+        quantize_wm(3)
+        product_via_vector(1, quarters[1], 2)
+        product_via_vector(2, halves[0], 3)
+        scatter_on_vector(1, slice(0, COVER))
+
+        picked_times_slope(nc.gpsimd, LAST, 1)
+        nc.gpsimd.tensor_scalar(*dz_views(halves[1], late_planes), 1.0, 0.0, MULT, ADD)
 
         scatter_on_scalar(0, quarters[0])
-        product_via_scalar(0, quarters[1], 2)
-        product_via_scalar(1, quarters[1], 3)
-        scatter_on_scalar(1, quarters[0])
-        round_dz_on_vector(halves[1], late_planes)
-        round_wm_on_vector(3)
-        product_via_vector(2, halves[0], 4)
-        quantize_dz(halves[1])
-        quantize_wm(3)
-        scatter_on_vector(2, halves[0])
+        product_via_scalar(0, quarters[1], 4)
+        scatter_on_scalar(2, slice(0, LONG))
         scatter_on_scalar(0, quarters[1])
-        product_via_scalar(0, halves[1], 5)
-        product_via_scalar(1, halves[1], 6)
-        product_via_vector(2, halves[1], 7)
-        product_via_vector(3, halves[1], 0)
-        product_via_vector(3, halves[0], 1)
+        quantize_dz(quarters[2])
+        quantize_dz(quarters[3])
+        product_via_vector(3, halves[0], 5)
+        product_via_vector(1, quarters[2], 6)
+        product_via_vector(1, quarters[3], 7)
+        scatter_on_vector(1, slice(COVER, quarters[2].stop))
+        product_via_scalar(0, halves[1], 0)
+        product_via_scalar(2, halves[1], 1)
+        product_via_vector(3, halves[1], 2)
 
         scatter_on_scalar(0, quarters[2])
-        scatter_on_vector(2, halves[1])
-        store(2)
-        scatter_on_scalar(1, slice(QUARTER, BLOCK1_CUT))
+        scatter_on_vector(1, quarters[3])
+        store(1)
+        scatter_on_scalar(2, slice(LONG, N - LONG))
         scatter_on_scalar(0, quarters[3])
         store(0)
-        scatter_on_scalar(1, slice(BLOCK1_CUT, N))
-        store(1, nc.scalar)
+        scatter_on_scalar(2, slice(N - LONG, N))
+        store(2, nc.scalar)
         scatter_on_vector(3, whole)
         store(3)

@@ -16,7 +16,6 @@ E4M3X4 = mybir.dt.float8_e4m3fn_x4
 E5M2X4 = mybir.dt.float8_e5m2_x4
 ACT = mybir.ActivationFunctionType
 MULT = mybir.AluOpType.mult
-ADD = mybir.AluOpType.add
 MAX = mybir.AluOpType.max
 
 P = 128
@@ -30,7 +29,8 @@ LINE = 4
 MX_ALIGN = 64
 TURNS = HALF // P
 SPREAD_BANK = 6
-COVER = 448
+COVER = 384
+HELD = 32
 LONG = 384
 
 
@@ -43,7 +43,7 @@ def tile_attend_gex_x_kernel(tc, dyT, hT, ts, wm, offs, out):
         whole = slice(0, N)
         halves = [slice(0, HALF), slice(HALF, N)]
         quarters = [slice(q * QUARTER, (q + 1) * QUARTER) for q in range(N // QUARTER)]
-        all_planes, early_planes, late_planes = slice(0, PACK), slice(0, 2), slice(2, PACK)
+        early_planes, late_planes = slice(0, 2), slice(2, PACK)
 
         offsets = keep.tile([P, N // LIST_ROWS], U16, name="offsets")
         ts_all = keep.tile([P, T], F32, name="ts_all", tag="ts_all")
@@ -53,8 +53,9 @@ def tile_attend_gex_x_kernel(tc, dyT, hT, ts, wm, offs, out):
         ts_listed = keep.tile([P, N], F32, name="ts_listed", tag="ts_listed")
         ts_down = keep.tile([P, N // P], F32, name="ts_down")
         h_listed = [keep.tile([P, N], F32, name="h_listed%d" % t) for t in range(PACK)]
-        dy_listed = [keep.tile([P, HALF], F32, name="dy_listed%d" % t) for t in range(PACK)]
-        dz_halves = [keep.tile([P, PACK * HALF], F32, name="dz%d" % h, align_bytes=MX_ALIGN) for h in range(2)]
+        dy_early = [keep.tile([P, HALF], F32, name="dy_early%d" % t) for t in range(2)]
+        dy_late = keep.tile([P, 2 * HALF], F32, name="dy_late")
+        dz_halves = [keep.tile([P, planes * HALF], F32, name="dz%d" % planes) for planes in (PACK, 2)]
         dz16_quarter0 = keep.tile([P, PACK * QUARTER], BF16, name="dz16_quarter0", align_bytes=MX_ALIGN)
         dz_codes = keep.tile([P, N], U32, name="dz_codes", align_bytes=MX_ALIGN)
         dz_scales = keep.tile([P, N], U8, name="dz_scales", align_bytes=MX_ALIGN)
@@ -62,19 +63,18 @@ def tile_attend_gex_x_kernel(tc, dyT, hT, ts, wm, offs, out):
         wm_codes = keep.tile([P, D], U32, name="wm_codes", align_bytes=MX_ALIGN)
         wm_scales = keep.tile([P, D], U8, name="wm_scales", align_bytes=MX_ALIGN)
 
-        late_bytes = dz_halves[1][:, LAST * HALF :].bitcast(BF16)
+        chain = keep.tile([P, N + HALF], F32, name="chain", align_bytes=MX_ALIGN)
+        dz16_quarter1 = chain[:, N:].bitcast(BF16)
         shared = keep.tile([P, N], F32, name="shared", align_bytes=MX_ALIGN)
         dz16_second = shared[:].bitcast(BF16)
         wm16 = [keep.tile([P, P * PACK], BF16, name="wm16_%d" % b, align_bytes=MX_ALIGN)[:] for b in range(LAST)]
-        wm16.append(late_bytes[:, : P * PACK])
+        wm16.append(chain[:, N - HELD : N - HELD + QUARTER].bitcast(BF16))
         sums = [keep.tile([P, N], F32, name="sums%d" % b) for b in range(D_BLOCKS - 1)] + [shared]
         slope = {
             (t, h): keep.tile([P, HALF], F32, name="slope%d_%d" % (t, h))[:]
-            for t in range(PACK)
-            for h in range(2)
-            if (t, h) != (2, 1)
+            for t, h in ((0, 0), (0, 1), (1, 0), (1, 1), (2, 0), (LAST, 0))
         }
-        slope[2, 1] = shared[:, halves[1]]
+        slope[2, 1], slope[LAST, 1] = chain[:, halves[0]], chain[:, halves[1]]
 
         h_rows = hT.rearrange("(p t) c -> p t c", t=PACK)
         dy_rows = dyT.rearrange("(p t) c -> p t c", t=PACK)
@@ -123,35 +123,36 @@ def tile_attend_gex_x_kernel(tc, dyT, hT, ts, wm, offs, out):
                 col = h * TURNS + j
                 nc.tensor.transpose(spread[h][:, j, :], ts_down[:, col : col + 1].to_broadcast([P, P]), identity[:])
 
+        def make_slope(t, slots):
+            h, cols = in_half(slots)
+            nc.vector.scalar_tensor_tensor(
+                slope[t, h][:, cols], h_listed[t][:, slots], 0.0,
+                spread[h][:].rearrange("p j s -> p (j s)")[:, cols], MAX, MULT,
+            )
+
         def make_slopes(t):
             gather_on_scalar(h_listed[t][:, halves[0]], h_all[t], halves[0])
             gather_on_vector(h_listed[t][:, quarters[3]], h_all[t], quarters[3])
             gather_on_scalar(h_listed[t][:, quarters[2]], h_all[t], quarters[2])
-            for h in range(2):
-                nc.vector.scalar_tensor_tensor(
-                    slope[t, h], h_listed[t][:, halves[h]], 0.0,
-                    spread[h][:].rearrange("p j s -> p (j s)"), MAX, MULT,
-                )
+            make_slope(t, halves[0])
+            make_slope(t, slice(HALF, N - HELD) if t == LAST else halves[1])
 
         def dz(planes, slots):
             h, cols = in_half(slots)
-            return dz_halves[h][:].rearrange("p (t c) -> p t c", t=PACK)[:, planes, cols]
+            return dz_halves[h][:].rearrange("p (t c) -> p t c", c=HALF)[:, planes, cols]
 
         def gather_times_slope(t, slots):
             h, cols = in_half(slots)
             nc.vector.tensor_tensor(dz(t, slots), dy_all[t][:].indirect(listed(slots)), slope[t, h][:, cols], MULT)
 
-        def pick_dy(t, h):
-            gather_on_scalar(dy_listed[t][:], dy_all[t], halves[h])
-
-        def picked_times_slope(engine, t, h):
-            engine.tensor_tensor(dz(t, halves[h]), dy_listed[t][:], slope[t, h], MULT)
+        def pick_late_dy(t):
+            gather_on_scalar(dy_late[:, halves[t - 2]], dy_all[t], halves[1])
 
         def dz16(slots):
             h, cols = in_half(slots)
             if h:
                 return dz16_second[:, PACK * cols.start : PACK * cols.stop]
-            return late_bytes if cols.start else dz16_quarter0[:]
+            return dz16_quarter1 if cols.start else dz16_quarter0[:]
 
         def interleaved(dst, src):
             return (
@@ -213,21 +214,24 @@ def tile_attend_gex_x_kernel(tc, dyT, hT, ts, wm, offs, out):
         for t in range(1, PACK):
             make_slopes(t)
 
-        for t in range(LAST):
-            pick_dy(t, 0)
+        for t in range(2):
+            gather_on_scalar(dy_early[t][:], dy_all[t], halves[0])
             gather_times_slope(t, halves[1])
-            picked_times_slope(nc.vector, t, 0)
-            if t > 0:
-                nc.scalar.activation(*dz_views(quarters[1 + t], early_planes), ACT.Copy)
-        nc.vector.tensor_copy(*dz_views(quarters[1], early_planes))
+            nc.vector.tensor_tensor(dz(t, halves[0]), dy_early[t][:], slope[t, 0], MULT)
+        nc.scalar.activation(*dz_views(quarters[2], early_planes), ACT.Copy)
+        pick_late_dy(2)
+        gather_times_slope(2, halves[0])
+        nc.scalar.activation(*dz_views(quarters[3], early_planes), ACT.Copy)
+        for q in range(2):
+            nc.vector.tensor_copy(*dz_views(quarters[q], early_planes))
 
-        pick_dy(LAST, 1)
+        pick_late_dy(LAST)
         gather_times_slope(LAST, quarters[0])
         gather_times_slope(LAST, quarters[1])
         round_wm_on_scalar(0)
         round_wm_on_scalar(1)
         round_wm_on_scalar(2)
-        nc.vector.tensor_copy(*dz_views(quarters[0], all_planes))
+        nc.vector.tensor_copy(*dz_views(quarters[0], late_planes))
         quantize_wm(0)
         quantize_dz(quarters[0])
         product_via_scalar(0, quarters[0], 0)
@@ -239,11 +243,16 @@ def tile_attend_gex_x_kernel(tc, dyT, hT, ts, wm, offs, out):
         product_via_vector(1, quarters[0], 1)
         quantize_wm(3)
         product_via_vector(1, quarters[1], 2)
+        make_slope(LAST, slice(N - HELD, N))
         product_via_vector(2, halves[0], 3)
         scatter_on_vector(1, slice(0, COVER))
 
-        picked_times_slope(nc.gpsimd, LAST, 1)
-        nc.gpsimd.tensor_scalar(*dz_views(halves[1], late_planes), 1.0, 0.0, MULT, ADD)
+        nc.gpsimd.tensor_tensor(
+            dz16_second.rearrange("p (c i t) -> p c t i", i=2, t=PACK)[:, :, late_planes, :],
+            dy_late[:].rearrange("p (t c i) -> p c t i", t=2, i=2),
+            chain[:, :N].rearrange("p (t c i) -> p c t i", t=2, i=2),
+            MULT,
+        )
 
         scatter_on_scalar(0, quarters[0])
         product_via_scalar(0, quarters[1], 4)

from contextlib import ExitStack

import concourse.mybir as mybir
from concourse.masks import make_identity

N, T, D, DV = 1024, 2048, 512, 512
FLOPS = 2 * N * D * DV

F32 = mybir.dt.float32
BF16 = mybir.dt.bfloat16
U32 = mybir.dt.uint32
I32 = mybir.dt.int32
U16 = mybir.dt.uint16
U8 = mybir.dt.uint8
E4M3X4 = mybir.dt.float8_e4m3fn_x4
E5M2X4 = mybir.dt.float8_e5m2_x4
ACT = mybir.ActivationFunctionType
MULT = mybir.AluOpType.mult
MAX = mybir.AluOpType.max

P = 128
PACK = 4
LAST = PACK - 1
HALF = 512
QUARTER = 256
LIST_ROWS = 16
D_BLOCKS = D // P
LINE = 4
MX_ALIGN = 64
TURNS = HALF // P
SPREAD_BANK = 6
COVER = 384
HELD = 32
LONG = 384


def tile_attend_gex_x_kernel(tc, dyT, hT, ts, wm, offs, out):
    nc = tc.nc
    with ExitStack() as ctx:
        keep = ctx.enter_context(tc.tile_pool(name="keep", bufs=1))
        psum = ctx.enter_context(tc.psum_pool(name="psum", bufs=1))

        whole = slice(0, N)
        halves = [slice(0, HALF), slice(HALF, N)]
        quarters = [slice(q * QUARTER, (q + 1) * QUARTER) for q in range(N // QUARTER)]
        early_planes, late_planes = slice(0, 2), slice(2, PACK)

        offsets = keep.tile([P, N // LIST_ROWS], U16, name="offsets")
        ts_all = keep.tile([P, T], F32, name="ts_all", tag="ts_all")
        identity = keep.tile([P, P], F32, name="identity", tag="identity")
        h_all = [keep.tile([P, T], F32, name="h_all%d" % t, tag="h_all%d" % t) for t in range(PACK)]
        dy_all = [keep.tile([P, T], F32, name="dy_all%d" % t, tag="dy_all%d" % t) for t in range(PACK)]
        ts_listed = keep.tile([P, N], F32, name="ts_listed", tag="ts_listed")
        ts_down = keep.tile([P, N // P], F32, name="ts_down")
        h_listed = [keep.tile([P, N], F32, name="h_listed%d" % t) for t in range(PACK)]
        dy_early = [keep.tile([P, HALF], F32, name="dy_early%d" % t) for t in range(2)]
        dy_late = keep.tile([P, 2 * HALF], F32, name="dy_late")
        dz_halves = [keep.tile([P, planes * HALF], F32, name="dz%d" % planes) for planes in (PACK, 2)]
        dz16_quarter0 = keep.tile([P, PACK * QUARTER], BF16, name="dz16_quarter0", align_bytes=MX_ALIGN)
        dz_codes = keep.tile([P, N], U32, name="dz_codes", align_bytes=MX_ALIGN)
        dz_scales = keep.tile([P, N], U8, name="dz_scales", align_bytes=MX_ALIGN)
        wm_raw = [keep.tile([P, PACK, P], F32, name="wm_raw%d" % b) for b in range(D_BLOCKS)]
        wm_codes = keep.tile([P, D], U32, name="wm_codes", align_bytes=MX_ALIGN)
        wm_scales = keep.tile([P, D], U8, name="wm_scales", align_bytes=MX_ALIGN)

        chain = keep.tile([P, N + HALF], F32, name="chain", align_bytes=MX_ALIGN)
        dz16_quarter1 = chain[:, N:].bitcast(BF16)
        shared = keep.tile([P, N], F32, name="shared", align_bytes=MX_ALIGN)
        dz16_second = shared[:].bitcast(BF16)
        wm16 = [keep.tile([P, P * PACK], BF16, name="wm16_%d" % b, align_bytes=MX_ALIGN)[:] for b in range(LAST)]
        wm16.append(chain[:, N - HELD : N - HELD + QUARTER].bitcast(BF16))
        sums = [keep.tile([P, N], F32, name="sums%d" % b) for b in range(D_BLOCKS - 1)] + [shared]
        slope = {
            (t, h): keep.tile([P, HALF], F32, name="slope%d_%d" % (t, h))[:]
            for t, h in ((0, 0), (0, 1), (1, 0), (1, 1), (2, 0), (LAST, 0))
        }
        slope[2, 1], slope[LAST, 1] = chain[:, halves[0]], chain[:, halves[1]]

        h_rows = hT.rearrange("(p t) c -> p t c", t=PACK)
        dy_rows = dyT.rearrange("(p t) c -> p t c", t=PACK)
        wm_rows = wm.rearrange("b (p t) d -> p (b t) d", t=PACK)

        nc.sync.dma_start(ts_all[P - 1 :, :], ts[0:1, :])
        nc.sync.dma_start(offsets[:], offs)
        for tiles, rows in ((h_all, h_rows), (dy_all, dy_rows)):
            for t in range(PACK):
                nc.sync.dma_start(tiles[t][:], rows[:, t, :])
        for b in range(D_BLOCKS):
            nc.sync.dma_start(wm_raw[b][:], wm_rows[:, :, b * P : (b + 1) * P])

        nc.vector.memset(ts_all[: P - 1, :].bitcast(I32), 0)
        make_identity(nc, identity[:])

        def listed(slots):
            return offsets[:, slots.start // LIST_ROWS : slots.stop // LIST_ROWS]

        def in_half(slots):
            h = slots.start // HALF
            return h, slice(slots.start - h * HALF, slots.stop - h * HALF)

        def bank(shape, name, k):
            return psum.tile(shape, F32, name=name, tag="bank%d" % k)

        def gather_on_vector(dst, window, slots):
            nc.vector.tensor_copy(dst, window[:].indirect(listed(slots)))

        def gather_on_scalar(dst, window, slots):
            nc.scalar.activation(dst, window[:].indirect(listed(slots)), ACT.Copy)

        spread = [bank([P, TURNS, P], "spread%d" % h, SPREAD_BANK + h) for h in range(2)]
        for h, slots in enumerate(halves):
            if h == 0:
                gather_on_vector(ts_listed[:, slots], ts_all, slots)
            else:
                gather_on_vector(ts_listed[:, quarters[2]], ts_all, quarters[2])
                gather_on_scalar(ts_listed[:, quarters[3]], ts_all, quarters[3])
            turned = bank([P, TURNS, P], "ts_turned%d" % h, h)
            for j in range(TURNS):
                first = slots.start + j * P
                nc.tensor.transpose(turned[:, j, :], ts_listed[:, first : first + P], identity[:])
            nc.vector.tensor_scalar_mul(ts_down[:, h * TURNS : (h + 1) * TURNS], turned[:, :, P - 1], 2.0)
            for j in range(TURNS):
                col = h * TURNS + j
                nc.tensor.transpose(spread[h][:, j, :], ts_down[:, col : col + 1].to_broadcast([P, P]), identity[:])

        def make_slope(t, slots):
            h, cols = in_half(slots)
            nc.vector.scalar_tensor_tensor(
                slope[t, h][:, cols], h_listed[t][:, slots], 0.0,
                spread[h][:].rearrange("p j s -> p (j s)")[:, cols], MAX, MULT,
            )

        def make_slopes(t):
            gather_on_scalar(h_listed[t][:, halves[0]], h_all[t], halves[0])
            gather_on_vector(h_listed[t][:, quarters[3]], h_all[t], quarters[3])
            gather_on_scalar(h_listed[t][:, quarters[2]], h_all[t], quarters[2])
            make_slope(t, halves[0])
            make_slope(t, slice(HALF, N - HELD) if t == LAST else halves[1])

        def dz(planes, slots):
            h, cols = in_half(slots)
            return dz_halves[h][:].rearrange("p (t c) -> p t c", c=HALF)[:, planes, cols]

        def gather_times_slope(t, slots):
            h, cols = in_half(slots)
            nc.vector.tensor_tensor(dz(t, slots), dy_all[t][:].indirect(listed(slots)), slope[t, h][:, cols], MULT)

        def pick_late_dy(t):
            gather_on_scalar(dy_late[:, halves[t - 2]], dy_all[t], halves[1])

        def dz16(slots):
            h, cols = in_half(slots)
            if h:
                return dz16_second[:, PACK * cols.start : PACK * cols.stop]
            return dz16_quarter1 if cols.start else dz16_quarter0[:]

        def interleaved(dst, src):
            return (
                dst.rearrange("p (c i t) -> p c t i", i=LINE, t=PACK),
                src.rearrange("p t (c i) -> p c t i", i=LINE),
            )

        def dz_views(slots, planes):
            dst, src = interleaved(dz16(slots), dz(planes, slots))
            return dst[:, :, planes, :], src

        def round_wm_on_vector(b):
            nc.vector.tensor_copy(*interleaved(wm16[b], wm_raw[b][:]))

        def round_wm_on_scalar(b):
            nc.scalar.activation(*interleaved(wm16[b], wm_raw[b][:]), ACT.Copy)

        def quantize_dz(slots):
            nc.vector.quantize_mx(out=dz_codes[:, slots].bitcast(E5M2X4), scales=dz_scales[:, slots], in_=dz16(slots))

        def quantize_wm(b):
            cols = slice(b * P, (b + 1) * P)
            nc.vector.quantize_mx(out=wm_codes[:, cols].bitcast(E4M3X4), scales=wm_scales[:, cols], in_=wm16[b])

        def multiply(b, slots, k):
            cols = slice(b * P, (b + 1) * P)
            acc = bank([P, slots.stop - slots.start], "acc%d_%d" % (b, slots.start), k)
            nc.tensor.matmul_mx(
                out=acc[:],
                lhsT=wm_codes[:, cols].bitcast(E4M3X4),
                lhsT_scale=wm_scales[:, cols],
                rhs=dz_codes[:, slots].bitcast(E5M2X4),
                rhs_scale=dz_scales[:, slots],
                start=True,
                stop=True,
            )
            return acc

        def product_via_scalar(b, slots, k):
            nc.scalar.activation(sums[b][:, slots], multiply(b, slots, k)[:], ACT.Copy)

        def product_via_vector(b, slots, k):
            nc.vector.tensor_copy(sums[b][:, slots], multiply(b, slots, k)[:])

        def scatter_on_scalar(b, slots):
            nc.scalar.activation(out_rows[b][:].indirect(listed(slots)), sums[b][:, slots], ACT.Copy)

        def scatter_on_vector(b, slots):
            nc.vector.tensor_copy(out_rows[b][:].indirect(listed(slots)), sums[b][:, slots])

        def store(b, queue=nc.sync):
            queue.dma_start(out[b * P : (b + 1) * P, :], out_rows[b][:])

        make_slopes(0)
        out_rows = []
        for b, tag in enumerate(("ts_all", "ts_listed", "identity", "h_all0")):
            out_rows.append(keep.tile([P, T], F32, name="out_rows%d" % b, tag=tag))
            nc.gpsimd.memset(out_rows[b][:], 0.0)
        for t in range(1, PACK):
            make_slopes(t)

        for t in range(2):
            gather_on_scalar(dy_early[t][:], dy_all[t], halves[0])
            gather_times_slope(t, halves[1])
            nc.vector.tensor_tensor(dz(t, halves[0]), dy_early[t][:], slope[t, 0], MULT)
        nc.scalar.activation(*dz_views(quarters[2], early_planes), ACT.Copy)
        pick_late_dy(2)
        gather_times_slope(2, halves[0])
        nc.scalar.activation(*dz_views(quarters[3], early_planes), ACT.Copy)
        for q in range(2):
            nc.vector.tensor_copy(*dz_views(quarters[q], early_planes))

        pick_late_dy(LAST)
        gather_times_slope(LAST, quarters[0])
        gather_times_slope(LAST, quarters[1])
        round_wm_on_scalar(0)
        round_wm_on_scalar(1)
        round_wm_on_scalar(2)
        nc.vector.tensor_copy(*dz_views(quarters[0], late_planes))
        quantize_wm(0)
        quantize_dz(quarters[0])
        product_via_scalar(0, quarters[0], 0)
        nc.vector.tensor_copy(*dz_views(quarters[1], late_planes))
        quantize_wm(1)
        quantize_dz(quarters[1])
        quantize_wm(2)
        round_wm_on_vector(3)
        product_via_vector(1, quarters[0], 1)
        quantize_wm(3)
        product_via_vector(1, quarters[1], 2)
        make_slope(LAST, slice(N - HELD, N))
        product_via_vector(2, halves[0], 3)
        scatter_on_vector(1, slice(0, COVER))

        nc.gpsimd.tensor_tensor(
            dz16_second.rearrange("p (c i t) -> p c t i", i=2, t=PACK)[:, :, late_planes, :],
            dy_late[:].rearrange("p (t c i) -> p c t i", t=2, i=2),
            chain[:, :N].rearrange("p (t c i) -> p c t i", t=2, i=2),
            MULT,
        )

        scatter_on_scalar(0, quarters[0])
        product_via_scalar(0, quarters[1], 4)
        scatter_on_scalar(2, slice(0, LONG))
        scatter_on_scalar(0, quarters[1])
        quantize_dz(quarters[2])
        quantize_dz(quarters[3])
        product_via_vector(3, halves[0], 5)
        product_via_vector(1, quarters[2], 6)
        product_via_vector(1, quarters[3], 7)
        scatter_on_vector(1, slice(COVER, quarters[2].stop))
        product_via_scalar(0, halves[1], 0)
        product_via_scalar(2, halves[1], 1)
        product_via_vector(3, halves[1], 2)

        scatter_on_scalar(0, quarters[2])
        scatter_on_vector(1, quarters[3])
        store(1)
        scatter_on_scalar(2, slice(LONG, N - LONG))
        scatter_on_scalar(0, quarters[3])
        store(0)
        scatter_on_scalar(2, slice(N - LONG, N))
        store(2, nc.scalar)
        scatter_on_vector(3, whole)
        store(3)
